import numpy as np, ml_dtypes
CORES = [78,86,94,102,110,118]
N = 6
BF = ml_dtypes.bfloat16
def gentries(a):
    return np.ascontiguousarray(a.reshape(8, 16, -1).transpose(0, 2, 1)).reshape(8, -1)
def gtable(e):
    e = np.asarray(e); return np.ascontiguousarray(e.reshape(8, -1, 16).transpose(0, 2, 1)).reshape(128, -1).astype(np.int32)
V, K, RO, TH, NR, A = 3328, 256, 3, 10, 8, 2
EPS = 0.5
P = V // 16
def kinds(rng):
    i = np.arange(V); cut = rng.random(V) < 0.04; cut[0] = True
    last = np.maximum.accumulate(np.where(cut, i, 0)); v = rng.integers(0, P, V)
    return (v[last] + i - last) % P
def names(rng, kd):
    o = np.argsort(kd, kind="stable"); n = np.bincount(kd, minlength=P); s = np.add.accumulate(n) - n
    b = np.zeros((N, 8, 16, P), np.int64)
    for k in range(P):
        new = o[np.minimum(s[k] + (rng.random((N, 8, 16)) * n[k]).astype(np.int64), V - 1)]
        nxt = (b[..., k - 1] + 1) % V
        b[..., k] = np.where((kd[nxt] == k) & (rng.random((N, 8, 16)) < 0.85), nxt, new) if k else new
    return b
def blur(rng, r, lev):
    u = rng.random(r.shape, dtype=np.float32)
    r = np.where(u < lev, r + rng.integers(-3, 4, r.shape), r)
    return np.where(u < 0.3 * lev, rng.integers(0, V, r.shape), r) % V
def parts(rng, lev=(0.0, 0.15, 0.35, 0.8), dev=(0.1, 0.3, 0.6, 1.0)):
    kd = kinds(rng); b = names(rng, kd)
    r = blur(rng, b[..., kd], rng.choice(np.array(lev), (N, 8, 1, V)))
    x = rng.standard_normal((N, 8, 16, P), dtype=np.float32)[..., kd]
    x = x + rng.choice(np.array(dev), (N, 8, 1, V)).astype(np.float32) * rng.standard_normal((N, 8, 16, V), dtype=np.float32)
    return kd, b, x, r, rng.integers(0, V, (N, 8, K))
def pack(x, r, w):
    x = np.clip(x, -4.0, 4.0); x = np.where(np.abs(x) < 2.0 ** -19, 0.0, x)
    return {"x": np.ascontiguousarray(x.reshape(N, 128, V)).astype(np.float32).astype(BF), "rec": np.ascontiguousarray(r.reshape(N, 128, V)).astype(np.int32), "w0": np.stack([gtable(a) for a in w])}
def setup_inputs(rng):
    kd, b, x, r, w = parts(rng)
    return pack(x, r, w)
def setup_inputs_spread(rng):
    kd, b, x, r, w = parts(rng, (0.0, 0.05, 0.4, 1.0), (0.02, 0.1, 0.5, 1.2))
    x = x * np.exp2(rng.integers(-1, 2, (N, 8, 1, V))).astype(np.float32)
    far = (rng.random((N, 8, 1, V)) < 0.7) & (np.arange(N) % 2 == 1)[:, None, None, None]
    x = x + np.where(far, 2.5, 0.0).astype(np.float32) * rng.standard_normal((N, 8, 16, V), dtype=np.float32)
    w = np.minimum((V * rng.random((N, 8, K)) ** 2).astype(np.int64), V - 1)
    return pack(x, r, w)
def setup_inputs_ends(rng):
    kd, b, x, r, w = parts(rng)
    pat = rng.choice(np.array([0, V - 1]), (N, 8, 16, 1)); pat[:, :, 0] = 0; pat[:, :, 15] = V - 1
    val = np.where(rng.random(r.shape, dtype=np.float32) < 0.2, V - 1 - pat, pat); kind = rng.integers(0, 4, (N, 8, 1, V))
    val = np.where(kind == 0, 0, np.where(kind == 1, V - 1, val))
    r = np.where(rng.random((N, 8, 1, V)) < 0.78, val, r)
    x = np.where(rng.random((N, 8, 1, V)) < 0.78, np.where(x < 0, -4.0, 4.0), x)
    xp = rng.choice(np.array([-4.0, 4.0]), (N, 8, 16)); pl = pat[..., 0]
    o1 = np.argsort(rng.random((N, 8, 16)), axis=2); o2 = np.argsort(rng.random((N, 8, 16)), axis=2)
    for v in [V - 1] + list(range(RO + 2)):
        n1 = rng.choice(np.array([0, 0, 16 - TH, 16 - TH, 17 - TH, 16]), (N, 8, 1)); n2 = rng.choice(np.array([0, 16 - NR, 16 - NR, 17 - NR]), (N, 8, 1))
        if v == V - 1: n1 = n1 * 0; n2 = n2 * 0
        r[..., v] = np.where(o1 < n1, V - 1 - pl, pl); x[..., v] = np.where(o2 < n2, -xp, xp)
    w = np.where(rng.random((N, 8, K)) < 0.75, rng.choice(np.array([0, V - 1]), (N, 8, K)), w)
    w[..., 0] = V - 1; w[..., 1] = 0; w[..., K - 1] = V - 1
    return pack(x, r, w)
def setup_inputs_corners(rng):
    kd, b, x, r, w = parts(rng); i = np.arange(V)
    for q in range(N):
        o = rng.permutation(8)
        for g in range(8):
            if o[g] == 0: r[q, g] = i
            if o[g] == 1: r[q, g] = 0
            if o[g] == 2: r[q, g] = V - 1
            if 3 <= o[g] <= 5: r[q, g] = (i + (int(o[g]) - 2)) % V
    w = np.where(rng.random((N, 8, K)) < 0.5, rng.choice(np.array([0, 1, 2, V - 3, V - 2, V - 1]), (N, 8, K)), w)
    w[..., 0] = V - 1; w[..., K - 1] = V - 1
    return pack(x, r, w)
def setup_inputs_ties(rng):
    kd = kinds(rng); b = names(rng, kd); c = b[..., kd]
    o = np.argsort(rng.random(c.shape, dtype=np.float32), axis=2); kind = rng.choice(np.array([0, 1, 2]), (N, 8, 1, V), p=[0.5, 0.3, 0.2])
    far = np.where(kind == 0, 0, np.where(kind == 1, 16 - TH, 17 - TH)); sg = rng.choice(np.array([-1, 1]), (N, 8, 1, V))
    s = np.where(o < far, 3 * sg, np.where((kind > 0) & (o % 2 == 1), 2 * sg, 0))
    r = c + s; r = np.where((r < 0) | (r >= V), c - s, r)
    x = 0.25 * rng.integers(-8, 9, (N, 8, 16, P))[..., kd]
    o = np.argsort(rng.random(c.shape, dtype=np.float32), axis=2); kind = rng.choice(np.array([0, 1, 2]), (N, 8, 1, V), p=[0.4, 0.3, 0.3])
    far = np.where(kind == 1, 16 - NR, 17 - NR); sg = rng.choice(np.array([-1.0, 1.0]), c.shape)
    x = x + np.where(kind > 0, np.where(o < far, 0.515625, 0.5) * sg, 0.0)
    return pack(x, r, rng.integers(0, V, (N, 8, K)))
def setup_inputs_crowd(rng):
    kd, b, x, r, w = parts(rng, (0.0, 0.1, 0.2, 0.3)); r[:, :, 1] = b[:, :, 1][..., kd]
    for q in range(N):
        for g in range(8):
            k = (g + q) % 8; v = int(rng.integers(0, V)); mem = np.flatnonzero(kd == kd[v])
            if k < 4: w[q, g] = v
            if k == 2: w[q, g, K - 1] = mem[int(rng.integers(0, len(mem)))]
            if k == 3: w[q, g, 0] = mem[int(rng.integers(0, len(mem)))]
            if k == 4 or k == 5: w[q, g] = mem[rng.integers(0, len(mem), K)]
            if k == 6: w[q, g] = rng.choice(np.array([v, (v + 1) % V, V - 1]), K)
    return pack(x, r, w)
def check_ranges(d):
    bad = []
    for k in ("rec", "w0"):
        if np.min(d[k]) < 0 or np.max(d[k]) > V - 1: bad.append("range of " + k)
    a = np.abs(np.asarray(d["x"]).astype(np.float32))
    if not np.all((a == 0) | ((a >= 2.0 ** -19) & (a <= 4.0))): bad.append("range of x")
    return bad
def likeness(R, c, w):
    rc = np.take_along_axis(R, c.reshape(8, 1, 16 * K), 2).reshape(8, 16, 16, K)
    rw = np.take_along_axis(R, w[:, None, :], 2)[:, :, None, :]
    return np.add.reduce(np.abs(rc - rw) <= 2, axis=1, dtype=np.int32)
def reference(x, rec, w0):
    X = np.asarray(x).astype(np.float32).reshape(N, 8, 16, V); R = rec.astype(np.int32).reshape(N, 8, 16, V)
    w = np.stack([gentries(a) for a in w0]).astype(np.int32); ys = []
    for t in range(1, RO + 1):
        new = R.copy(); S = []; nxt = []
        for a in range(N):
            c = np.take_along_axis(R[a], w[a][:, None, :], 2)
            ok = likeness(R[a], c, w[a]) >= TH
            for b in range(A):
                q = (a + 1 + ((t - 1) * A + b) % (N - 1)) % N
                ok = ok & (likeness(R[q][(np.arange(8) + t + b) % 8], c, w[a]) >= TH)
            o = ok[:, (t + np.arange(16)) % 16]; has = np.any(o, axis=1); k = (t + np.argmax(o, axis=1)) % 16
            j = np.where(has, np.take_along_axis(c, k[:, None, :], 1)[:, 0], w[a])
            z = ((j + 1) % V).astype(np.int32); n = (c + 1) % V
            xn = np.take_along_axis(X[a], n.reshape(8, 1, 16 * K), 2).reshape(8, 16, 16, K)
            xz = np.take_along_axis(X[a], z[:, None, :], 2)[:, :, None, :]
            S.append(np.add.reduce(np.exp(-np.abs(xn.astype(np.float64) - xz.astype(np.float64))), axis=2))
            if t < RO:
                put = np.add.reduce(np.abs(xn - xz) <= np.float32(EPS), axis=1, dtype=np.int32) >= NR
                for g in range(8):
                    at = np.flatnonzero(has[g])
                    u, first = np.unique(z[g, at], return_index=True); lw = at[first]
                    new[a, g][:, u] = np.where(put[g][:, lw], n[g][:, lw], R[a, g][:, u])
            nxt.append(z)
        R = new; w = np.stack(nxt); ys.append(np.stack(S))
    return {"y": np.concatenate(ys, axis=3).reshape(N, 128, RO * K).astype(np.float32)}

def check_inputs(d):
    bad = list(check_ranges(d))
    if not bad:
        for name, y in reference(**d).items():
            for q in range(N):
                v = np.abs(np.asarray(y[q], np.float64)); s = np.sqrt(np.mean(v * v))
                if v.max() > 4 * s or s < 2.0 ** 1: bad.append('%s of rank %d is uneven or too small' % (name, q))
    return bad

@@ -1,0 +1,710 @@
+import numpy as np
+from concourse.bass import DstId, RemoteDMATransfer
+from concourse.mybir import dt, AluOpType, AxisListType, ActivationFunctionType
+
+V, K, RO, NR = 3328, 256, 3, 6
+CEN = 1664
+BIG = 8192.0
+MAGIC = 50331648.0
+HALF = 12582912.0
+HOPS = ((1, 2), (3, 4), (5, 1))
+
+PAR = {
+    "yo": (3, 2, 2),
+    "ou": (0, 0, 0),
+    "yg": ((5, 3), (4, 2), (4, 2)),
+    "yu": ((2, 2), (3, 4), (3, 4)),
+    "late": (4, 3, 2),
+    "sg": 3,
+    "mins": (1, 3, 5, 6),
+    "nch": 5,
+    "indb": 2,
+    "early": 1, "dfirst": 0, "wfirst": 1, "bonus": (0.0, 0.0), "seed": 1, "jit": 0.0, "look": 0.0,
+}
+COST = {"cy": 1.04e-3, "ga": 1.56, "sc": 3.8, "pe": 0.52e-3, "hop": 0.10, "same": 0.06, "dma": 2.0,
+        "rem": 3.5, "first": 2.0, "issue": 0.6}
+
+SCRATCH = {
+    "ri": ("sbuf", [128, V], "int32"),
+    "rw": ("sbuf", [128, V + 16], "float32"),
+    "xs": ("sbuf", [128, V + 32], "bfloat16"),
+    "xu": ("sbuf", [128, V], "bfloat16"),
+    "wi": ("sbuf", [128, 16], "int32"),
+    "d0": ("sbuf", [128, 4096], "float16"),
+    "d1": ("sbuf", [128, 4096], "float16"),
+    "d2": ("sbuf", [128, 4096], "float16"),
+    "mn": ("sbuf", [128, 1024], "bfloat16"),
+    "nb": ("sbuf", [128, 2048], "bfloat16"),
+    "bf": ("sbuf", [128, 8], "bfloat16"),
+    "thr": ("sbuf", [128, 256], "float16"),
+    "xn": ("sbuf", [128, 4096], "bfloat16"),
+    "gg": ("sbuf", [128, 4096], "float32"),
+    "ab": ("sbuf", [128, 4096], "float32"),
+    "acc": ("sbuf", [128, 512], "float32"),
+    "c16": ("sbuf", [128, 256], "float16"),
+    "t2": ("sbuf", [128, 256], "float16"),
+    "ol": ("sbuf", [128, 256], "uint16"),
+    "w1": ("sbuf", [128, 256], "float16"),
+    "w2": ("sbuf", [128, 256], "float16"),
+    "tp": ("sbuf", [128, 256], "bfloat16"),
+    "n32": ("sbuf", [128, 256], "float32"),
+    "ee": ("sbuf", [128, 256], "float32"),
+    "qe": ("sbuf", [128, 256], "float32"),
+    "zr": ("sbuf", [128, 256], "float32"),
+    "eq": ("sbuf", [128, 256], "float16"),
+    "ok": ("sbuf", [128, 256], "float16"),
+    "sn": ("sbuf", [128, 256], "float16"),
+    "xz": ("sbuf", [128, 256], "bfloat16"),
+    "wl": ("sbuf", [128, 16], "uint16"),
+    "w16": ("sbuf", [128, 16], "float16"),
+    "t16": ("sbuf", [128, 16], "float16"),
+    "z16": ("sbuf", [128, 16], "float16"),
+    "nh": ("sbuf", [128, 16], "float16"),
+    "qq": ("sbuf", [128, 16], "float32"),
+    "hh": ("sbuf", [128, 16], "float32"),
+    "so": ("sbuf", [128, 32], "uint16"),
+    "ka": ("sbuf", [128, 256], "float32"),
+    "kq": ("sbuf", [128, 384], "int32"),
+    "kr": ("sbuf", [128, 256], "float32"),
+    "kp": ("sbuf", [128, 16], "int32"),
+    "kp2": ("sbuf", [128, 16], "int32"),
+    "kf": ("sbuf", [128, 16], "float32"),
+    "kl": ("sbuf", [128, 16], "int32"),
+    "cl": ("sbuf", [128, 16], "uint16"),
+    "jj": ("sbuf", [128, 256], "float16"),
+    "j0": ("sbuf", [128, 256], "float16"),
+    "j1": ("sbuf", [128, 256], "float16"),
+    "bb": ("sbuf", [128, 256], "float16"),
+    "bs": ("sbuf", [128, 256], "float16"),
+    "ib2": ("sbuf", [128, 128], "bfloat16"),
+    "ni": ("sbuf", [128, 128], "float16"),
+    "i32": ("sbuf", [128, 128], "float32"),
+    "ib": ("sbuf", [128, 128], "bfloat16"),
+    "nib": ("sbuf", [128, 128], "bfloat16"),
+    "bo": ("sbuf", [128, 128], "float16"),
+    "uu": ("sbuf", [128, 384], "float16"),
+    "tri": ("sbuf", [128, 256], "float16"),
+}
+for _t in range(RO):
+    for _b in range(2):
+        SCRATCH["qs%d%d" % (_t, _b)] = ("sbuf", [128, 272], "uint16")
+        SCRATCH["ql%d%d" % (_t, _b)] = ("sbuf", [128, 272], "uint16")
+        SCRATCH["rs%d%d" % (_t, _b)] = ("sbuf", [128, 256], "float16")
+        SCRATCH["rl%d%d" % (_t, _b)] = ("sbuf", [128, 256], "float16")
+for _b in range(2):
+    SCRATCH["vs%d" % _b] = ("sbuf", [128, 16], "uint16")
+    SCRATCH["vl%d" % _b] = ("sbuf", [128, 16], "uint16")
+for _b in range(8):
+    SCRATCH["p%d" % _b] = ("psum", [128, 512], "float32")
+
+SEMAPHORES = (["dve", "act", "pe", "pool", "sent", "av0", "av1"] + ["dm%d" % _i for _i in range(30)]
+              + ["aq%d%d" % (_t, _b) for _t in range(RO) for _b in range(2)]
+              + ["ar%d%d" % (_t, _b) for _t in range(RO) for _b in range(2)])
+
+AL = AluOpType
+AF = ActivationFunctionType
+
+
+def rf(name, a=0, b=None, s=1):
+    if b is None:
+        b = SCRATCH[name][1][1]
+    return (name, a, b, s)
+
+
+def cnt(r):
+    return len(range(r[1], r[2], r[3]))
+
+
+def meet(r, q):
+    if r[2] <= q[1] or q[2] <= r[1]:
+        return False
+    if r[3] == 1 and q[3] == 1:
+        return True
+    return len(set(range(r[1], r[2], r[3])) & set(range(q[1], q[2], q[3]))) > 0
+
+
+def two_bytes(r):
+    return SCRATCH[r[0]][2] in ("float16", "bfloat16", "uint16")
+
+
+def in_psum(r):
+    return SCRATCH[r[0]][0] == "psum"
+
+
+def build(g, core, T, topo, rank):
+    ops = []
+    ahead = [0.0]
+    C = COST
+
+    def ap(r):
+        if len(r) == 2:
+            return ap(r[0]).indirect(ap(r[1]))
+        return T[r[0]][:, r[1]:r[2]] if r[3] == 1 else T[r[0]][:, r[1]:r[2]:r[3]]
+
+    def flat(rs):
+        out = []
+        for r in rs:
+            if isinstance(r, tuple):
+                out.extend(r if len(r) == 2 else [r])
+        return out
+
+    def add(eng, fn, reads, writes, dur, lat=0.0, kind="c", arrive=None, after=None):
+        ops.append({"eng": eng, "fn": fn, "r": flat(reads), "w": flat(writes), "dur": dur, "lat": lat, "kind": kind,
+                    "arrive": arrive, "after": after, "bonus": ahead[0]})
+        return len(ops) - 1
+
+    def sc(x):
+        return ap(x) if isinstance(x, tuple) else x
+
+    def vdur(out, ins, both=False):
+        if len(ins[0]) == 2:
+            return 0.05 + cnt(out) * C["ga"] * C["cy"]
+        n = cnt(out) * (2.0 if both else 1.0)
+        if not both and two_bytes(out) and all(two_bytes(i) for i in ins):
+            n *= 0.5
+        return max(n, 64) * C["cy"]
+
+    def ts(out, in0, s1, s2, op0, op1=None, **kw):
+        def fn():
+            if op1 is None:
+                return g.vector.tensor_scalar(ap(out), ap(in0), sc(s1), None, op0)
+            return g.vector.tensor_scalar(ap(out), ap(in0), sc(s1), sc(s2), op0, op1)
+        return add("dve", fn, [in0, s1, s2], [out], vdur(out, [in0]), **kw)
+
+    def tt(out, in0, in1, op, **kw):
+        both = len(in0) == 4 and not in_psum(in0) and not in_psum(in1)
+        return add("dve", lambda: g.vector.tensor_tensor(ap(out), ap(in0), ap(in1), op), [in0, in1], [out],
+                   vdur(out, [in0, in1], both), **kw)
+
+    def cp(out, in0, **kw):
+        return add("dve", lambda: g.vector.tensor_copy(ap(out), ap(in0)), [in0], [out], vdur(out, [in0]), **kw)
+
+    def act(out, in0, func, bias=None, scale=None, **kw):
+        def fn():
+            k = {}
+            if bias is not None:
+                k["bias"] = bias
+            if scale is not None:
+                k["scale"] = scale
+            return g.scalar.activation(ap(out), ap(in0), func, **k)
+        d = 0.065 + cnt(out) * C["ga"] * C["cy"] if len(in0) == 2 else max(cnt(out), 64) * C["cy"] + 0.03
+        return add("act", fn, [in0], [out], d, **kw)
+
+    def mm(out, lhs, rhs, start, stop, fam=None, auto=None, **kw):
+        d = max(64, cnt(rhs)) * C["pe"] * (4 if SCRATCH[rhs[0]][2] == "float32" else 1)
+        fl = {"start": start, "stop": stop}
+        i = add("pe", lambda: g.tensor.matmul(ap(out), ap(lhs), ap(rhs), fl["start"], fl["stop"]), [lhs, rhs], [out], d,
+                lat=0.05, **kw)
+        ops[i].update({"fam": fam, "auto": auto, "fl": fl})
+        return i
+
+    def group(out, terms):
+        for i, term in enumerate(terms):
+            kw = term[2] if len(term) > 2 else {}
+            mm(out, term[0], term[1], i == 0, i == len(terms) - 1, **kw)
+
+    def iota(out, pattern, base, cm):
+        def fn():
+            if SCRATCH[out[0]][2] == "int32":
+                return g.iota(ap(out), pattern, base, cm)
+            return g.iota(ap(out), pattern, base, cm, allow_small_or_imprecise_dtypes=True)
+        return add("pool", fn, [], [out], 0.13 + 2 * cnt(out) * C["cy"])
+
+    def asel(buf, pattern, op, fill, base, cm, **kw):
+        return add("pool", lambda: g.affine_select(ap(buf), ap(buf), pattern, op, fill, base, cm), [buf], [buf],
+                   0.17 + 2 * cnt(buf) * C["cy"], **kw)
+
+    def dma(eng, fn, reads, writes, nbytes, **kw):
+        return add(eng, fn, reads, writes, 0.1 if eng != "pool" else C["issue"], lat=C["dma"] + nbytes / 600e3, kind="dma", **kw)
+
+    def send(src, dst_name, sem, to_rank, first=False):
+        to = T.cores[to_rank]
+        rid, pid, _ = topo.addr(to)
+
+        def fn():
+            return g.remote_dma(T[dst_name][:, 0:cnt(src)], ap(src), T.sem[sem], T.sem.sent, pid, rid, topo.mask(core, to))
+        i = add("pool", fn, [src], [], C["issue"], lat=C["rem"] + (C["first"] if first else 0.0), kind="rem")
+        ops[i]["width"] = len(topo.engines(core, to))
+        return i
+
+    def jsl(name, shift):
+        x = (-shift) % 128
+        return rf(name, x, x + 128)
+
+    RW = rf("rw", 0, V)
+    I16 = rf("jj", 0, 128)
+
+    dma("sync", lambda: g.sync.dma_start(T.wi[:], T.w0[:]), [], [rf("wi")], 8192)
+    nch = PAR["nch"]
+    step = V // nch
+    for i in range(nch):
+        a, b = i * step, (V if i == nch - 1 else (i + 1) * step)
+        q = g.scalar if i % 2 == 0 else g.sync
+        dma("act" if i % 2 == 0 else "sync", (lambda q=q, a=a, b=b: q.dma_start(T.ri[:, a:b], T.rec[:, a:b])), [],
+            [rf("ri", a, b)], 128 * 4 * b)
+    dma("sync", lambda: g.sync.dma_start(T.xs[:, 15:15 + V], T.x[:]), [], [rf("xs", 15, 15 + V)], 128 * 6 * V)
+    dma("sync", lambda: g.sync.dma_start(T.xs[:, 15 + V:17 + V], T.x[:, 0:2]), [], [rf("xs", 15 + V, 17 + V)], 128 * 6 * V)
+    dma("sync", lambda: g.sync.dma_start(T.xu[:], T.x[:]), [], [rf("xu")], 128 * 8 * V)
+    XS = rf("xs", 16, 16 + V)
+
+    iota(rf("kp", 0, 4), [[0, 4]], 0, 1)
+    iota(rf("ka"), [[0, 2], [1, 128]], 0, -1)
+    iota(rf("kp", 4, 7), [[-1, 3]], 15, 1)
+    ts(rf("kp2", 0, 1), rf("kp", 0, 1), 16, None, AL.bitwise_and)
+    ts(rf("kp2", 1, 7), rf("kp", 1, 7), 15, None, AL.bitwise_and)
+    cp(rf("kf", 0, 7), rf("kp2", 0, 7))
+    PR = rf("kf", 1, 2)
+    ts(rf("kf", 8, 9), rf("kf", 0, 1), 0.0, None, AL.is_equal)
+    ts(rf("kf", 9, 10), rf("kf", 0, 1), 0.0, None, AL.is_gt)
+    ts(rf("jj"), rf("ka"), 0.0, None, AL.is_equal)
+    ts(rf("j0"), rf("jj"), rf("kf", 8, 9), None, AL.mult)
+    ts(rf("j1"), rf("jj"), rf("kf", 9, 10), None, AL.mult)
+    ts(rf("bb"), rf("ka"), PR, 0.0, AL.add, AL.is_equal)
+    ts(rf("ni"), I16, -1.0, None, AL.mult)
+    cp(rf("i32"), I16)
+    act(rf("nib"), rf("i32"), AF.Identity, scale=-1.0)
+    act(rf("ib"), rf("i32"), AF.Identity)
+    act(rf("ib2"), rf("i32"), AF.Identity, scale=2.0)
+    ts(rf("bs"), rf("bb"), BIG, None, AL.mult)
+    add("dve", lambda: g.vector.memset(T.rw[:, V:V + 16], 0.0), [], [rf("rw", V, V + 16)], 0.07)
+    add("dve", lambda: g.vector.memset(T.bo[:], 1.0), [], [rf("bo")], 0.07)
+    add("dve", lambda: g.vector.memset(T.thr[:], 7.5), [], [rf("thr")], 0.14)
+    cp(rf("bf"), rf("bb", 0, 128, 16))
+    iota(rf("kq"), [[-1, 3], [0, 8], [1, 16]], 15, 0)
+    iota(rf("kr"), [[0, 16], [1, 16]], 0, 0)
+    iota(rf("kl"), [[1, 16]], 0, 0)
+    ts(rf("kq"), rf("kq"), 15, None, AL.bitwise_and)
+    for t in range(RO):
+        ts(rf("uu", 128 * t, 128 * t + 128), rf("kq", 128 * t, 128 * t + 128), rf("kf", 4 + t, 5 + t), None, AL.is_gt)
+    ts(rf("tri"), rf("kr"), PR, BIG, AL.is_le, AL.mult)
+    cp(rf("cl"), rf("kl"))
+    ts(rf("kf", 10, 11), PR, V - CEN - 1 - BIG, None, AL.add)
+
+    cp(rf("wl"), rf("wi"))
+    ts(rf("w16"), rf("wi"), float(CEN), None, AL.subtract)
+    wsend = []
+    if PAR["wfirst"]:
+        for b in range(2):
+            group(rf("p%d" % (b + 1), 256, 272), [(jsl("jj", 16 * (1 + b)), rf("w16"))])
+            ts(rf("vs%d" % b), rf("p%d" % (b + 1), 256, 272), float(CEN), None, AL.add)
+            wsend.append(send(rf("vs%d" % b), "vl%d" % b, "av%d" % b, (rank + HOPS[0][b]) % NR, first=True))
+    for i in range(nch):
+        a, b = i * step, (V if i == nch - 1 else (i + 1) * step)
+        ts(rf("rw", a, b), rf("ri", a, b), float(CEN), None, AL.subtract)
+
+    ring = {"p": 0, "g": 0}
+
+    def bank(banks):
+        ring["p"] += 1
+        return "p%d" % banks[ring["p"] % len(banks)]
+
+    def count_by_walkers(dbuf, k, cbank, c0, shift, fam):
+        x = (16 * shift) % 128
+        for h in range(2):
+            mm(rf(cbank, c0 + 128 * h + k, c0 + 128 * h + 128, 16), rf(dbuf, 256 * k + 128 * h, 256 * k + 128 * h + 128),
+               rf("bf") if dbuf == "nb" else rf("bb", x, x + 128, 16), True, True, fam=fam)
+
+    def likeness(dbuf, lists, wref, ns, nu, wps, banks, arrive, counter, rows=(0, 16), cut=16, after=None):
+        kw = {"arrive": arrive, "after": after}
+        units = []
+        npairs = ns + nu
+        kinds = sorted([((i + 0.5) / ns, "s") for i in range(ns)] + [((i + 0.6) / nu, "u") for i in range(nu)])
+        for i in range(npairs):
+            units.append(((i + 1.0) / npairs, kinds[i][1], 2 * i, 2 * i + 2))
+        k, nd = 2 * npairs, 16 - 2 * npairs
+        while k < 16:
+            e = min(cut if k < cut else 16, k + PAR["indb"])
+            units.append(((e - 2.0 * npairs) / nd - 1e-3, "v", k, e))
+            k = e
+        units.sort()
+        for _, how, k0, k1 in units:
+            if k0 < rows[0] or k0 >= rows[1]:
+                continue
+            dd = rf(dbuf, 256 * k0, 256 * k1)
+            if how != "v":
+                c0 = 512 * (ring["g"] % 8)
+                ring["g"] += 1
+                act(rf("gg", c0, c0 + 512), (RW, rf(lists, 16 * k0, 16 * k1)), AF.Copy, **kw)
+            if how == "s":
+                pb = bank(banks)
+                for h in range(2):
+                    group(rf(pb, 256 * h, 256 * h + 256),
+                          [(rf("ni"), wref), (rf("i32"), rf("gg", c0 + 256 * h, c0 + 256 * h + 256))])
+                ts(dd, rf(pb), MAGIC, MAGIC, AL.add, AL.is_equal)
+            else:
+                for k in range(k0, k1):
+                    dk = rf(dbuf, 256 * k, 256 * k + 256)
+                    if how == "u":
+                        tt(dk, rf("gg", c0 + 256 * (k - k0), c0 + 256 * (k - k0) + 256), wps, AL.subtract)
+                    else:
+                        tt(dk, (RW, rf(lists, 16 * k, 16 * k + 16)), wref, AL.subtract, **kw)
+                ts(dd, dd, MAGIC, MAGIC, AL.add, AL.is_equal)
+            for k in range(k0, k1):
+                counter(k)
+
+    for t in range(RO):
+        last = t == RO - 1
+        tt_ = t + 1
+        if t == 0 and PAR["early"]:
+            ts(rf("c16"), (rf("ri"), rf("wl")), float(CEN), None, AL.subtract)
+        else:
+            cp(rf("c16"), (RW, rf("wl")))
+        act(rf("tp"), (RW, rf("wl")), AF.Relu, bias=-float(V * (V - CEN - 2)), scale=float(V))
+        for be in range(8):
+            add("dve", (lambda be=be: g.vector.transpose(T.t2[:, be:256:8], T.c16[:, 32 * be:32 * be + 32])),
+                [rf("c16", 32 * be, 32 * be + 32)], [rf("t2", be, 256, 8)], 64 * C["cy"])
+        sends = []
+        for b, pb in ((0, "p1"), (1, "p2"), (2, "p3")):
+            s = 0 if b == 2 else tt_ + b
+            for gp in range(2):
+                group(rf(pb, gp, 256, 2),
+                      [(jsl("j%d" % gp, 16 * (ga - gp + s)), rf("t2", 128 * ga, 128 * ga + 128)) for ga in range(2)])
+            if b < 2:
+                wide = 256 if t == 0 and PAR["wfirst"] else 272
+                if wide > 256:
+                    group(rf(pb, 256, 272), [(jsl("jj", 16 * s), rf("w16"))])
+                ts(rf("qs%d%d" % (t, b), 0, wide), rf(pb, 0, wide), float(CEN), None, AL.add)
+                sends.append(send(rf("qs%d%d" % (t, b), 0, wide), "ql%d%d" % (t, b), "aq%d%d" % (t, b),
+                                  (rank + HOPS[t][b]) % NR, first=(t == 0 and wide > 256)))
+            else:
+                ts(rf("ol"), rf(pb, 0, 256), float(CEN), None, AL.add)
+        if t == 0:
+            for buf, rep in ((rf("uu"), 3), (rf("bo"), 1)):
+                asel(buf, [[0, rep], [-16, 8], [0, 16]], AL.is_ge, 0.0, 0, 1, after=sends)
+                asel(buf, [[0, rep], [16, 8], [0, 16]], AL.is_ge, 0.0, 15, -1)
+            asel(rf("uu"), [[0, 3], [-1, 128]], AL.not_equal, -1.0, 0, 1)
+            if PAR["sg"]:
+                asel(rf("thr"), [[0, 16], [1, 16]], AL.is_ge, -0.5, -2 * PAR["sg"], 0, after=sends)
+        else:
+            w = 2048
+            prev = sends
+            while w >= 256:
+                dma("pool", (lambda w=w: g.dma_start(T.ab[:, 0:w], T.ab[:, w:2 * w], accum_op=AL.add)),
+                    [rf("ab", 0, 2 * w)], [rf("ab", 0, w)], 128 * 8 * w, after=prev)
+                prev = None
+                w //= 2
+            dma("sync", (lambda t=t: g.sync.dma_start(T.y[:, 256 * (t - 1):256 * t], T.ab[:, 0:256])),
+                [rf("ab", 0, 256)], [], 128 * 1024)
+        ts(rf("t16"), rf("w16"), float(V - CEN - 1), -float(V), AL.is_equal, AL.mult)
+        tt(rf("t16"), rf("t16"), rf("w16"), AL.add)
+        if not last:
+            group(rf("p3", 0, 256), [(I16, rf("c16")), (rf("nib"), rf("tp"))])
+            act(rf("n32"), rf("p3", 0, 256), AF.Identity, bias=1.0)
+        if PAR["ou"][t]:
+            group(rf("p3", 256, 512), [(I16, rf("c16"))])
+
+        arr = [("aq%d%d" % (t, b), sends[b]) for b in range(2)]
+        answers = []
+        nu = PAR["yu"][t]
+        banks = (4, 5, 6) if max(nu) else (4, 5, 6, 7)
+        for b in range(2):
+            ql = "ql%d%d" % (t, b)
+            ahead[0] = PAR["bonus"][b]
+            if t == 0 and PAR["wfirst"]:
+                cp(rf("w%d" % (b + 1)), (RW, rf("vl%d" % b)), arrive=("av%d" % b, wsend[b]))
+            else:
+                cp(rf("w%d" % (b + 1)), (RW, rf(ql, 256, 272)), arrive=arr[b])
+            ahead[0] = 0.0
+            if nu[b]:
+                group(rf("p7", 256 * b, 256 * b + 256), [(I16, rf("w%d" % (b + 1)))])
+        own = "own%d" % t
+        cut = 16 - PAR["late"][t]
+
+        def own_rows(rows, after):
+            likeness("d0", "ol", rf("c16"), PAR["yo"][t], PAR["ou"][t], rf("p3", 256, 512), banks, None,
+                     lambda k: mm(rf("p0", 0, 256), jsl("bb", k), rf("d0", 256 * k, 256 * k + 256), False, False, fam=own,
+                                  auto=own), rows, cut, after)
+        own_rows((0, cut), None)
+        made = []
+        for b in range(2):
+            ql = "ql%d%d" % (t, b)
+            pb = "p%d" % (b + 1)
+            ahead[0] = PAR["bonus"][b]
+            likeness("d%d" % (b + 1), ql, rf("w%d" % (b + 1)), PAR["yg"][t][b], nu[b], rf("p7", 256 * b, 256 * b + 256), banks,
+                     arr[b], lambda k: count_by_walkers("d%d" % (b + 1), k, pb, 0, tt_ + b, ql))
+            made.append(len(ops) - 1)
+            ts(rf("rs%d%d" % (t, b)), rf(pb, 0, 256), 9.5, 32.0, AL.is_ge, AL.mult)
+            answers.append(send(rf("rs%d%d" % (t, b)), "rl%d%d" % (t, b), "ar%d%d" % (t, b), (rank - HOPS[t][b]) % NR))
+        ahead[0] = 0.0
+        last_ind = max(i for i in range(made[1]) if ops[i]["eng"] == "dve")
+        own_rows((cut, 16), [last_ind])
+        for i in range(8):
+            act(rf("xn", 512 * i, 512 * i + 512), (XS, rf("ol", 32 * i, 32 * i + 32)), AF.Copy)
+        for b in range(2):
+            for h in range(2):
+                mm(rf("p0", 128 * h, 128 * h + 128), rf("rl%d%d" % (t, b), 128 * h, 128 * h + 128), I16, False, False,
+                   auto=own, arrive=("ar%d%d" % (t, b), answers[b]))
+
+        mm(rf("p1", 0, 256), I16, rf("c16"), True, False)
+        mm(rf("p1", 0, 256), rf("nib"), rf("tp"), False, False)
+        ts(rf("ok"), rf("p0", 0, 256), 73.5, -BIG, AL.is_ge, AL.mult)
+        mm(rf("p1", 0, 256), rf("uu", 128 * t, 128 * t + 128), rf("ok"), False, True)
+        ts(rf("sn"), rf("p1", 0, 256), BIG - 1666.0, BIG, AL.max, AL.subtract)
+        group(rf("p3", 256, 272), [(jsl("bb", r), rf("sn", r, 256, 16)) for r in range(16)])
+        ts(rf("nh"), rf("p3", 256, 272), -16 * 1666.0 + 0.5, -BIG, AL.is_gt, AL.mult)
+        ts(rf("qq"), rf("p3", 256, 272), 15 * 1666.0, None, AL.add)
+        tt(rf("hh"), rf("nh"), rf("t16"), AL.add)
+        tt(rf("z16"), rf("hh"), rf("qq"), AL.max)
+        ts(rf("wl"), rf("z16"), float(CEN + 1), None, AL.add)
+        xz = act(rf("xz"), (rf("xu"), rf("wl")), AF.Copy)
+        if not last:
+            ts(rf("w16"), rf("z16"), 1.0, None, AL.add)
+            group(rf("p1", 256, 512), [(I16, rf("tri")), (rf("bo"), rf("sn"))])
+            act(rf("zr"), rf("p1", 256, 512), AF.Identity, bias=15 * 1666.0, after=[xz])
+            tt(rf("ee"), (RW, rf("wl")), rf("n32"), AL.subtract)
+            tt(rf("eq"), (rf("qq"), rf("cl")), rf("zr"), AL.is_equal)
+            group(rf("p3", 288, 304), [(I16, rf("nh")), (I16, rf("z16"))]
+                  + [(jsl("bs", r), rf("eq", r, 256, 16)) for r in range(16)])
+            ts(rf("so", 0, 32, 2), rf("p3", 288, 304), rf("kf", 10, 11), CEN + 1 + BIG, AL.min, AL.add)
+
+        banks = (4, 5, 6, 7, 2)
+        if last:
+            mins = PAR["mins"]
+            if mins:
+                for h in range(2):
+                    group(rf("p0", 256 * h, 256 * h + 256), [(rf("ib"), rf("xz"))])
+        elif PAR["sg"]:
+            sg = PAR["sg"]
+            slots = {}
+            todo = []
+            for i in range(8):
+                j = sg + i
+                pair = ([i] if i < sg else []) + ([j] if j < 8 else [])
+                todo += pair[::-1] if i < PAR["dfirst"] else pair
+            spare = list(banks)
+            for i in todo:
+                pb = "p%d" % spare.pop(0)
+                slots[i] = pb
+                ab = rf("ab", 512 * i, 512 * i + 512)
+                mm(rf(pb), rf("ib"), rf("xn", 512 * i, 512 * i + 512), True, False)
+                for h in range(2):
+                    mm(rf(pb, 256 * h, 256 * h + 256), rf("nib"), rf("xz"), False, h == 1)
+                if i < sg:
+                    act(ab, rf(pb), AF.Abs)
+                    spare.append(int(pb[1]))
+                    act(rf("nb", 512 * i, 512 * i + 512), ab, AF.Sign, bias=0.5 + 2.0 ** -21, scale=-1.0)
+                else:
+                    ts(rf("d0", 512 * i, 512 * i + 512), rf(pb), HALF, HALF, AL.add, AL.is_equal)
+                for k in (2 * i, 2 * i + 1):
+                    count_by_walkers("nb" if i < sg else "d0", k, "p0", 256, 0, "near%d" % t)
+            for i in range(sg, 8):
+                act(rf("ab", 512 * i, 512 * i + 512), rf(slots[i]), AF.Abs)
+        for i in range(8 if last or not PAR["sg"] else 0):
+            pb = bank(banks)
+            xn = rf("xn", 512 * i, 512 * i + 512)
+            ab = rf("ab", 512 * i, 512 * i + 512)
+            bymin = last and i in mins
+            mm(rf(pb), rf("nib" if bymin else "ib"), xn, True, False)
+            for h in range(2):
+                mm(rf(pb, 256 * h, 256 * h + 256), rf("nib"), rf("xz"), False, h == 1 and not bymin)
+            if bymin:
+                mn = rf("mn", 512 * (i % 2), 512 * (i % 2) + 512)
+                tt(mn, xn, rf("p0"), AL.min)
+                mm(rf(pb), rf("ib2"), mn, False, True)
+                act(rf(pb), rf(pb), AF.Exp)
+            else:
+                act(ab, rf(pb), AF.Abs)
+            if last:
+                if not bymin:
+                    act(rf(pb), ab, AF.Exp, scale=-1.0)
+                if i == 0:
+                    cp(rf("acc"), rf(pb))
+                elif i < 7:
+                    tt(rf("acc"), rf(pb), rf("acc"), AL.add)
+                else:
+                    tt(rf("acc", 0, 256), rf("acc", 0, 256), rf("acc", 256, 512), AL.add)
+                    for h in range(2):
+                        tt(rf("acc", 0, 256), rf(pb, 256 * h, 256 * h + 256), rf("acc", 0, 256), AL.add)
+            else:
+                ts(rf("d0", 512 * i, 512 * i + 512), ab, 0.5, None, AL.is_le)
+                for k in (2 * i, 2 * i + 1):
+                    count_by_walkers("d0", k, "p0", 256, 0, "near%d" % t)
+        if last:
+            dma("sync", (lambda t=t: g.sync.dma_start(T.y[:, 256 * t:256 * t + 256], T.acc[:, 0:256])),
+                [rf("acc", 0, 256)], [], 128 * 1024)
+            break
+        for h in (1, 0):
+            a, b = 128 * h, 128 * h + 128
+            tt(rf("ok", a, b), rf("p0", 256 + a, 256 + b), rf("thr", a, b), AL.is_lt)
+        for h in (1, 0):
+            a, b = 128 * h, 128 * h + 128
+            pb = "p1" if h else "p3"
+            group(rf(pb, a, b), [(rf("ok", a, b), I16)])
+            tt(rf("qe", a, b), rf(pb, a, b), rf("ee", a, b), AL.mult)
+        win = rf("rw")
+        for m in range(15, -1, -1):
+            add("dve", (lambda m=m: g.vector.tensor_tensor(ap((win, rf("so", 2 * m, 2 * m + 1))), T.qe[:, 16 * m:16 * m + 16],
+                                                           T.n32[:, 16 * m:16 * m + 16], AL.add)),
+                [rf("so", 2 * m, 2 * m + 1), rf("qe", 16 * m, 16 * m + 16), rf("n32", 16 * m, 16 * m + 16)], [win],
+                0.05 + 16 * C["sc"] * C["cy"])
+        for i in range(4):
+            ab = rf("ab", 1024 * i, 1024 * i + 1024)
+            act(ab, ab, AF.Exp, scale=-1.0)
+    return ops
+
+
+def plan(ops):
+    n = len(ops)
+    index = {}
+    seen = {}
+    for i, o in enumerate(ops):
+        dep, soft = set(), set()
+        for r, isw in [(r, False) for r in o["r"]] + [(r, True) for r in o["w"]]:
+            for j, q, wasw in seen.get(r[0], ()):
+                if j == i:
+                    continue
+                ej = ops[j]["eng"]
+                if in_psum(r) and ej != o["eng"]:
+                    dep.add(j)
+                elif in_psum(r) and ej == "pe":
+                    if o["fam"] is None or o["fam"] != ops[j]["fam"]:
+                        soft.add(j)
+                elif (isw or wasw) and meet(r, q):
+                    dep.add(j)
+        for r, isw in [(r, False) for r in o["r"]] + [(r, True) for r in o["w"]]:
+            lst = seen.setdefault(r[0], [])
+            if isw and not in_psum(r) and r[3] == 1:
+                lst[:] = [e for e in lst if not (r[1] <= e[1][1] and e[1][2] <= r[2])]
+            lst.append((i, r, isw))
+        o["dep"], o["soft"] = dep, soft
+    return n
+
+
+def order(ops):
+    n = len(ops)
+    C = COST
+    pred = []
+    for i, o in enumerate(ops):
+        p = {}
+        for j in o["dep"]:
+            p[j] = ops[j]["dur"] + ops[j]["lat"] + (C["same"] if ops[j]["eng"] == o["eng"] else C["hop"])
+        for j in o["soft"]:
+            p.setdefault(j, ops[j]["dur"])
+        for j in o["after"] or ():
+            p.setdefault(j, ops[j]["dur"])
+        if o["arrive"] is not None:
+            j = o["arrive"][1]
+            p[j] = ops[j]["dur"] + ops[j]["lat"]
+        pred.append(p)
+    succ = [[] for _ in range(n)]
+    for i in range(n):
+        for j in pred[i]:
+            succ[j].append(i)
+    prio = [0.0] * n
+    for i in range(n - 1, -1, -1):
+        best = ops[i]["dur"] + ops[i]["lat"]
+        for s in succ[i]:
+            best = max(best, pred[s][i] + prio[s])
+        prio[i] = best
+    x = PAR["seed"]
+    for i in range(n):
+        x = (x * 1103515245 + 12345) % 2147483648
+        prio[i] += PAR["jit"] * x / 2147483648.0 + ops[i]["bonus"]
+    left = [len(p) for p in pred]
+    ready = {}
+    for i in range(n):
+        if left[i] == 0:
+            ready[i] = 0.0
+    free = {}
+    start = [0.0] * n
+    seq = []
+    while ready:
+        t0 = min(max(tm, free.get(ops[i]["eng"], 0.0)) for i, tm in ready.items())
+        cand = [i for i, tm in ready.items() if max(tm, free.get(ops[i]["eng"], 0.0)) <= t0 + 1e-9]
+        eng = ops[cand[0]]["eng"]
+        cand = [i for i, tm in ready.items() if ops[i]["eng"] == eng and tm <= t0 + 1e-9 + PAR["look"]]
+        i = max(cand, key=lambda c: (prio[c], -c))
+        start[i] = max(ready[i], free.get(eng, 0.0))
+        free[eng] = start[i] + ops[i]["dur"]
+        del ready[i]
+        seq.append(i)
+        for s in succ[i]:
+            left[s] -= 1
+            if left[s] == 0:
+                ready[s] = max(start[j] + d for j, d in pred[s].items())
+    return seq, start
+
+
+def emit(g, T, topo, core, ops, seq):
+    queue = {"dve": g.vector, "act": g.scalar, "pe": g.tensor, "pool": g, "sync": g.sync}
+    num, key = {}, {}
+    ends = {}
+    for i in seq:
+        if ops[i].get("auto") is not None:
+            ends.setdefault(ops[i]["auto"], []).append(i)
+    for members in ends.values():
+        ops[members[0]]["fl"]["start"] = True
+        ops[members[-1]]["fl"]["stop"] = True
+    ndma = 0
+    for i in seq:
+        o = ops[i]
+        if o["kind"] == "c":
+            num[o["eng"]] = num.get(o["eng"], 0) + 1
+            key[i] = (o["eng"], num[o["eng"]])
+        elif o["kind"] == "dma":
+            key[i] = ("dm%d" % ndma, 1)
+            ndma += 1
+    clock = {e: {} for e in queue}
+    snap, waits, needed = {}, {}, set()
+    for i in seq:
+        o = ops[i]
+        ck = clock[o["eng"]]
+        ws = []
+        if o["arrive"] is not None and ck.get(o["arrive"][0], 0) < 1:
+            ck[o["arrive"][0]] = 1
+            ws.append(("arrive", o["arrive"][0]))
+        deps = sorted([j for j in o["dep"] if j in key], key=lambda j: -key[j][1])
+        for j in deps:
+            s, c = key[j]
+            if ck.get(s, 0) < c:
+                ws.append(("op", j))
+                needed.add(j)
+                for s2, c2 in snap[j].items():
+                    if ck.get(s2, 0) < c2:
+                        ck[s2] = c2
+                ck[s] = c
+        waits[i] = ws
+        snap[i] = dict(ck)
+    count, value = {}, {}
+    for i in seq:
+        if i in needed and ops[i]["kind"] == "c":
+            count[ops[i]["eng"]] = count.get(ops[i]["eng"], 0) + 1
+            value[i] = count[ops[i]["eng"]]
+    rank = T.rank_of(core)
+
+    def arrival(name):
+        hop = HOPS[0][int(name[2])] if name[1] == "v" else HOPS[int(name[2])][int(name[3])]
+        sender = (rank + hop if name[1] == "r" else rank - hop) % NR
+        return len(topo.engines(T.cores[sender], core))
+    nsent = 0
+    for i in seq:
+        o = ops[i]
+        q = queue[o["eng"]]
+        for kind, j in waits[i]:
+            if kind == "arrive":
+                q.wait_ge(T.sem[j], arrival(j))
+            elif ops[j]["kind"] == "dma":
+                q.wait_ge(T.sem[key[j][0]], 16)
+            else:
+                q.wait_ge(T.sem[key[j][0]], value[j])
+        ins = o["fn"]()
+        if o["kind"] == "dma":
+            ins.then_inc(T.sem[key[i][0]], 16)
+        elif o["kind"] == "rem":
+            nsent += o["width"]
+        elif i in needed:
+            ins.then_inc(T.sem[o["eng"]], 1)
+    for i in seq:
+        if ops[i]["kind"] == "dma" and i not in needed:
+            g.sync.wait_ge(T.sem[key[i][0]], 16)
+    g.wait_ge(T.sem.sent, nsent)
+
+
+def rank_program(g, core, T, topo):
+    rank = T.rank_of(core)
+    if rank is None:
+        return
+    ops = build(g, core, T, topo, rank)
+    plan(ops)
+    seq, _ = order(ops)
+    emit(g, T, topo, core, ops, seq)

@@ -1,8 +1,6 @@
-import numpy as np
-from concourse.bass import DstId, RemoteDMATransfer
-from concourse.mybir import dt, AluOpType, AxisListType, ActivationFunctionType
+from concourse.mybir import AluOpType, ActivationFunctionType
 
-V, K, RO, NR = 3328, 256, 3, 6
+V, RO, NR = 3328, 3, 6
 CEN = 1664
 BIG = 8192.0
 MAGIC = 50331648.0
@@ -10,23 +8,24 @@ HALF = 12582912.0
 HOPS = ((1, 2), (3, 4), (5, 1))
 
 PAR = {
-    "yo": (3, 2, 2),
-    "ou": (0, 0, 0),
-    "yg": ((5, 3), (4, 2), (4, 2)),
-    "yu": ((2, 2), (3, 4), (3, 4)),
-    "late": (4, 3, 2),
-    "sg": 3,
-    "mins": (1, 3, 5, 6),
-    "nch": 5,
-    "indb": 2,
-    "early": 1, "dfirst": 0, "wfirst": 1, "bonus": (0.0, 0.0), "seed": 1, "jit": 0.0, "look": 0.0,
+    "yo": ((0, 2), (1, 2), (1, 2)),
+    "yg": (((2, 2), (2, 2)), ((1, 2), (2, 2)), ((1, 2), (2, 2))),
+    "yu": (((2, 2), (1, 1)), ((3, 2), (1, 1)), ((2, 2), (1, 2))),
+    "late": ((5, 0), (4, 0), (4, 0)),
+    "sg": (2, 1),
+    "mins": ((1, 3), (1, 2)),
+    "nch": 6,
+    "indb": 3,
+    "tree": 2,
+    "xzv": (1, 1),
+    "first": 2.0, "upper": 1.0, "bonus": (3.0, 6.0), "seed": 2325, "jit": 0.0, "look": 0.03,
 }
-COST = {"cy": 1.04e-3, "ga": 1.56, "sc": 3.8, "pe": 0.52e-3, "hop": 0.10, "same": 0.06, "dma": 2.0,
-        "rem": 3.5, "first": 2.0, "issue": 0.6}
+COST = {"cy": 1.08e-3, "ga": 1.75, "sc": 4.5, "pc": 0.53e-3, "dve": 0.0, "act": 0.0, "pe": 0.0, "hop": 0.2, "same": 0.18, "dma": 2.0,
+        "rem": 2.8, "first": 2.0, "issue": 0.6}
 
 SCRATCH = {
     "ri": ("sbuf", [128, V], "int32"),
-    "rw": ("sbuf", [128, V + 16], "float32"),
+    "rw": ("sbuf", [128, V + 32], "float32"),
     "xs": ("sbuf", [128, V + 32], "bfloat16"),
     "xu": ("sbuf", [128, V], "bfloat16"),
     "wi": ("sbuf", [128, 16], "int32"),
@@ -34,25 +33,26 @@ SCRATCH = {
     "d1": ("sbuf", [128, 4096], "float16"),
     "d2": ("sbuf", [128, 4096], "float16"),
     "mn": ("sbuf", [128, 1024], "bfloat16"),
-    "nb": ("sbuf", [128, 2048], "bfloat16"),
-    "bf": ("sbuf", [128, 8], "bfloat16"),
-    "thr": ("sbuf", [128, 256], "float16"),
+    "nb": ("sbuf", [128, 4096], "bfloat16"),
     "xn": ("sbuf", [128, 4096], "bfloat16"),
     "gg": ("sbuf", [128, 4096], "float32"),
-    "ab": ("sbuf", [128, 4096], "float32"),
-    "acc": ("sbuf", [128, 512], "float32"),
-    "c16": ("sbuf", [128, 256], "float16"),
+    "ab0": ("sbuf", [128, 2, 2048], "float32"),
+    "ab1": ("sbuf", [128, 2, 2048], "float32"),
+    "acc": ("sbuf", [128, 1024], "float32"),
+    "c16": ("sbuf", [128, 512], "float16"),
+    "w1": ("sbuf", [128, 512], "float16"),
+    "w2": ("sbuf", [128, 512], "float16"),
     "t2": ("sbuf", [128, 256], "float16"),
     "ol": ("sbuf", [128, 256], "uint16"),
-    "w1": ("sbuf", [128, 256], "float16"),
-    "w2": ("sbuf", [128, 256], "float16"),
     "tp": ("sbuf", [128, 256], "bfloat16"),
     "n32": ("sbuf", [128, 256], "float32"),
     "ee": ("sbuf", [128, 256], "float32"),
     "qe": ("sbuf", [128, 256], "float32"),
-    "zr": ("sbuf", [128, 256], "float32"),
-    "eq": ("sbuf", [128, 256], "float16"),
+    "zr": ("sbuf", [128, 512], "float32"),
+    "eq": ("sbuf", [128, 512], "float16"),
+    "o0": ("sbuf", [128, 256], "float16"),
     "ok": ("sbuf", [128, 256], "float16"),
+    "np_": ("sbuf", [128, 256], "float16"),
     "sn": ("sbuf", [128, 256], "float16"),
     "xz": ("sbuf", [128, 256], "bfloat16"),
     "wl": ("sbuf", [128, 16], "uint16"),
@@ -65,7 +65,7 @@ SCRATCH = {
     "so": ("sbuf", [128, 32], "uint16"),
     "ka": ("sbuf", [128, 256], "float32"),
     "kq": ("sbuf", [128, 384], "int32"),
-    "kr": ("sbuf", [128, 256], "float32"),
+    "kr": ("sbuf", [128, 128], "float32"),
     "kp": ("sbuf", [128, 16], "int32"),
     "kp2": ("sbuf", [128, 16], "int32"),
     "kf": ("sbuf", [128, 16], "float32"),
@@ -76,14 +76,17 @@ SCRATCH = {
     "j1": ("sbuf", [128, 256], "float16"),
     "bb": ("sbuf", [128, 256], "float16"),
     "bs": ("sbuf", [128, 256], "float16"),
-    "ib2": ("sbuf", [128, 128], "bfloat16"),
+    "bf": ("sbuf", [128, 8], "bfloat16"),
+    "thr": ("sbuf", [128, 256], "float16"),
     "ni": ("sbuf", [128, 128], "float16"),
     "i32": ("sbuf", [128, 128], "float32"),
     "ib": ("sbuf", [128, 128], "bfloat16"),
+    "ib2": ("sbuf", [128, 128], "bfloat16"),
     "nib": ("sbuf", [128, 128], "bfloat16"),
     "bo": ("sbuf", [128, 128], "float16"),
     "uu": ("sbuf", [128, 384], "float16"),
     "tri": ("sbuf", [128, 256], "float16"),
+    "dum": ("sbuf", [128, 8], "float32"),
 }
 for _t in range(RO):
     for _b in range(2):
@@ -99,7 +102,7 @@ for _b in range(8):
 
 SEMAPHORES = (["dve", "act", "pe", "pool", "sent", "av0", "av1"] + ["dm%d" % _i for _i in range(30)]
               + ["aq%d%d" % (_t, _b) for _t in range(RO) for _b in range(2)]
-              + ["ar%d%d" % (_t, _b) for _t in range(RO) for _b in range(2)])
+              + ["ar%d%d%d" % (_t, _b, _h) for _t in range(RO) for _b in range(2) for _h in range(2)])
 
 AL = AluOpType
 AF = ActivationFunctionType
@@ -139,6 +142,9 @@ def build(g, core, T, topo, rank):
     def ap(r):
         if len(r) == 2:
             return ap(r[0]).indirect(ap(r[1]))
+        if len(SCRATCH[r[0]][1]) == 3:
+            h = r[1] // 2048
+            return T[r[0]][:, h, r[1] - 2048 * h:r[2] - 2048 * h]
         return T[r[0]][:, r[1]:r[2]] if r[3] == 1 else T[r[0]][:, r[1]:r[2]:r[3]]
 
     def flat(rs):
@@ -149,7 +155,7 @@ def build(g, core, T, topo, rank):
         return out
 
     def add(eng, fn, reads, writes, dur, lat=0.0, kind="c", arrive=None, after=None):
-        ops.append({"eng": eng, "fn": fn, "r": flat(reads), "w": flat(writes), "dur": dur, "lat": lat, "kind": kind,
+        ops.append({"eng": eng, "fn": fn, "r": flat(reads), "w": flat(writes), "dur": dur + C.get(eng, 0.0), "lat": lat, "kind": kind,
                     "arrive": arrive, "after": after, "bonus": ahead[0]})
         return len(ops) - 1
 
@@ -190,12 +196,10 @@ def build(g, core, T, topo, rank):
         d = 0.065 + cnt(out) * C["ga"] * C["cy"] if len(in0) == 2 else max(cnt(out), 64) * C["cy"] + 0.03
         return add("act", fn, [in0], [out], d, **kw)
 
-    def mm(out, lhs, rhs, start, stop, fam=None, auto=None, **kw):
-        d = max(64, cnt(rhs)) * C["pe"] * (4 if SCRATCH[rhs[0]][2] == "float32" else 1)
-        fl = {"start": start, "stop": stop}
-        i = add("pe", lambda: g.tensor.matmul(ap(out), ap(lhs), ap(rhs), fl["start"], fl["stop"]), [lhs, rhs], [out], d,
-                lat=0.05, **kw)
-        ops[i].update({"fam": fam, "auto": auto, "fl": fl})
+    def mm(out, lhs, rhs, start, stop, fam=None, **kw):
+        d = max(64, cnt(rhs)) * C["pc"] * (4 if SCRATCH[rhs[0]][2] == "float32" else 1)
+        i = add("pe", lambda: g.tensor.matmul(ap(out), ap(lhs), ap(rhs), start, stop), [lhs, rhs], [out], d, lat=0.05, **kw)
+        ops[i]["fam"] = fam
         return i
 
     def group(out, terms):
@@ -222,7 +226,7 @@ def build(g, core, T, topo, rank):
         rid, pid, _ = topo.addr(to)
 
         def fn():
-            return g.remote_dma(T[dst_name][:, 0:cnt(src)], ap(src), T.sem[sem], T.sem.sent, pid, rid, topo.mask(core, to))
+            return g.remote_dma(T[dst_name][:, src[1]:src[2]], ap(src), T.sem[sem], T.sem.sent, pid, rid, topo.mask(core, to))
         i = add("pool", fn, [src], [], C["issue"], lat=C["rem"] + (C["first"] if first else 0.0), kind="rem")
         ops[i]["width"] = len(topo.engines(core, to))
         return i
@@ -266,28 +270,30 @@ def build(g, core, T, topo, rank):
     act(rf("ib"), rf("i32"), AF.Identity)
     act(rf("ib2"), rf("i32"), AF.Identity, scale=2.0)
     ts(rf("bs"), rf("bb"), BIG, None, AL.mult)
-    add("dve", lambda: g.vector.memset(T.rw[:, V:V + 16], 0.0), [], [rf("rw", V, V + 16)], 0.07)
+    add("dve", lambda: g.vector.memset(T.rw[:, V:V + 32], 0.0), [], [rf("rw", V, V + 32)], 0.07)
     add("dve", lambda: g.vector.memset(T.bo[:], 1.0), [], [rf("bo")], 0.07)
     add("dve", lambda: g.vector.memset(T.thr[:], 7.5), [], [rf("thr")], 0.14)
+    add("dve", lambda: g.vector.memset(T.qq[:], 0.0), [], [rf("qq")], 0.07)
     cp(rf("bf"), rf("bb", 0, 128, 16))
     iota(rf("kq"), [[-1, 3], [0, 8], [1, 16]], 15, 0)
-    iota(rf("kr"), [[0, 16], [1, 16]], 0, 0)
-    iota(rf("kl"), [[1, 16]], 0, 0)
+    iota(rf("kr"), [[0, 8], [1, 16]], 0, 0)
+    iota(rf("kl"), [[-1, 2], [1, 8]], 0, 0)
     ts(rf("kq"), rf("kq"), 15, None, AL.bitwise_and)
     for t in range(RO):
         ts(rf("uu", 128 * t, 128 * t + 128), rf("kq", 128 * t, 128 * t + 128), rf("kf", 4 + t, 5 + t), None, AL.is_gt)
-    ts(rf("tri"), rf("kr"), PR, BIG, AL.is_le, AL.mult)
+    ts(rf("tri", 0, 128), rf("kr"), PR, BIG, AL.is_le, AL.mult)
+    add("dve", lambda: g.vector.memset(T.tri[:, 128:256], BIG), [], [rf("tri", 128, 256)], 0.07)
     cp(rf("cl"), rf("kl"))
-    ts(rf("kf", 10, 11), PR, V - CEN - 1 - BIG, None, AL.add)
+    iota(rf("dum"), [[0, 4], [16, 2]], int(V - CEN - 1 - BIG), 0)
+    ts(rf("dum"), rf("dum"), PR, None, AL.add)
 
     cp(rf("wl"), rf("wi"))
     ts(rf("w16"), rf("wi"), float(CEN), None, AL.subtract)
     wsend = []
-    if PAR["wfirst"]:
-        for b in range(2):
-            group(rf("p%d" % (b + 1), 256, 272), [(jsl("jj", 16 * (1 + b)), rf("w16"))])
-            ts(rf("vs%d" % b), rf("p%d" % (b + 1), 256, 272), float(CEN), None, AL.add)
-            wsend.append(send(rf("vs%d" % b), "vl%d" % b, "av%d" % b, (rank + HOPS[0][b]) % NR, first=True))
+    for b in range(2):
+        group(rf("p%d" % (b + 1), 256, 272), [(jsl("jj", 16 * (1 + b)), rf("w16"))])
+        ts(rf("vs%d" % b), rf("p%d" % (b + 1), 256, 272), float(CEN), None, AL.add)
+        wsend.append(send(rf("vs%d" % b), "vl%d" % b, "av%d" % b, (rank + HOPS[0][b]) % NR, first=True))
     for i in range(nch):
         a, b = i * step, (V if i == nch - 1 else (i + 1) * step)
         ts(rf("rw", a, b), rf("ri", a, b), float(CEN), None, AL.subtract)
@@ -298,254 +304,271 @@ def build(g, core, T, topo, rank):
         ring["p"] += 1
         return "p%d" % banks[ring["p"] % len(banks)]
 
-    def count_by_walkers(dbuf, k, cbank, c0, shift, fam):
-        x = (16 * shift) % 128
-        for h in range(2):
-            mm(rf(cbank, c0 + 128 * h + k, c0 + 128 * h + 128, 16), rf(dbuf, 256 * k + 128 * h, 256 * k + 128 * h + 128),
-               rf("bf") if dbuf == "nb" else rf("bb", x, x + 128, 16), True, True, fam=fam)
+    def twice(buf):
+        cp(rf(buf, 0, 128), rf(buf, 128, 256))
+        cp(rf(buf, 384, 512), rf(buf, 256, 384))
 
-    def likeness(dbuf, lists, wref, ns, nu, wps, banks, arrive, counter, rows=(0, 16), cut=16, after=None):
+    def count_rows(dbuf, h, k, cbank, c0, shift, fam):
+        x = (16 * shift) % 128
+        a = 2048 * h + 128 * k
+        mm(rf(cbank, c0 + k, c0 + 128, 16), rf(dbuf, a, a + 128),
+           rf("bf") if dbuf == "nb" else rf("bb", x, x + 128, 16), True, True, fam=fam)
+
+    def likeness(dbuf, h, lists, wref, ns, nu, wps, arrive, cbank, shift, fam, part=(0, 8), cut=8, after=None):
         kw = {"arrive": arrive, "after": after}
         units = []
-        npairs = ns + nu
+        nn = ns + nu
         kinds = sorted([((i + 0.5) / ns, "s") for i in range(ns)] + [((i + 0.6) / nu, "u") for i in range(nu)])
-        for i in range(npairs):
-            units.append(((i + 1.0) / npairs, kinds[i][1], 2 * i, 2 * i + 2))
-        k, nd = 2 * npairs, 16 - 2 * npairs
-        while k < 16:
-            e = min(cut if k < cut else 16, k + PAR["indb"])
-            units.append(((e - 2.0 * npairs) / nd - 1e-3, "v", k, e))
+        for i in range(nn):
+            units.append(((i + 1.0) / nn, kinds[i][1], 2 * i, 2 * i + 2))
+        k, nd = 2 * nn, 8 - 2 * nn
+        while k < 8:
+            e = min(cut if k < cut else 8, k + PAR["indb"])
+            units.append(((e - 2.0 * nn) / nd - 1e-3, "v", k, e))
             k = e
         units.sort()
+        d0, l0 = 2048 * h, 128 * h
         for _, how, k0, k1 in units:
-            if k0 < rows[0] or k0 >= rows[1]:
+            if k0 < part[0] or k0 >= part[1]:
                 continue
-            dd = rf(dbuf, 256 * k0, 256 * k1)
+            dd = rf(dbuf, d0 + 256 * k0, d0 + 256 * k1)
             if how != "v":
                 c0 = 512 * (ring["g"] % 8)
                 ring["g"] += 1
-                act(rf("gg", c0, c0 + 512), (RW, rf(lists, 16 * k0, 16 * k1)), AF.Copy, **kw)
+                act(rf("gg", c0, c0 + 512), (RW, rf(lists, l0 + 16 * k0, l0 + 16 * k1)), AF.Copy, **kw)
             if how == "s":
-                pb = bank(banks)
-                for h in range(2):
-                    group(rf(pb, 256 * h, 256 * h + 256),
-                          [(rf("ni"), wref), (rf("i32"), rf("gg", c0 + 256 * h, c0 + 256 * h + 256))])
+                pb = bank((4, 5, 6))
+                for i in range(2):
+                    group(rf(pb, 256 * i, 256 * i + 256),
+                          [(rf("ni"), wref), (rf("i32"), rf("gg", c0 + 256 * i, c0 + 256 * i + 256))])
                 ts(dd, rf(pb), MAGIC, MAGIC, AL.add, AL.is_equal)
             else:
                 for k in range(k0, k1):
-                    dk = rf(dbuf, 256 * k, 256 * k + 256)
+                    dk = rf(dbuf, d0 + 256 * k, d0 + 256 * k + 256)
                     if how == "u":
                         tt(dk, rf("gg", c0 + 256 * (k - k0), c0 + 256 * (k - k0) + 256), wps, AL.subtract)
                     else:
-                        tt(dk, (RW, rf(lists, 16 * k, 16 * k + 16)), wref, AL.subtract, **kw)
+                        tt(dk, (RW, rf(lists, l0 + 16 * k, l0 + 16 * k + 16)), wref, AL.subtract, **kw)
                 ts(dd, dd, MAGIC, MAGIC, AL.add, AL.is_equal)
-            for k in range(k0, k1):
-                counter(k)
+            for k in range(2 * k0, 2 * k1):
+                count_rows(dbuf, h, k, cbank, 128 * h, shift, fam)
+
+    def halve(s, levels, after):
+        buf = "ab%d" % (s % 2)
+        for lv in levels:
+            w = 1024 >> lv
+            dma("pool", (lambda w=w: g.dma_start(T[buf][:, :, 0:w], T[buf][:, :, w:2 * w], accum_op=AL.add)),
+                [rf(buf, 0, 4096)], [rf(buf, 0, 4096)], 128 * 16 * w, after=after)
+            if lv == 3:
+                dma("sync", lambda: g.sync.dma_start(T.y[:, 256 * s:256 * s + 256], T[buf][:, :, 0:128]),
+                    [rf(buf, 0, 4096)], [], 128 * 1024)
+
+    def choose(t, h, answers):
+        a, b, m0, m1 = 128 * h, 128 * h + 128, 8 * h, 8 * h + 8
+        pb = "p1" if h else "p2"
+        group(rf(pb, 0, 128), [(rf("o0", a, b), I16)]
+              + [(rf("rl%d%d" % (t, i), a, b), I16, {"arrive": ("ar%d%d%d" % (t, i, h), answers[(i, h)])}) for i in range(2)])
+        ts(rf("ok", a, b), rf(pb, 0, 128), 95.5, -BIG, AL.is_ge, AL.mult)
+        group(rf(pb, 128, 256), [(rf("uu", 128 * t, 128 * t + 128), rf("ok", a, b)), (I16, rf("c16", 128 + a, 128 + b)),
+                                 (rf("nib"), rf("tp", a, b))])
+        ts(rf("sn", a, b), rf(pb, 128, 256), BIG - 1666.0, BIG, AL.max, AL.subtract)
+        zs = rf("p3", 256 + m0, 256 + m1)
+        group(zs, [(jsl("bb", r), rf("sn", a + r, b, 16)) for r in range(16)])
+        ts(rf("nh", m0, m1), zs, -16 * 1666.0 + 0.5, -BIG, AL.is_gt, AL.mult)
+        ts(rf("qq", m0, m1), zs, 15 * 1666.0, None, AL.add)
+        tt(rf("hh", m0, m1), rf("nh", m0, m1), rf("t16", m0, m1), AL.add)
+        tt(rf("z16", m0, m1), rf("hh", m0, m1), rf("qq", m0, m1), AL.max)
+        ts(rf("wl", m0, m1), rf("z16", m0, m1), float(CEN + 1), None, AL.add)
+        if PAR["xzv"][h]:
+            xz = cp(rf("xz", a, b), (rf("xu"), rf("wl", m0, m1)))
+        else:
+            xz = act(rf("xz", a, b), (rf("xu"), rf("wl", m0, m1)), AF.Copy)
+        if t == RO - 1:
+            return
+        ts(rf("w16", m0, m1), rf("z16", m0, m1), 1.0, None, AL.add)
+        for j in range(2):
+            group(rf(pb, 256 + 128 * j, 384 + 128 * j), [(I16, rf("tri", 128 * j, 128 * j + 128)), (rf("bo"), rf("sn", a, b))])
+        act(rf("zr", 2 * a, 2 * b), rf(pb, 256, 512), AF.Identity, bias=15 * 1666.0, after=[xz])
+        tt(rf("ee", a, b), (RW, rf("wl", m0, m1)), rf("n32", a, b), AL.subtract)
+        tt(rf("eq", 2 * a, 2 * b), (rf("qq", m0, m1), rf("cl")), rf("zr", 2 * a, 2 * b), AL.is_equal)
+        tt(rf("eq", 2 * a, 2 * a + 128), rf("eq", 2 * a, 2 * a + 128), rf("eq", 2 * a + 128, 2 * b), AL.add)
+        ps = rf(pb, 0, 8)
+        group(ps, [(I16, rf("nh", m0, m1)), (I16, rf("z16", m0, m1))]
+              + [(jsl("bs", r), rf("eq", 2 * a + r, 2 * a + 128, 16)) for r in range(16)])
+        tt(rf("hh", m0, m1), ps, rf("dum", 0, 8), AL.min)
+        ts(rf("so", m0, m1), rf("hh", m0, m1), CEN + 1 + BIG, None, AL.add)
+
+    def differ(pb, h, i, lhs, close):
+        mm(rf(pb), rf(lhs), rf("xn", 2048 * h + 512 * i, 2048 * h + 512 * i + 512), True, False)
+        for j in range(4):
+            mm(rf(pb, 128 * j, 128 * j + 128), rf("nib"), rf("xz", 128 * h, 128 * h + 128), False, close and j == 3)
+
+    def near(t, h):
+        sg, buf = PAR["sg"][h], "ab%d" % (t % 2)
+        a, b = 128 * h, 128 * h + 128
+        for i in [3, 0, 2, 1]:
+            pb = "p%d" % (4 + i)
+            c0 = 2048 * h + 512 * i
+            differ(pb, h, i, "ib", True)
+            if i < sg:
+                act(rf(buf, c0, c0 + 512), rf(pb), AF.Abs)
+                act(rf("nb", c0, c0 + 512), rf(buf, c0, c0 + 512), AF.Sign, bias=0.5 + 2.0 ** -21, scale=-1.0)
+            else:
+                ts(rf("d0", c0, c0 + 512), rf(pb), HALF, HALF, AL.add, AL.is_equal)
+            for k in range(4 * i, 4 * i + 4):
+                count_rows("nb" if i < sg else "d0", h, k, "p0", 256 + a, 0, "near%d%d" % (t, h))
+        for i in range(3, sg - 1, -1):
+            act(rf(buf, 2048 * h + 512 * i, 2048 * h + 512 * i + 512), rf("p%d" % (4 + i)), AF.Abs)
+        tt(rf("np_", a, b), rf("p0", 256 + a, 256 + b), rf("thr", a, b), AL.is_lt)
+        pb = "p1" if h else "p2"
+        group(rf(pb, 384, 512), [(rf("np_", a, b), I16)])
+        tt(rf("qe", a, b), rf(pb, 384, 512), rf("ee", a, b), AL.mult)
+        for i in range(4):
+            ab = rf(buf, 2048 * h + 512 * i, 2048 * h + 512 * i + 512)
+            act(ab, ab, AF.Exp, scale=-1.0)
+
+    def rewrite(h):
+        win = rf("rw")
+        for m in range(8 * h + 6, 8 * h - 2, -2):
+            add("dve", (lambda m=m: g.vector.tensor_tensor(ap((win, rf("so", m, m + 2))), T.qe[:, 16 * m:16 * m + 32],
+                                                           T.n32[:, 16 * m:16 * m + 32], AL.add)),
+                [rf("so", m, m + 2), rf("qe", 16 * m, 16 * m + 32), rf("n32", 16 * m, 16 * m + 32)], [win],
+                0.05 + 32 * C["sc"] * C["cy"])
+
+    def sums(t, h):
+        mins, buf, xb, s0 = PAR["mins"][h], "ab%d" % (t % 2), ("p1" if h else "p2"), 512 * h
+        if mins:
+            for j in range(4):
+                group(rf(xb, 128 * j, 128 * j + 128), [(rf("ib"), rf("xz", 128 * h, 128 * h + 128))])
+        for i in range(4):
+            pb = "p%d" % (4 + i)
+            c0 = 2048 * h + 512 * i
+            if i in mins:
+                differ(pb, h, i, "nib", False)
+                mn = rf("mn", 512 * (i % 2), 512 * (i % 2) + 512)
+                tt(mn, rf("xn", c0, c0 + 512), rf(xb), AL.min)
+                mm(rf(pb), rf("ib2"), mn, False, True)
+                act(rf(pb), rf(pb), AF.Exp)
+            else:
+                differ(pb, h, i, "ib", True)
+                act(rf(buf, c0, c0 + 512), rf(pb), AF.Abs)
+                act(rf(pb), rf(buf, c0, c0 + 512), AF.Exp, scale=-1.0)
+            if i == 0:
+                cp(rf("acc", s0, s0 + 512), rf(pb))
+            elif i < 3:
+                tt(rf("acc", s0, s0 + 512), rf(pb), rf("acc", s0, s0 + 512), AL.add)
+            else:
+                for w in (256, 128):
+                    tt(rf("acc", s0, s0 + w), rf("acc", s0, s0 + w), rf("acc", s0 + w, s0 + 2 * w), AL.add)
+                for j in range(4):
+                    tt(rf("acc", s0, s0 + 128), rf(pb, 128 * j, 128 * j + 128), rf("acc", s0, s0 + 128), AL.add)
+        dma("sync", lambda: g.sync.dma_start(T.y[:, 256 * t + 128 * h:256 * t + 128 * h + 128], T.acc[:, s0:s0 + 128]),
+            [rf("acc", s0, s0 + 128)], [], 128 * 512)
 
     for t in range(RO):
         last = t == RO - 1
-        tt_ = t + 1
-        if t == 0 and PAR["early"]:
-            ts(rf("c16"), (rf("ri"), rf("wl")), float(CEN), None, AL.subtract)
+        CC = rf("c16", 128, 384)
+        if t == 0:
+            ts(CC, (rf("ri"), rf("wl")), float(CEN), None, AL.subtract)
         else:
-            cp(rf("c16"), (RW, rf("wl")))
+            cp(CC, (RW, rf("wl")))
         act(rf("tp"), (RW, rf("wl")), AF.Relu, bias=-float(V * (V - CEN - 2)), scale=float(V))
         for be in range(8):
-            add("dve", (lambda be=be: g.vector.transpose(T.t2[:, be:256:8], T.c16[:, 32 * be:32 * be + 32])),
-                [rf("c16", 32 * be, 32 * be + 32)], [rf("t2", be, 256, 8)], 64 * C["cy"])
+            o = rf("t2", 128 * (be // 4) + be % 4, 128 * (be // 4) + 128, 4)
+            i = rf("c16", 128 + 32 * be, 160 + 32 * be)
+            add("dve", (lambda o=o, i=i: g.vector.transpose(ap(o), ap(i))), [i], [o], 64 * C["cy"])
         sends = []
         for b, pb in ((0, "p1"), (1, "p2"), (2, "p3")):
-            s = 0 if b == 2 else tt_ + b
-            for gp in range(2):
-                group(rf(pb, gp, 256, 2),
-                      [(jsl("j%d" % gp, 16 * (ga - gp + s)), rf("t2", 128 * ga, 128 * ga + 128)) for ga in range(2)])
+            s = 0 if b == 2 else t + 1 + b
+            for h in range(2):
+                for gp in range(2):
+                    group(rf(pb, 128 * h + gp, 128 * h + 128, 2),
+                          [(jsl("j%d" % gp, 16 * (ga - gp + s)), rf("t2", 128 * h + 64 * ga, 128 * h + 64 * ga + 64))
+                           for ga in range(2)])
             if b < 2:
-                wide = 256 if t == 0 and PAR["wfirst"] else 272
+                wide = 256 if t == 0 else 272
                 if wide > 256:
                     group(rf(pb, 256, 272), [(jsl("jj", 16 * s), rf("w16"))])
                 ts(rf("qs%d%d" % (t, b), 0, wide), rf(pb, 0, wide), float(CEN), None, AL.add)
                 sends.append(send(rf("qs%d%d" % (t, b), 0, wide), "ql%d%d" % (t, b), "aq%d%d" % (t, b),
-                                  (rank + HOPS[t][b]) % NR, first=(t == 0 and wide > 256)))
+                                  (rank + HOPS[t][b]) % NR))
             else:
                 ts(rf("ol"), rf(pb, 0, 256), float(CEN), None, AL.add)
+        twice("c16")
         if t == 0:
             for buf, rep in ((rf("uu"), 3), (rf("bo"), 1)):
                 asel(buf, [[0, rep], [-16, 8], [0, 16]], AL.is_ge, 0.0, 0, 1, after=sends)
                 asel(buf, [[0, rep], [16, 8], [0, 16]], AL.is_ge, 0.0, 15, -1)
             asel(rf("uu"), [[0, 3], [-1, 128]], AL.not_equal, -1.0, 0, 1)
-            if PAR["sg"]:
-                asel(rf("thr"), [[0, 16], [1, 16]], AL.is_ge, -0.5, -2 * PAR["sg"], 0, after=sends)
+            asel(rf("tri", 128, 256), [[0, 4], [1, 2], [0, 16]], AL.is_equal, 0.0, 0, 0, after=sends)
+            for h in range(2):
+                if PAR["sg"][h]:
+                    asel(rf("thr", 128 * h, 128 * h + 128), [[0, 8], [1, 16]], AL.is_ge, -0.5, -4 * PAR["sg"][h], 0, after=sends)
         else:
-            w = 2048
-            prev = sends
-            while w >= 256:
-                dma("pool", (lambda w=w: g.dma_start(T.ab[:, 0:w], T.ab[:, w:2 * w], accum_op=AL.add)),
-                    [rf("ab", 0, 2 * w)], [rf("ab", 0, w)], 128 * 8 * w, after=prev)
-                prev = None
-                w //= 2
-            dma("sync", (lambda t=t: g.sync.dma_start(T.y[:, 256 * (t - 1):256 * t], T.ab[:, 0:256])),
-                [rf("ab", 0, 256)], [], 128 * 1024)
+            halve(t - 1, range(PAR["tree"]), sends)
         ts(rf("t16"), rf("w16"), float(V - CEN - 1), -float(V), AL.is_equal, AL.mult)
         tt(rf("t16"), rf("t16"), rf("w16"), AL.add)
         if not last:
-            group(rf("p3", 0, 256), [(I16, rf("c16")), (rf("nib"), rf("tp"))])
+            group(rf("p3", 0, 256), [(I16, CC), (rf("nib"), rf("tp"))])
             act(rf("n32"), rf("p3", 0, 256), AF.Identity, bias=1.0)
-        if PAR["ou"][t]:
-            group(rf("p3", 256, 512), [(I16, rf("c16"))])
 
         arr = [("aq%d%d" % (t, b), sends[b]) for b in range(2)]
-        answers = []
-        nu = PAR["yu"][t]
-        banks = (4, 5, 6) if max(nu) else (4, 5, 6, 7)
         for b in range(2):
-            ql = "ql%d%d" % (t, b)
-            ahead[0] = PAR["bonus"][b]
-            if t == 0 and PAR["wfirst"]:
-                cp(rf("w%d" % (b + 1)), (RW, rf("vl%d" % b)), arrive=("av%d" % b, wsend[b]))
+            wb = "w%d" % (b + 1)
+            if t == 0:
+                cp(rf(wb, 128, 384), (RW, rf("vl%d" % b)), arrive=("av%d" % b, wsend[b]))
             else:
-                cp(rf("w%d" % (b + 1)), (RW, rf(ql, 256, 272)), arrive=arr[b])
-            ahead[0] = 0.0
-            if nu[b]:
-                group(rf("p7", 256 * b, 256 * b + 256), [(I16, rf("w%d" % (b + 1)))])
-        own = "own%d" % t
-        cut = 16 - PAR["late"][t]
+                cp(rf(wb, 128, 384), (RW, rf("ql%d%d" % (t, b), 256, 272)), arrive=arr[b])
+            twice(wb)
 
-        def own_rows(rows, after):
-            likeness("d0", "ol", rf("c16"), PAR["yo"][t], PAR["ou"][t], rf("p3", 256, 512), banks, None,
-                     lambda k: mm(rf("p0", 0, 256), jsl("bb", k), rf("d0", 256 * k, 256 * k + 256), False, False, fam=own,
-                                  auto=own), rows, cut, after)
-        own_rows((0, cut), None)
-        made = []
-        for b in range(2):
-            ql = "ql%d%d" % (t, b)
-            pb = "p%d" % (b + 1)
-            ahead[0] = PAR["bonus"][b]
-            likeness("d%d" % (b + 1), ql, rf("w%d" % (b + 1)), PAR["yg"][t][b], nu[b], rf("p7", 256 * b, 256 * b + 256), banks,
-                     arr[b], lambda k: count_by_walkers("d%d" % (b + 1), k, pb, 0, tt_ + b, ql))
-            made.append(len(ops) - 1)
-            ts(rf("rs%d%d" % (t, b)), rf(pb, 0, 256), 9.5, 32.0, AL.is_ge, AL.mult)
-            answers.append(send(rf("rs%d%d" % (t, b)), "rl%d%d" % (t, b), "ar%d%d" % (t, b), (rank - HOPS[t][b]) % NR))
+        def own_rows(h, late, after):
+            cut = 8 - PAR["late"][t][h]
+            likeness("d0", h, "ol", rf("c16", 256 * h, 256 * h + 256), PAR["yo"][t][h], 0, None, None, "p0", 0,
+                     "own%d" % t, (cut, 8) if late else (0, cut), cut, after)
+        for h in (1, 0):
+            own_rows(h, False, None)
+        answers, made = {}, []
+        for h in (1, 0):
+            for b in range(2):
+                ahead[0] = PAR["bonus"][h] + (0.0 if b else PAR["first"])
+                wb, pb = rf("w%d" % (b + 1), 256 * h, 256 * h + 256), "p%d" % (b + 1)
+                nu, wps = PAR["yu"][t][b][h], rf("p7", 256 * b, 256 * b + 256)
+                if nu:
+                    group(wps, [(I16, wb)])
+                likeness("d%d" % (b + 1), h, "ql%d%d" % (t, b), wb, PAR["yg"][t][b][h], nu, wps, arr[b], pb, t + 1 + b,
+                         "g%d%d%d" % (t, b, h))
+                rs = rf("rs%d%d" % (t, b), 128 * h, 128 * h + 128)
+                made.append(ts(rs, rf(pb, 128 * h, 128 * h + 128), 9.5, 32.0, AL.is_ge, AL.mult))
+                answers[(b, h)] = send(rs, "rl%d%d" % (t, b), "ar%d%d%d" % (t, b, h), (rank - HOPS[t][b]) % NR)
         ahead[0] = 0.0
-        last_ind = max(i for i in range(made[1]) if ops[i]["eng"] == "dve")
-        own_rows((cut, 16), [last_ind])
-        for i in range(8):
-            act(rf("xn", 512 * i, 512 * i + 512), (XS, rf("ol", 32 * i, 32 * i + 32)), AF.Copy)
-        for b in range(2):
-            for h in range(2):
-                mm(rf("p0", 128 * h, 128 * h + 128), rf("rl%d%d" % (t, b), 128 * h, 128 * h + 128), I16, False, False,
-                   auto=own, arrive=("ar%d%d" % (t, b), answers[b]))
-
-        mm(rf("p1", 0, 256), I16, rf("c16"), True, False)
-        mm(rf("p1", 0, 256), rf("nib"), rf("tp"), False, False)
-        ts(rf("ok"), rf("p0", 0, 256), 73.5, -BIG, AL.is_ge, AL.mult)
-        mm(rf("p1", 0, 256), rf("uu", 128 * t, 128 * t + 128), rf("ok"), False, True)
-        ts(rf("sn"), rf("p1", 0, 256), BIG - 1666.0, BIG, AL.max, AL.subtract)
-        group(rf("p3", 256, 272), [(jsl("bb", r), rf("sn", r, 256, 16)) for r in range(16)])
-        ts(rf("nh"), rf("p3", 256, 272), -16 * 1666.0 + 0.5, -BIG, AL.is_gt, AL.mult)
-        ts(rf("qq"), rf("p3", 256, 272), 15 * 1666.0, None, AL.add)
-        tt(rf("hh"), rf("nh"), rf("t16"), AL.add)
-        tt(rf("z16"), rf("hh"), rf("qq"), AL.max)
-        ts(rf("wl"), rf("z16"), float(CEN + 1), None, AL.add)
-        xz = act(rf("xz"), (rf("xu"), rf("wl")), AF.Copy)
-        if not last:
-            ts(rf("w16"), rf("z16"), 1.0, None, AL.add)
-            group(rf("p1", 256, 512), [(I16, rf("tri")), (rf("bo"), rf("sn"))])
-            act(rf("zr"), rf("p1", 256, 512), AF.Identity, bias=15 * 1666.0, after=[xz])
-            tt(rf("ee"), (RW, rf("wl")), rf("n32"), AL.subtract)
-            tt(rf("eq"), (rf("qq"), rf("cl")), rf("zr"), AL.is_equal)
-            group(rf("p3", 288, 304), [(I16, rf("nh")), (I16, rf("z16"))]
-                  + [(jsl("bs", r), rf("eq", r, 256, 16)) for r in range(16)])
-            ts(rf("so", 0, 32, 2), rf("p3", 288, 304), rf("kf", 10, 11), CEN + 1 + BIG, AL.min, AL.add)
-
-        banks = (4, 5, 6, 7, 2)
-        if last:
-            mins = PAR["mins"]
-            if mins:
-                for h in range(2):
-                    group(rf("p0", 256 * h, 256 * h + 256), [(rf("ib"), rf("xz"))])
-        elif PAR["sg"]:
-            sg = PAR["sg"]
-            slots = {}
-            todo = []
-            for i in range(8):
-                j = sg + i
-                pair = ([i] if i < sg else []) + ([j] if j < 8 else [])
-                todo += pair[::-1] if i < PAR["dfirst"] else pair
-            spare = list(banks)
-            for i in todo:
-                pb = "p%d" % spare.pop(0)
-                slots[i] = pb
-                ab = rf("ab", 512 * i, 512 * i + 512)
-                mm(rf(pb), rf("ib"), rf("xn", 512 * i, 512 * i + 512), True, False)
-                for h in range(2):
-                    mm(rf(pb, 256 * h, 256 * h + 256), rf("nib"), rf("xz"), False, h == 1)
-                if i < sg:
-                    act(ab, rf(pb), AF.Abs)
-                    spare.append(int(pb[1]))
-                    act(rf("nb", 512 * i, 512 * i + 512), ab, AF.Sign, bias=0.5 + 2.0 ** -21, scale=-1.0)
-                else:
-                    ts(rf("d0", 512 * i, 512 * i + 512), rf(pb), HALF, HALF, AL.add, AL.is_equal)
-                for k in (2 * i, 2 * i + 1):
-                    count_by_walkers("nb" if i < sg else "d0", k, "p0", 256, 0, "near%d" % t)
-            for i in range(sg, 8):
-                act(rf("ab", 512 * i, 512 * i + 512), rf(slots[i]), AF.Abs)
-        for i in range(8 if last or not PAR["sg"] else 0):
-            pb = bank(banks)
-            xn = rf("xn", 512 * i, 512 * i + 512)
-            ab = rf("ab", 512 * i, 512 * i + 512)
-            bymin = last and i in mins
-            mm(rf(pb), rf("nib" if bymin else "ib"), xn, True, False)
-            for h in range(2):
-                mm(rf(pb, 256 * h, 256 * h + 256), rf("nib"), rf("xz"), False, h == 1 and not bymin)
-            if bymin:
-                mn = rf("mn", 512 * (i % 2), 512 * (i % 2) + 512)
-                tt(mn, xn, rf("p0"), AL.min)
-                mm(rf(pb), rf("ib2"), mn, False, True)
-                act(rf(pb), rf(pb), AF.Exp)
-            else:
-                act(ab, rf(pb), AF.Abs)
-            if last:
-                if not bymin:
-                    act(rf(pb), ab, AF.Exp, scale=-1.0)
-                if i == 0:
-                    cp(rf("acc"), rf(pb))
-                elif i < 7:
-                    tt(rf("acc"), rf(pb), rf("acc"), AL.add)
-                else:
-                    tt(rf("acc", 0, 256), rf("acc", 0, 256), rf("acc", 256, 512), AL.add)
-                    for h in range(2):
-                        tt(rf("acc", 0, 256), rf(pb, 256 * h, 256 * h + 256), rf("acc", 0, 256), AL.add)
-            else:
-                ts(rf("d0", 512 * i, 512 * i + 512), ab, 0.5, None, AL.is_le)
-                for k in (2 * i, 2 * i + 1):
-                    count_by_walkers("d0", k, "p0", 256, 0, "near%d" % t)
-        if last:
-            dma("sync", (lambda t=t: g.sync.dma_start(T.y[:, 256 * t:256 * t + 256], T.acc[:, 0:256])),
-                [rf("acc", 0, 256)], [], 128 * 1024)
-            break
+        if t > 0:
+            halve(t - 1, range(PAR["tree"], 4), list(answers.values()))
+        own_rows(1, True, made)
         for h in (1, 0):
-            a, b = 128 * h, 128 * h + 128
-            tt(rf("ok", a, b), rf("p0", 256 + a, 256 + b), rf("thr", a, b), AL.is_lt)
-        for h in (1, 0):
-            a, b = 128 * h, 128 * h + 128
-            pb = "p1" if h else "p3"
-            group(rf(pb, a, b), [(rf("ok", a, b), I16)])
-            tt(rf("qe", a, b), rf(pb, a, b), rf("ee", a, b), AL.mult)
-        win = rf("rw")
-        for m in range(15, -1, -1):
-            add("dve", (lambda m=m: g.vector.tensor_tensor(ap((win, rf("so", 2 * m, 2 * m + 1))), T.qe[:, 16 * m:16 * m + 16],
-                                                           T.n32[:, 16 * m:16 * m + 16], AL.add)),
-                [rf("so", 2 * m, 2 * m + 1), rf("qe", 16 * m, 16 * m + 16), rf("n32", 16 * m, 16 * m + 16)], [win],
-                0.05 + 16 * C["sc"] * C["cy"])
-        for i in range(4):
-            ab = rf("ab", 1024 * i, 1024 * i + 1024)
-            act(ab, ab, AF.Exp, scale=-1.0)
+            for i in range(4):
+                c0 = 2048 * h + 512 * i
+                act(rf("xn", c0, c0 + 512), (XS, rf("ol", c0 // 16, c0 // 16 + 32)), AF.Copy)
+
+        ts(rf("o0", 128, 256), rf("p0", 128, 256), 9.5, 32.0, AL.is_ge, AL.mult)
+        ahead[0] = PAR["upper"]
+        choose(t, 1, answers)
+        ahead[0] = 0.0
+        own_rows(0, True, made)
+        ts(rf("o0", 0, 128), rf("p0", 0, 128), 9.5, 32.0, AL.is_ge, AL.mult)
+        if last:
+            sums(t, 1)
+            choose(t, 0, answers)
+            sums(t, 0)
+        else:
+            near(t, 1)
+            choose(t, 0, answers)
+            rewrite(1)
+            near(t, 0)
+            rewrite(0)
     return ops
 
 
 def plan(ops):
-    n = len(ops)
-    index = {}
     seen = {}
     for i, o in enumerate(ops):
         dep, soft = set(), set()
@@ -567,7 +590,6 @@ def plan(ops):
                 lst[:] = [e for e in lst if not (r[1] <= e[1][1] and e[1][2] <= r[2])]
             lst.append((i, r, isw))
         o["dep"], o["soft"] = dep, soft
-    return n
 
 
 def order(ops):
@@ -628,13 +650,6 @@ def order(ops):
 def emit(g, T, topo, core, ops, seq):
     queue = {"dve": g.vector, "act": g.scalar, "pe": g.tensor, "pool": g, "sync": g.sync}
     num, key = {}, {}
-    ends = {}
-    for i in seq:
-        if ops[i].get("auto") is not None:
-            ends.setdefault(ops[i]["auto"], []).append(i)
-    for members in ends.values():
-        ops[members[0]]["fl"]["start"] = True
-        ops[members[-1]]["fl"]["stop"] = True
     ndma = 0
     for i in seq:
         o = ops[i]

@@ -3,54 +3,62 @@ from concourse.mybir import AluOpType, ActivationFunctionType
 V, RO, NR = 3328, 3, 6
 CEN = 1664
 BIG = 8192.0
+LOW = -1681.0
+TOZ = CEN + 1 - 16 * LOW
 MAGIC = 50331648.0
 HALF = 12582912.0
 HOPS = ((1, 2), (3, 4), (5, 1))
 
 PAR = {
-    "yo": ((0, 2), (1, 2), (1, 2)),
-    "yg": (((2, 2), (2, 2)), ((1, 2), (2, 2)), ((1, 2), (2, 2))),
-    "yu": (((2, 2), (1, 1)), ((3, 2), (1, 1)), ((2, 2), (1, 2))),
-    "late": ((5, 0), (4, 0), (4, 0)),
-    "sg": (2, 1),
-    "mins": ((1, 3), (1, 2)),
+    "own": (("VvVv", "vssv"), ("vVuV", "vssv"), ("VvvV", "vssv")),
+    "guest": ((("uvss", "ssvu"), ("ssvu", "suss")), (("svsu", "ssvu"), ("suvs", "svss")), (("svus", "ssvu"), ("ssvu", "sssv"))),
+    "sg": ((2, 1), (0, 1)),
+    "size": ("ammm", "amma"),
+    "sum": ("vvve", "vvvv"),
+    "tree3": (0, 1), "evac": (1, 0),
+    "split": (1, 1),
     "nch": 6,
-    "indb": 3,
-    "tree": 2,
-    "xzv": (1, 1),
-    "first": 2.0, "upper": 1.0, "bonus": (3.0, 6.0), "seed": 2325, "jit": 0.0, "look": 0.03,
+    "xafter": 3,
+    "tree": 3,
+    "xzv": ((1, 1), (1, 1), (1, 1)),
+    "oact": (0, 0), "ract": ((0, 0), (0, 0)),
+    "first": 1.33, "upper": 1.07, "bonus": (1.04, 4.32), "rounds": 1, "look": 0.0, "greedy": 0,
+    "lower": 0.0, "ownp": (0.0, 0.0), "latep": (0.0, 0.0), "xnp": (0.0, 0.0), "nearp": (0.0, 0.0), "expp": 0.0, "keep": 0.0,
 }
-COST = {"cy": 1.08e-3, "ga": 1.75, "sc": 4.5, "pc": 0.53e-3, "dve": 0.0, "act": 0.0, "pe": 0.0, "hop": 0.2, "same": 0.18, "dma": 2.0,
-        "rem": 2.8, "first": 2.0, "issue": 0.6}
+COST = {"cy": 1.0e-3, "ga": 1.656, "sc": 4.0, "pc": 0.5e-3, "hop": 0.218, "same": 0.239, "dma": 2.0,
+        "rem": 2.841, "first": 2.0, "issue": 0.6}
+PAR.update({"own": [["vpVV", "ssvv"], ["pVVv", "vsvs"], ["VvVv", "sspv"]], "guest": [[["ppsv", "psvp"], ["vvps", "spsp"]], [["ppsv", "psvp"], ["ppvv", "spsp"]], [["psvp", "spvp"], ["svpv", "sppp"]]], "sg": [[2, 0], [1, 2]], "size": ["mamm", "ammm"], "sum": ["epep", "vevv"], "tree3": [0, 1], "evac": [1, 1], "split": [2, 1], "nch": 6, "xafter": 3, "tree": 2, "xzv": [[1, 1], [1, 1], [0, 1]], "oact": [0, 0], "ract": [[0, 0], [0, 0]], "first": 1.485, "upper": -1.33, "bonus": [0, 7.708], "rounds": 2, "look": 0, "greedy": 0, "lower": -0.236, "ownp": [-0.762, 4.275], "latep": [-6, -1.735], "xnp": [-5.724, -3.975], "nearp": [-1.057, 0.769], "expp": -6.421, "keep": 0})
+COST.update({"cy": 0.001, "ga": 1.7, "sc": 4.0, "pc": 0.0005, "hop": 0.218, "same": 0.138, "dma": 2.0, "rem": 2.628, "first": 2.0, "issue": 0.6})
 
 SCRATCH = {
     "ri": ("sbuf", [128, V], "int32"),
-    "rw": ("sbuf", [128, V + 32], "float32"),
+    "rw": ("sbuf", [128, V + 128], "float32"),
     "xs": ("sbuf", [128, V + 32], "bfloat16"),
     "xu": ("sbuf", [128, V], "bfloat16"),
     "wi": ("sbuf", [128, 16], "int32"),
     "d0": ("sbuf", [128, 4096], "float16"),
     "d1": ("sbuf", [128, 4096], "float16"),
     "d2": ("sbuf", [128, 4096], "float16"),
-    "mn": ("sbuf", [128, 1024], "bfloat16"),
+    "mn": ("sbuf", [128, 2048], "bfloat16"),
     "nb": ("sbuf", [128, 4096], "bfloat16"),
     "xn": ("sbuf", [128, 4096], "bfloat16"),
     "gg": ("sbuf", [128, 4096], "float32"),
+    "gh": ("sbuf", [128, 2048], "float16"),
     "ab0": ("sbuf", [128, 2, 2048], "float32"),
     "ab1": ("sbuf", [128, 2, 2048], "float32"),
-    "acc": ("sbuf", [128, 1024], "float32"),
+    "acc": ("sbuf", [128, 256], "float32"),
     "c16": ("sbuf", [128, 512], "float16"),
     "w1": ("sbuf", [128, 512], "float16"),
     "w2": ("sbuf", [128, 512], "float16"),
     "t2": ("sbuf", [128, 256], "float16"),
     "ol": ("sbuf", [128, 256], "uint16"),
-    "tp": ("sbuf", [128, 256], "bfloat16"),
+    "tp": ("sbuf", [128, 256], "float16"),
     "n32": ("sbuf", [128, 256], "float32"),
     "ee": ("sbuf", [128, 256], "float32"),
     "qe": ("sbuf", [128, 256], "float32"),
-    "zr": ("sbuf", [128, 512], "float32"),
-    "eq": ("sbuf", [128, 512], "float16"),
-    "o0": ("sbuf", [128, 256], "float16"),
+    "eq": ("sbuf", [128, 1024], "float16"),
+    "run": ("sbuf", [128, 1024], "float16"),
+    "o0": ("sbuf", [128, 256], "bfloat16"),
     "ok": ("sbuf", [128, 256], "float16"),
     "np_": ("sbuf", [128, 256], "float16"),
     "sn": ("sbuf", [128, 256], "float16"),
@@ -58,26 +66,22 @@ SCRATCH = {
     "wl": ("sbuf", [128, 16], "uint16"),
     "w16": ("sbuf", [128, 16], "float16"),
     "t16": ("sbuf", [128, 16], "float16"),
-    "z16": ("sbuf", [128, 16], "float16"),
-    "nh": ("sbuf", [128, 16], "float16"),
+    "fb": ("sbuf", [128, 16], "float16"),
     "qq": ("sbuf", [128, 16], "float32"),
     "hh": ("sbuf", [128, 16], "float32"),
-    "so": ("sbuf", [128, 32], "uint16"),
+    "so": ("sbuf", [128, 16], "uint16"),
     "ka": ("sbuf", [128, 256], "float32"),
     "kq": ("sbuf", [128, 384], "int32"),
-    "kr": ("sbuf", [128, 128], "float32"),
+    "kr": ("sbuf", [128, 256], "float32"),
     "kp": ("sbuf", [128, 16], "int32"),
     "kp2": ("sbuf", [128, 16], "int32"),
     "kf": ("sbuf", [128, 16], "float32"),
-    "kl": ("sbuf", [128, 16], "int32"),
-    "cl": ("sbuf", [128, 16], "uint16"),
     "jj": ("sbuf", [128, 256], "float16"),
     "j0": ("sbuf", [128, 256], "float16"),
     "j1": ("sbuf", [128, 256], "float16"),
     "bb": ("sbuf", [128, 256], "float16"),
-    "bs": ("sbuf", [128, 256], "float16"),
     "bf": ("sbuf", [128, 8], "bfloat16"),
-    "thr": ("sbuf", [128, 256], "float16"),
+    "thr": ("sbuf", [128, 512], "float16"),
     "ni": ("sbuf", [128, 128], "float16"),
     "i32": ("sbuf", [128, 128], "float32"),
     "ib": ("sbuf", [128, 128], "bfloat16"),
@@ -85,15 +89,16 @@ SCRATCH = {
     "nib": ("sbuf", [128, 128], "bfloat16"),
     "bo": ("sbuf", [128, 128], "float16"),
     "uu": ("sbuf", [128, 384], "float16"),
-    "tri": ("sbuf", [128, 256], "float16"),
-    "dum": ("sbuf", [128, 8], "float32"),
+    "tri": ("sbuf", [128, 512], "float16"),
+    "cut": ("sbuf", [128, 512], "float16"),
+    "dum": ("sbuf", [128, 4], "float32"),
 }
 for _t in range(RO):
     for _b in range(2):
         SCRATCH["qs%d%d" % (_t, _b)] = ("sbuf", [128, 272], "uint16")
         SCRATCH["ql%d%d" % (_t, _b)] = ("sbuf", [128, 272], "uint16")
-        SCRATCH["rs%d%d" % (_t, _b)] = ("sbuf", [128, 256], "float16")
-        SCRATCH["rl%d%d" % (_t, _b)] = ("sbuf", [128, 256], "float16")
+        SCRATCH["rs%d%d" % (_t, _b)] = ("sbuf", [128, 256], "bfloat16")
+        SCRATCH["rl%d%d" % (_t, _b)] = ("sbuf", [128, 256], "bfloat16")
 for _b in range(2):
     SCRATCH["vs%d" % _b] = ("sbuf", [128, 16], "uint16")
     SCRATCH["vl%d" % _b] = ("sbuf", [128, 16], "uint16")
@@ -134,10 +139,17 @@ def in_psum(r):
     return SCRATCH[r[0]][0] == "psum"
 
 
+def price(ops, C):
+    for o in ops:
+        c = o["cost"]
+        o["dur"] = (c.get("fix", 0.0) + C["cy"] * (c.get("cy", 0) + C["ga"] * c.get("ga", 0) + C["sc"] * c.get("sc", 0))
+                    + C["pc"] * c.get("pc", 0) + C["issue"] * c.get("issue", 0))
+        o["lat"] = c.get("lat", 0.0) + C["dma"] * c.get("dma", 0) + C["rem"] * c.get("rem", 0) + C["first"] * c.get("first", 0)
+
+
 def build(g, core, T, topo, rank):
     ops = []
     ahead = [0.0]
-    C = COST
 
     def ap(r):
         if len(r) == 2:
@@ -154,36 +166,39 @@ def build(g, core, T, topo, rank):
                 out.extend(r if len(r) == 2 else [r])
         return out
 
-    def add(eng, fn, reads, writes, dur, lat=0.0, kind="c", arrive=None, after=None):
-        ops.append({"eng": eng, "fn": fn, "r": flat(reads), "w": flat(writes), "dur": dur + C.get(eng, 0.0), "lat": lat, "kind": kind,
+    def add(eng, fn, reads, writes, cost, kind="c", arrive=None, after=None):
+        ops.append({"eng": eng, "fn": fn, "r": flat(reads), "w": flat(writes), "cost": cost, "kind": kind,
                     "arrive": arrive, "after": after, "bonus": ahead[0]})
         return len(ops) - 1
 
     def sc(x):
         return ap(x) if isinstance(x, tuple) else x
 
-    def vdur(out, ins, both=False):
+    def vcost(out, ins, both=False):
         if len(ins[0]) == 2:
-            return 0.05 + cnt(out) * C["ga"] * C["cy"]
+            return {"fix": 0.05, "ga": cnt(out)}
         n = cnt(out) * (2.0 if both else 1.0)
         if not both and two_bytes(out) and all(two_bytes(i) for i in ins):
             n *= 0.5
-        return max(n, 64) * C["cy"]
+        return {"cy": max(n, 64)}
 
     def ts(out, in0, s1, s2, op0, op1=None, **kw):
         def fn():
             if op1 is None:
                 return g.vector.tensor_scalar(ap(out), ap(in0), sc(s1), None, op0)
             return g.vector.tensor_scalar(ap(out), ap(in0), sc(s1), sc(s2), op0, op1)
-        return add("dve", fn, [in0, s1, s2], [out], vdur(out, [in0]), **kw)
+        return add("dve", fn, [in0, s1, s2], [out], vcost(out, [in0]), **kw)
 
     def tt(out, in0, in1, op, **kw):
         both = len(in0) == 4 and not in_psum(in0) and not in_psum(in1)
         return add("dve", lambda: g.vector.tensor_tensor(ap(out), ap(in0), ap(in1), op), [in0, in1], [out],
-                   vdur(out, [in0, in1], both), **kw)
+                   vcost(out, [in0, in1], both), **kw)
 
     def cp(out, in0, **kw):
-        return add("dve", lambda: g.vector.tensor_copy(ap(out), ap(in0)), [in0], [out], vdur(out, [in0]), **kw)
+        return add("dve", lambda: g.vector.tensor_copy(ap(out), ap(in0)), [in0], [out], vcost(out, [in0]), **kw)
+
+    def fill(out, value):
+        return add("dve", lambda: g.vector.memset(ap(out), value), [], [out], vcost(out, [out]))
 
     def act(out, in0, func, bias=None, scale=None, **kw):
         def fn():
@@ -193,12 +208,12 @@ def build(g, core, T, topo, rank):
             if scale is not None:
                 k["scale"] = scale
             return g.scalar.activation(ap(out), ap(in0), func, **k)
-        d = 0.065 + cnt(out) * C["ga"] * C["cy"] if len(in0) == 2 else max(cnt(out), 64) * C["cy"] + 0.03
-        return add("act", fn, [in0], [out], d, **kw)
+        c = {"fix": 0.065, "ga": cnt(out)} if len(in0) == 2 else {"fix": 0.03, "cy": max(cnt(out), 64)}
+        return add("act", fn, [in0], [out], c, **kw)
 
     def mm(out, lhs, rhs, start, stop, fam=None, **kw):
-        d = max(64, cnt(rhs)) * C["pc"] * (4 if SCRATCH[rhs[0]][2] == "float32" else 1)
-        i = add("pe", lambda: g.tensor.matmul(ap(out), ap(lhs), ap(rhs), start, stop), [lhs, rhs], [out], d, lat=0.05, **kw)
+        c = {"pc": max(64, cnt(rhs)) * (4 if SCRATCH[rhs[0]][2] == "float32" else 1), "lat": 0.05}
+        i = add("pe", lambda: g.tensor.matmul(ap(out), ap(lhs), ap(rhs), start, stop), [lhs, rhs], [out], c, **kw)
         ops[i]["fam"] = fam
         return i
 
@@ -212,14 +227,16 @@ def build(g, core, T, topo, rank):
             if SCRATCH[out[0]][2] == "int32":
                 return g.iota(ap(out), pattern, base, cm)
             return g.iota(ap(out), pattern, base, cm, allow_small_or_imprecise_dtypes=True)
-        return add("pool", fn, [], [out], 0.13 + 2 * cnt(out) * C["cy"])
+        return add("pool", fn, [], [out], {"fix": 0.13, "cy": 2 * cnt(out)})
 
-    def asel(buf, pattern, op, fill, base, cm, **kw):
-        return add("pool", lambda: g.affine_select(ap(buf), ap(buf), pattern, op, fill, base, cm), [buf], [buf],
-                   0.17 + 2 * cnt(buf) * C["cy"], **kw)
+    def asel(buf, pattern, op, value, base, cm, **kw):
+        return add("pool", lambda: g.affine_select(ap(buf), ap(buf), pattern, op, value, base, cm), [buf], [buf],
+                   {"fix": 0.17, "cy": 2 * cnt(buf)}, **kw)
 
     def dma(eng, fn, reads, writes, nbytes, **kw):
-        return add(eng, fn, reads, writes, 0.1 if eng != "pool" else C["issue"], lat=C["dma"] + nbytes / 600e3, kind="dma", **kw)
+        c = {"dma": 1, "lat": nbytes / 600e3}
+        c.update({"issue": 1} if eng == "pool" else {"fix": 0.1})
+        return add(eng, fn, reads, writes, c, kind="dma", **kw)
 
     def send(src, dst_name, sem, to_rank, first=False):
         to = T.cores[to_rank]
@@ -227,7 +244,7 @@ def build(g, core, T, topo, rank):
 
         def fn():
             return g.remote_dma(T[dst_name][:, src[1]:src[2]], ap(src), T.sem[sem], T.sem.sent, pid, rid, topo.mask(core, to))
-        i = add("pool", fn, [src], [], C["issue"], lat=C["rem"] + (C["first"] if first else 0.0), kind="rem")
+        i = add("pool", fn, [src], [], {"issue": 1, "rem": 1, "first": 1 if first else 0}, kind="rem")
         ops[i]["width"] = len(topo.engines(core, to))
         return i
 
@@ -238,17 +255,23 @@ def build(g, core, T, topo, rank):
     RW = rf("rw", 0, V)
     I16 = rf("jj", 0, 128)
 
+    ahead[0] = 9.0
     dma("sync", lambda: g.sync.dma_start(T.wi[:], T.w0[:]), [], [rf("wi")], 8192)
+    ahead[0] = 0.0
     nch = PAR["nch"]
     step = V // nch
-    for i in range(nch):
-        a, b = i * step, (V if i == nch - 1 else (i + 1) * step)
+    pieces = [(i * step, V if i == nch - 1 else (i + 1) * step) for i in range(nch)]
+    for i, (a, b) in enumerate(pieces):
         q = g.scalar if i % 2 == 0 else g.sync
+        ahead[0] = 8.0 - i
         dma("act" if i % 2 == 0 else "sync", (lambda q=q, a=a, b=b: q.dma_start(T.ri[:, a:b], T.rec[:, a:b])), [],
             [rf("ri", a, b)], 128 * 4 * b)
-    dma("sync", lambda: g.sync.dma_start(T.xs[:, 15:15 + V], T.x[:]), [], [rf("xs", 15, 15 + V)], 128 * 6 * V)
-    dma("sync", lambda: g.sync.dma_start(T.xs[:, 15 + V:17 + V], T.x[:, 0:2]), [], [rf("xs", 15 + V, 17 + V)], 128 * 6 * V)
-    dma("sync", lambda: g.sync.dma_start(T.xu[:], T.x[:]), [], [rf("xu")], 128 * 8 * V)
+    ahead[0] = 0.0
+    gate = [rf("ri", *pieces[PAR["xafter"]])]
+    late = 128 * 4 * (V - pieces[PAR["xafter"]][1])
+    dma("sync", lambda: g.sync.dma_start(T.xs[:, 15:15 + V], T.x[:]), gate, [rf("xs", 15, 15 + V)], late + 128 * 2 * V)
+    dma("sync", lambda: g.sync.dma_start(T.xs[:, 15 + V:17 + V], T.x[:, 0:2]), gate, [rf("xs", 15 + V, 17 + V)], late + 128 * 2 * V)
+    dma("sync", lambda: g.sync.dma_start(T.xu[:], T.x[:]), [rf("xs", 15, 15 + V)], [rf("xu")], 128 * 2 * V)
     XS = rf("xs", 16, 16 + V)
 
     iota(rf("kp", 0, 4), [[0, 4]], 0, 1)
@@ -265,27 +288,28 @@ def build(g, core, T, topo, rank):
     ts(rf("j1"), rf("jj"), rf("kf", 9, 10), None, AL.mult)
     ts(rf("bb"), rf("ka"), PR, 0.0, AL.add, AL.is_equal)
     ts(rf("ni"), I16, -1.0, None, AL.mult)
-    cp(rf("i32"), I16)
+    act(rf("i32"), rf("ka", 0, 128), AF.Abs)
+    act(rf("i32"), rf("i32"), AF.Relu, bias=1.0, scale=-1.0)
     act(rf("nib"), rf("i32"), AF.Identity, scale=-1.0)
     act(rf("ib"), rf("i32"), AF.Identity)
     act(rf("ib2"), rf("i32"), AF.Identity, scale=2.0)
-    ts(rf("bs"), rf("bb"), BIG, None, AL.mult)
-    add("dve", lambda: g.vector.memset(T.rw[:, V:V + 32], 0.0), [], [rf("rw", V, V + 32)], 0.07)
-    add("dve", lambda: g.vector.memset(T.bo[:], 1.0), [], [rf("bo")], 0.07)
-    add("dve", lambda: g.vector.memset(T.thr[:], 7.5), [], [rf("thr")], 0.14)
-    add("dve", lambda: g.vector.memset(T.qq[:], 0.0), [], [rf("qq")], 0.07)
+    fill(rf("rw", V, V + 128), 0.0)
+    fill(rf("bo"), 1.0)
+    fill(rf("thr"), 7.5)
+    fill(rf("cut"), 1.0)
+    fill(rf("cut", 0, 512, 64), 0.0)
     cp(rf("bf"), rf("bb", 0, 128, 16))
     iota(rf("kq"), [[-1, 3], [0, 8], [1, 16]], 15, 0)
-    iota(rf("kr"), [[0, 8], [1, 16]], 0, 0)
-    iota(rf("kl"), [[-1, 2], [1, 8]], 0, 0)
+    iota(rf("kr"), [[-16, 4], [1, 64]], 0, 0)
     ts(rf("kq"), rf("kq"), 15, None, AL.bitwise_and)
     for t in range(RO):
         ts(rf("uu", 128 * t, 128 * t + 128), rf("kq", 128 * t, 128 * t + 128), rf("kf", 4 + t, 5 + t), None, AL.is_gt)
-    ts(rf("tri", 0, 128), rf("kr"), PR, BIG, AL.is_le, AL.mult)
-    add("dve", lambda: g.vector.memset(T.tri[:, 128:256], BIG), [], [rf("tri", 128, 256)], 0.07)
-    cp(rf("cl"), rf("kl"))
-    iota(rf("dum"), [[0, 4], [16, 2]], int(V - CEN - 1 - BIG), 0)
-    ts(rf("dum"), rf("dum"), PR, None, AL.add)
+    ts(rf("tri", 0, 256), rf("kr"), PR, 14080.0, AL.is_ge, AL.mult)
+    ts(rf("tri", 0, 256), rf("tri", 0, 256), TOZ + LOW, None, AL.add)
+    fill(rf("tri", 63, 256, 64), float(CEN + 1))
+    cp(rf("tri", 256, 512), rf("tri", 0, 256))
+    iota(rf("dum"), [[32, 4]], V, 0)
+    ts(rf("dum"), rf("dum"), PR, PR, AL.add, AL.add)
 
     cp(rf("wl"), rf("wi"))
     ts(rf("w16"), rf("wi"), float(CEN), None, AL.subtract)
@@ -294,19 +318,19 @@ def build(g, core, T, topo, rank):
         group(rf("p%d" % (b + 1), 256, 272), [(jsl("jj", 16 * (1 + b)), rf("w16"))])
         ts(rf("vs%d" % b), rf("p%d" % (b + 1), 256, 272), float(CEN), None, AL.add)
         wsend.append(send(rf("vs%d" % b), "vl%d" % b, "av%d" % b, (rank + HOPS[0][b]) % NR, first=True))
-    for i in range(nch):
-        a, b = i * step, (V if i == nch - 1 else (i + 1) * step)
+    for a, b in pieces:
         ts(rf("rw", a, b), rf("ri", a, b), float(CEN), None, AL.subtract)
 
-    ring = {"p": 0, "g": 0}
+    ring = {"p": 0, "g": 0, "h": 0}
 
-    def bank(banks):
+    def bank():
+        kinds = "".join(y for x in list(PAR["guest"][ring["t"]]) + [PAR["own"][ring["t"]]] for y in x)
+        banks = (4, 5, 6) if "u" in kinds.lower() else (4, 5, 6, 7)
         ring["p"] += 1
         return "p%d" % banks[ring["p"] % len(banks)]
 
-    def twice(buf):
-        cp(rf(buf, 0, 128), rf(buf, 128, 256))
-        cp(rf(buf, 384, 512), rf(buf, 256, 384))
+    def twice(buf, h):
+        cp(rf(buf, 384 * h, 384 * h + 128), rf(buf, 128 + 128 * h, 256 + 128 * h))
 
     def count_rows(dbuf, h, k, cbank, c0, shift, fam):
         x = (16 * shift) % 128
@@ -314,33 +338,34 @@ def build(g, core, T, topo, rank):
         mm(rf(cbank, c0 + k, c0 + 128, 16), rf(dbuf, a, a + 128),
            rf("bf") if dbuf == "nb" else rf("bb", x, x + 128, 16), True, True, fam=fam)
 
-    def likeness(dbuf, h, lists, wref, ns, nu, wps, arrive, cbank, shift, fam, part=(0, 8), cut=8, after=None):
+    def likeness(dbuf, h, lists, wbuf, kinds, wps, arrive, cbank, shift, fam, after=None):
         kw = {"arrive": arrive, "after": after}
-        units = []
-        nn = ns + nu
-        kinds = sorted([((i + 0.5) / ns, "s") for i in range(ns)] + [((i + 0.6) / nu, "u") for i in range(nu)])
-        for i in range(nn):
-            units.append(((i + 1.0) / nn, kinds[i][1], 2 * i, 2 * i + 2))
-        k, nd = 2 * nn, 8 - 2 * nn
-        while k < 8:
-            e = min(cut if k < cut else 8, k + PAR["indb"])
-            units.append(((e - 2.0 * nn) / nd - 1e-3, "v", k, e))
-            k = e
-        units.sort()
+        wref, wone = rf(wbuf, 256 * h, 256 * h + 256), rf(wbuf, 128 + 128 * h, 256 + 128 * h)
         d0, l0 = 2048 * h, 128 * h
-        for _, how, k0, k1 in units:
-            if k0 < part[0] or k0 >= part[1]:
+        for unit, how in enumerate(kinds):
+            if how not in "psuv":
                 continue
+            k0, k1 = 2 * unit, 2 * unit + 2
             dd = rf(dbuf, d0 + 256 * k0, d0 + 256 * k1)
             if how != "v":
                 c0 = 512 * (ring["g"] % 8)
                 ring["g"] += 1
-                act(rf("gg", c0, c0 + 512), (RW, rf(lists, l0 + 16 * k0, l0 + 16 * k1)), AF.Copy, **kw)
-            if how == "s":
-                pb = bank((4, 5, 6))
-                for i in range(2):
-                    group(rf(pb, 256 * i, 256 * i + 256),
-                          [(rf("ni"), wref), (rf("i32"), rf("gg", c0 + 256 * i, c0 + 256 * i + 256))])
+                act(rf("gg", c0, c0 + 512), (RW, rf(lists, l0 + 16 * k0, l0 + 16 * k1)), AF.Copy, arrive=arrive)
+            if how == "p":
+                pb, e0 = bank(), 512 * (ring["h"] % 4)
+                ring["h"] += 1
+                src, dst = rf("gg", c0, c0 + 512), rf("gh", e0, e0 + 512)
+                add("pool", (lambda src=src, dst=dst: g.affine_select(ap(dst), ap(src), [[0, 512]], AL.is_ge, 0.0, 0, 0)),
+                    [src], [dst], {"fix": 0.17, "cy": 1024})
+                for i in range(4):
+                    group(rf(pb, 128 * i, 128 * i + 128),
+                          [(rf("ni"), wone), (I16, rf("gh", e0 + 128 * i, e0 + 128 * i + 128))])
+                ts(dd, rf(pb), MAGIC, MAGIC, AL.add, AL.is_equal)
+            elif how == "s":
+                pb = bank()
+                for i in range(4):
+                    group(rf(pb, 128 * i, 128 * i + 128),
+                          [(rf("ni"), wone), (rf("i32"), rf("gg", c0 + 128 * i, c0 + 128 * i + 128))])
                 ts(dd, rf(pb), MAGIC, MAGIC, AL.add, AL.is_equal)
             else:
                 for k in range(k0, k1):
@@ -352,6 +377,11 @@ def build(g, core, T, topo, rank):
                 ts(dd, dd, MAGIC, MAGIC, AL.add, AL.is_equal)
             for k in range(2 * k0, 2 * k1):
                 count_rows(dbuf, h, k, cbank, 128 * h, shift, fam)
+
+    def enough(out, counts, by_scalar):
+        if by_scalar:
+            return act(out, counts, AF.Sign, bias=-9.5)
+        return ts(out, counts, 9.5, None, AL.is_ge)
 
     def halve(s, levels, after):
         buf = "ab%d" % (s % 2)
@@ -366,37 +396,42 @@ def build(g, core, T, topo, rank):
     def choose(t, h, answers):
         a, b, m0, m1 = 128 * h, 128 * h + 128, 8 * h, 8 * h + 8
         pb = "p1" if h else "p2"
-        group(rf(pb, 0, 128), [(rf("o0", a, b), I16)]
-              + [(rf("rl%d%d" % (t, i), a, b), I16, {"arrive": ("ar%d%d%d" % (t, i, h), answers[(i, h)])}) for i in range(2)])
-        ts(rf("ok", a, b), rf(pb, 0, 128), 95.5, -BIG, AL.is_ge, AL.mult)
-        group(rf(pb, 128, 256), [(rf("uu", 128 * t, 128 * t + 128), rf("ok", a, b)), (I16, rf("c16", 128 + a, 128 + b)),
-                                 (rf("nib"), rf("tp", a, b))])
-        ts(rf("sn", a, b), rf(pb, 128, 256), BIG - 1666.0, BIG, AL.max, AL.subtract)
-        zs = rf("p3", 256 + m0, 256 + m1)
-        group(zs, [(jsl("bb", r), rf("sn", a + r, b, 16)) for r in range(16)])
-        ts(rf("nh", m0, m1), zs, -16 * 1666.0 + 0.5, -BIG, AL.is_gt, AL.mult)
-        ts(rf("qq", m0, m1), zs, 15 * 1666.0, None, AL.add)
-        tt(rf("hh", m0, m1), rf("nh", m0, m1), rf("t16", m0, m1), AL.add)
-        tt(rf("z16", m0, m1), rf("hh", m0, m1), rf("qq", m0, m1), AL.max)
-        ts(rf("wl", m0, m1), rf("z16", m0, m1), float(CEN + 1), None, AL.add)
-        if PAR["xzv"][h]:
-            xz = cp(rf("xz", a, b), (rf("xu"), rf("wl", m0, m1)))
+        group(rf(pb, 0, 128), [(rf("o0", a, b), rf("ib"))]
+              + [(rf("rl%d%d" % (t, i), a, b), rf("ib"), {"arrive": ("ar%d%d%d" % (t, i, h), answers[(i, h)])}) for i in range(2)])
+        ts(rf("ok", a, b), rf(pb, 0, 128), 2.5, -BIG, AL.is_ge, AL.mult)
+        group(rf(pb, 128, 256), [(I16, rf("c16", 128 + a, 128 + b)), (rf("ni"), rf("tp", a, b)),
+                                 (rf("uu", 128 * t, 128 * t + 128), rf("ok", a, b))])
+        none = rf("p3", 256 + m0, 256 + m1)
+        group(none, [(I16, rf("w16", m0, m1)), (rf("ni"), rf("t16", m0, m1))]
+              + [(jsl("bb", r), rf("ok", a + r, b, 16)) for r in range(16)])
+        ts(rf("sn", a, b), rf(pb, 128, 256), BIG + LOW, BIG, AL.max, AL.subtract)
+        ts(rf("fb", m0, m1), none, LOW, None, AL.max)
+        zs = rf(pb, 256, 264)
+        group(zs, [(jsl("bb", r), rf("sn", a + r, b, 16)) for r in range(16)] + [(I16, rf("fb", m0, m1))])
+        ts(rf("wl", m0, m1), zs, TOZ, None, AL.add)
+        if PAR["xzv"][t][h]:
+            cp(rf("xz", a, b), (rf("xu"), rf("wl", m0, m1)))
         else:
-            xz = act(rf("xz", a, b), (rf("xu"), rf("wl", m0, m1)), AF.Copy)
+            act(rf("xz", a, b), (rf("xu"), rf("wl", m0, m1)), AF.Copy)
         if t == RO - 1:
             return
-        ts(rf("w16", m0, m1), rf("z16", m0, m1), 1.0, None, AL.add)
-        for j in range(2):
-            group(rf(pb, 256 + 128 * j, 384 + 128 * j), [(I16, rf("tri", 128 * j, 128 * j + 128)), (rf("bo"), rf("sn", a, b))])
-        act(rf("zr", 2 * a, 2 * b), rf(pb, 256, 512), AF.Identity, bias=15 * 1666.0, after=[xz])
+        ts(rf("qq", m0, m1), zs, TOZ, None, AL.add)
+        ts(rf("w16", m0, m1), zs, TOZ - CEN, None, AL.add)
+        mm(rf(pb), I16, rf("tri"), True, False)
+        for m in range(8):
+            c0 = a + 64 * (m // 4)
+            mm(rf(pb, 64 * m, 64 * m + 63), rf("bo"), rf("sn", c0, c0 + 63), False, False)
+        mm(rf(pb, 63, 512, 64), I16, rf("fb", m0, m1), False, True)
         tt(rf("ee", a, b), (RW, rf("wl", m0, m1)), rf("n32", a, b), AL.subtract)
-        tt(rf("eq", 2 * a, 2 * b), (rf("qq", m0, m1), rf("cl")), rf("zr", 2 * a, 2 * b), AL.is_equal)
-        tt(rf("eq", 2 * a, 2 * a + 128), rf("eq", 2 * a, 2 * a + 128), rf("eq", 2 * a + 128, 2 * b), AL.add)
-        ps = rf(pb, 0, 8)
-        group(ps, [(I16, rf("nh", m0, m1)), (I16, rf("z16", m0, m1))]
-              + [(jsl("bs", r), rf("eq", 2 * a + r, 2 * a + 128, 16)) for r in range(16)])
-        tt(rf("hh", m0, m1), ps, rf("dum", 0, 8), AL.min)
-        ts(rf("so", m0, m1), rf("hh", m0, m1), CEN + 1 + BIG, None, AL.add)
+        e0 = 512 * h
+        for m in range(8):
+            ts(rf("eq", e0 + 64 * m, e0 + 64 * m + 64), rf(pb, 64 * m, 64 * m + 64), rf("qq", m0 + m, m0 + m + 1),
+               rf("dum", m % 4, m % 4 + 1), AL.is_equal, AL.mult)
+        eq, run = rf("eq", e0, e0 + 512), rf("run", e0, e0 + 512)
+        add("dve", lambda: g.vector.tensor_tensor_scan(ap(run), ap(rf("cut")), ap(eq), 0.0, AL.mult, AL.max),
+            [rf("cut"), eq], [run], {"cy": 256})
+        tt(rf("hh", m0, m1), rf("run", e0 + 63, e0 + 512, 64), rf("qq", m0, m1), AL.max)
+        cp(rf("so", m0, m1), rf("hh", m0, m1))
 
     def differ(pb, h, i, lhs, close):
         mm(rf(pb), rf(lhs), rf("xn", 2048 * h + 512 * i, 2048 * h + 512 * i + 512), True, False)
@@ -404,9 +439,9 @@ def build(g, core, T, topo, rank):
             mm(rf(pb, 128 * j, 128 * j + 128), rf("nib"), rf("xz", 128 * h, 128 * h + 128), False, close and j == 3)
 
     def near(t, h):
-        sg, buf = PAR["sg"][h], "ab%d" % (t % 2)
+        sg, buf = PAR["sg"][t][h], "ab%d" % (t % 2)
         a, b = 128 * h, 128 * h + 128
-        for i in [3, 0, 2, 1]:
+        for i in [0, 3, 2, 1]:
             pb = "p%d" % (4 + i)
             c0 = 2048 * h + 512 * i
             differ(pb, h, i, "ib", True)
@@ -419,64 +454,106 @@ def build(g, core, T, topo, rank):
                 count_rows("nb" if i < sg else "d0", h, k, "p0", 256 + a, 0, "near%d%d" % (t, h))
         for i in range(3, sg - 1, -1):
             act(rf(buf, 2048 * h + 512 * i, 2048 * h + 512 * i + 512), rf("p%d" % (4 + i)), AF.Abs)
-        tt(rf("np_", a, b), rf("p0", 256 + a, 256 + b), rf("thr", a, b), AL.is_lt)
+        tt(rf("np_", a, b), rf("p0", 256 + a, 256 + b), rf("thr", 256 * t + a, 256 * t + b), AL.is_lt)
         pb = "p1" if h else "p2"
         group(rf(pb, 384, 512), [(rf("np_", a, b), I16)])
         tt(rf("qe", a, b), rf(pb, 384, 512), rf("ee", a, b), AL.mult)
+        keep, ahead[0] = ahead[0], PAR["expp"]
         for i in range(4):
             ab = rf(buf, 2048 * h + 512 * i, 2048 * h + 512 * i + 512)
             act(ab, ab, AF.Exp, scale=-1.0)
+        ahead[0] = keep
 
     def rewrite(h):
         win = rf("rw")
-        for m in range(8 * h + 6, 8 * h - 2, -2):
-            add("dve", (lambda m=m: g.vector.tensor_tensor(ap((win, rf("so", m, m + 2))), T.qe[:, 16 * m:16 * m + 32],
-                                                           T.n32[:, 16 * m:16 * m + 32], AL.add)),
-                [rf("so", m, m + 2), rf("qe", 16 * m, 16 * m + 32), rf("n32", 16 * m, 16 * m + 32)], [win],
-                0.05 + 32 * C["sc"] * C["cy"])
+        for m in (8 * h + 4, 8 * h):
+            add("dve", (lambda m=m: g.vector.tensor_tensor(ap((win, rf("so", m, m + 4))), T.qe[:, 16 * m:16 * m + 64],
+                                                           T.n32[:, 16 * m:16 * m + 64], AL.add)),
+                [rf("so", m, m + 4), rf("qe", 16 * m, 16 * m + 64), rf("n32", 16 * m, 16 * m + 64)], [win],
+                {"fix": 0.05, "sc": 64})
 
     def sums(t, h):
-        mins, buf, xb, s0 = PAR["mins"][h], "ab%d" % (t % 2), ("p1" if h else "p2"), 512 * h
-        if mins:
-            for j in range(4):
-                group(rf(xb, 128 * j, 128 * j + 128), [(rf("ib"), rf("xz", 128 * h, 128 * h + 128))])
+        size, ways, buf, xb = PAR["size"][h], PAR["sum"][h], "ab%d" % (t % 2), ("p1" if h else "p2")
+        a, b = 128 * h, 128 * h + 128
+        if "m" in size:
+            group(rf(xb, 0, 128), [(rf("ib"), rf("xz", a, b))])
+        total, acc = rf("p7" if h else "p0", 0, 128), rf("acc", a, b)
+        chain = [i for i in range(4) if ways[i] == "v"]
+        tree = PAR["tree3"][h] and len(chain) > 1
+        nblocks = 4 * ways.count("p") + (4 if chain and not tree else 0)
+        done = {"blocks": 0, "acc": False}
+
+        def fold(c0, c1):
+            for c in range(c0, c1, 128):
+                done["blocks"] += 1
+                mm(total, rf("i32"), rf(buf, c, c + 128), done["blocks"] == 1, done["blocks"] == nblocks)
+
+        def onto(piece):
+            if done["acc"]:
+                tt(acc, piece, acc, AL.add)
+            else:
+                cp(acc, piece)
+            done["acc"] = True
         for i in range(4):
-            pb = "p%d" % (4 + i)
+            pb = ("p4", "p5", "p6", "p4")[i] if h else ("p5", "p6", "p4", "p7")[i]
             c0 = 2048 * h + 512 * i
-            if i in mins:
+            w = 512 // PAR["split"][h] if i == 3 else 512
+            if size[i] == "m":
                 differ(pb, h, i, "nib", False)
-                mn = rf("mn", 512 * (i % 2), 512 * (i % 2) + 512)
-                tt(mn, rf("xn", c0, c0 + 512), rf(xb), AL.min)
-                mm(rf(pb), rf("ib2"), mn, False, True)
-                act(rf(pb), rf(pb), AF.Exp)
+                for j in range(4):
+                    tt(rf("mn", 512 * i + 128 * j, 512 * i + 128 * j + 128), rf("xn", c0 + 128 * j, c0 + 128 * j + 128),
+                       rf(xb, 0, 128), AL.min)
+                mm(rf(pb), rf("ib2"), rf("mn", 512 * i, 512 * i + 512), False, True)
             else:
                 differ(pb, h, i, "ib", True)
                 act(rf(buf, c0, c0 + 512), rf(pb), AF.Abs)
-                act(rf(pb), rf(buf, c0, c0 + 512), AF.Exp, scale=-1.0)
-            if i == 0:
-                cp(rf("acc", s0, s0 + 512), rf(pb))
-            elif i < 3:
-                tt(rf("acc", s0, s0 + 512), rf(pb), rf("acc", s0, s0 + 512), AL.add)
-            else:
-                for w in (256, 128):
-                    tt(rf("acc", s0, s0 + w), rf("acc", s0, s0 + w), rf("acc", s0 + w, s0 + 2 * w), AL.add)
-                for j in range(4):
-                    tt(rf("acc", s0, s0 + 128), rf(pb, 128 * j, 128 * j + 128), rf("acc", s0, s0 + 128), AL.add)
-        dma("sync", lambda: g.sync.dma_start(T.y[:, 256 * t + 128 * h:256 * t + 128 * h + 128], T.acc[:, s0:s0 + 128]),
-            [rf("acc", s0, s0 + 128)], [], 128 * 512)
+            stay = ways[i] == "e" or (ways[i] == "v" and i != chain[0])
+            for c in range(0, 512, w):
+                out = rf(pb, c, c + w) if stay else rf(buf, c0 + c, c0 + c + w)
+                if size[i] == "m":
+                    act(out, rf(pb, c, c + w), AF.Exp)
+                else:
+                    act(out, rf(buf, c0 + c, c0 + c + w), AF.Exp, scale=-1.0)
+                if ways[i] == "p":
+                    fold(c0 + c, c0 + c + w)
+            if ways[i] == "e":
+                for c in range(0, 512, 128):
+                    onto(rf(pb, c, c + 128))
+            if ways[i] == "v":
+                f0 = 2048 * h + 512 * chain[0]
+                if tree and i == chain[-1]:
+                    tt(rf(buf, f0, f0 + 256), rf(pb, 0, 256), rf(buf, f0, f0 + 256), AL.add)
+                    tt(rf(pb, 256, 512), rf(pb, 256, 512), rf(buf, f0 + 256, f0 + 512), AL.add)
+                    tt(rf(buf, f0, f0 + 128), rf(pb, 256, 384), rf(buf, f0, f0 + 128), AL.add)
+                    tt(rf(pb, 384, 512), rf(pb, 384, 512), rf(buf, f0 + 128, f0 + 256), AL.add)
+                    if done["acc"]:
+                        onto(rf(pb, 384, 512))
+                        tt(acc, rf(buf, f0, f0 + 128), acc, AL.add)
+                    else:
+                        tt(acc, rf(pb, 384, 512), rf(buf, f0, f0 + 128), AL.add)
+                        done["acc"] = True
+                elif i != chain[0]:
+                    tt(rf(buf, f0, f0 + 512), rf(pb), rf(buf, f0, f0 + 512), AL.add)
+                if i == chain[-1] and not tree:
+                    fold(f0, f0 + 512)
+        if nblocks and (done["acc"] or PAR["evac"][h]):
+            onto(total)
+        elif nblocks:
+            act(acc, total, AF.Copy)
+        dma("sync", lambda: g.sync.dma_start(T.y[:, 256 * t + a:256 * t + b], T.acc[:, a:b]), [acc], [], 128 * 512)
 
     for t in range(RO):
         last = t == RO - 1
+        ring["t"] = t
         CC = rf("c16", 128, 384)
         if t == 0:
             ts(CC, (rf("ri"), rf("wl")), float(CEN), None, AL.subtract)
         else:
             cp(CC, (RW, rf("wl")))
-        act(rf("tp"), (RW, rf("wl")), AF.Relu, bias=-float(V * (V - CEN - 2)), scale=float(V))
         for be in range(8):
             o = rf("t2", 128 * (be // 4) + be % 4, 128 * (be // 4) + 128, 4)
             i = rf("c16", 128 + 32 * be, 160 + 32 * be)
-            add("dve", (lambda o=o, i=i: g.vector.transpose(ap(o), ap(i))), [i], [o], 64 * C["cy"])
+            add("dve", (lambda o=o, i=i: g.vector.transpose(ap(o), ap(i))), [i], [o], {"cy": 64})
         sends = []
         for b, pb in ((0, "p1"), (1, "p2"), (2, "p3")):
             s = 0 if b == 2 else t + 1 + b
@@ -494,22 +571,25 @@ def build(g, core, T, topo, rank):
                                   (rank + HOPS[t][b]) % NR))
             else:
                 ts(rf("ol"), rf(pb, 0, 256), float(CEN), None, AL.add)
-        twice("c16")
+        for h in range(2):
+            if "v" in PAR["own"][t][h].lower():
+                twice("c16", h)
+        ts(rf("tp"), CC, V - CEN - 1.5, float(V), AL.is_gt, AL.mult)
         if t == 0:
             for buf, rep in ((rf("uu"), 3), (rf("bo"), 1)):
                 asel(buf, [[0, rep], [-16, 8], [0, 16]], AL.is_ge, 0.0, 0, 1, after=sends)
                 asel(buf, [[0, rep], [16, 8], [0, 16]], AL.is_ge, 0.0, 15, -1)
             asel(rf("uu"), [[0, 3], [-1, 128]], AL.not_equal, -1.0, 0, 1)
-            asel(rf("tri", 128, 256), [[0, 4], [1, 2], [0, 16]], AL.is_equal, 0.0, 0, 0, after=sends)
-            for h in range(2):
-                if PAR["sg"][h]:
-                    asel(rf("thr", 128 * h, 128 * h + 128), [[0, 8], [1, 16]], AL.is_ge, -0.5, -4 * PAR["sg"][h], 0, after=sends)
+            for s in range(RO - 1):
+                for h in range(2):
+                    if PAR["sg"][s][h]:
+                        asel(rf("thr", 256 * s + 128 * h, 256 * s + 128 * h + 128), [[0, 8], [1, 16]], AL.is_ge, -0.5,
+                             -4 * PAR["sg"][s][h], 0, after=sends)
         else:
             halve(t - 1, range(PAR["tree"]), sends)
-        ts(rf("t16"), rf("w16"), float(V - CEN - 1), -float(V), AL.is_equal, AL.mult)
-        tt(rf("t16"), rf("t16"), rf("w16"), AL.add)
+        ts(rf("t16"), rf("w16"), float(V - CEN - 1), float(V), AL.is_equal, AL.mult)
         if not last:
-            group(rf("p3", 0, 256), [(I16, CC), (rf("nib"), rf("tp"))])
+            group(rf("p3", 0, 256), [(I16, CC), (rf("ni"), rf("tp"))])
             act(rf("n32"), rf("p3", 0, 256), AF.Identity, bias=1.0)
 
         arr = [("aq%d%d" % (t, b), sends[b]) for b in range(2)]
@@ -519,61 +599,78 @@ def build(g, core, T, topo, rank):
                 cp(rf(wb, 128, 384), (RW, rf("vl%d" % b)), arrive=("av%d" % b, wsend[b]))
             else:
                 cp(rf(wb, 128, 384), (RW, rf("ql%d%d" % (t, b), 256, 272)), arrive=arr[b])
-            twice(wb)
+            for h in range(2):
+                if "v" in PAR["guest"][t][b][h]:
+                    twice(wb, h)
 
         def own_rows(h, late, after):
-            cut = 8 - PAR["late"][t][h]
-            likeness("d0", h, "ol", rf("c16", 256 * h, 256 * h + 256), PAR["yo"][t][h], 0, None, None, "p0", 0,
-                     "own%d" % t, (cut, 8) if late else (0, cut), cut, after)
+            kinds = PAR["own"][t][h].swapcase() if late else PAR["own"][t][h]
+            if "u" in kinds:
+                for i in range(2):
+                    group(rf("p7", 128 * i, 128 * i + 128), [(I16, rf("c16", 128 + 128 * h, 256 + 128 * h))])
+            likeness("d0", h, "ol", "c16", kinds, rf("p7", 0, 256), None, "p0", 0, "own%d" % t, after)
         for h in (1, 0):
+            ahead[0] = PAR["ownp"][h]
             own_rows(h, False, None)
         answers, made = {}, []
         for h in (1, 0):
             for b in range(2):
                 ahead[0] = PAR["bonus"][h] + (0.0 if b else PAR["first"])
-                wb, pb = rf("w%d" % (b + 1), 256 * h, 256 * h + 256), "p%d" % (b + 1)
-                nu, wps = PAR["yu"][t][b][h], rf("p7", 256 * b, 256 * b + 256)
-                if nu:
-                    group(wps, [(I16, wb)])
-                likeness("d%d" % (b + 1), h, "ql%d%d" % (t, b), wb, PAR["yg"][t][b][h], nu, wps, arr[b], pb, t + 1 + b,
-                         "g%d%d%d" % (t, b, h))
+                wb, pb = "w%d" % (b + 1), "p%d" % (b + 1)
+                kinds, wps = PAR["guest"][t][b][h], rf("p7", 256 * b, 256 * b + 256)
+                if "u" in kinds:
+                    for i in range(2):
+                        group(rf("p7", 256 * b + 128 * i, 256 * b + 128 * i + 128), [(I16, rf(wb, 128 + 128 * h, 256 + 128 * h))])
+                likeness("d%d" % (b + 1), h, "ql%d%d" % (t, b), wb, kinds, wps, arr[b], pb, t + 1 + b, "g%d%d%d" % (t, b, h))
                 rs = rf("rs%d%d" % (t, b), 128 * h, 128 * h + 128)
-                made.append(ts(rs, rf(pb, 128 * h, 128 * h + 128), 9.5, 32.0, AL.is_ge, AL.mult))
+                made.append(enough(rs, rf(pb, 128 * h, 128 * h + 128), PAR["ract"][b][h]))
                 answers[(b, h)] = send(rs, "rl%d%d" % (t, b), "ar%d%d%d" % (t, b, h), (rank - HOPS[t][b]) % NR)
         ahead[0] = 0.0
         if t > 0:
             halve(t - 1, range(PAR["tree"], 4), list(answers.values()))
+        ahead[0] = PAR["latep"][1]
         own_rows(1, True, made)
         for h in (1, 0):
+            ahead[0] = PAR["xnp"][h]
             for i in range(4):
                 c0 = 2048 * h + 512 * i
                 act(rf("xn", c0, c0 + 512), (XS, rf("ol", c0 // 16, c0 // 16 + 32)), AF.Copy)
 
-        ts(rf("o0", 128, 256), rf("p0", 128, 256), 9.5, 32.0, AL.is_ge, AL.mult)
         ahead[0] = PAR["upper"]
+        enough(rf("o0", 128, 256), rf("p0", 128, 256), PAR["oact"][1])
         choose(t, 1, answers)
-        ahead[0] = 0.0
+        ahead[0] = PAR["latep"][0]
         own_rows(0, True, made)
-        ts(rf("o0", 0, 128), rf("p0", 0, 128), 9.5, 32.0, AL.is_ge, AL.mult)
+        enough(rf("o0", 0, 128), rf("p0", 0, 128), PAR["oact"][0])
+        ahead[0] = PAR["nearp"][1]
         if last:
             sums(t, 1)
+            ahead[0] = PAR["lower"]
             choose(t, 0, answers)
+            ahead[0] = PAR["nearp"][0]
             sums(t, 0)
         else:
             near(t, 1)
+            ahead[0] = PAR["lower"]
             choose(t, 0, answers)
             rewrite(1)
+            ahead[0] = PAR["nearp"][0]
             near(t, 0)
             rewrite(0)
+        ahead[0] = 0.0
+    price(ops, COST)
     return ops
 
 
 def plan(ops):
-    seen = {}
+    seen, older = {}, {}
     for i, o in enumerate(ops):
         dep, soft = set(), set()
+        for r in o["r"] + o["w"]:
+            if in_psum(r) and seen.get(r[0]) and ops[seen[r[0]][-1][0]]["eng"] != o["eng"]:
+                older[r[0]], seen[r[0]] = seen[r[0]], []
         for r, isw in [(r, False) for r in o["r"]] + [(r, True) for r in o["w"]]:
-            for j, q, wasw in seen.get(r[0], ()):
+            for j, q, wasw in older.get(r[0], []) + seen.get(r[0], []):
                 if j == i:
                     continue
                 ej = ops[j]["eng"]
@@ -618,33 +715,68 @@ def order(ops):
         for s in succ[i]:
             best = max(best, pred[s][i] + prio[s])
         prio[i] = best
-    x = PAR["seed"]
-    for i in range(n):
-        x = (x * 1103515245 + 12345) % 2147483648
-        prio[i] += PAR["jit"] * x / 2147483648.0 + ops[i]["bonus"]
-    left = [len(p) for p in pred]
-    ready = {}
-    for i in range(n):
-        if left[i] == 0:
-            ready[i] = 0.0
-    free = {}
-    start = [0.0] * n
-    seq = []
-    while ready:
-        t0 = min(max(tm, free.get(ops[i]["eng"], 0.0)) for i, tm in ready.items())
-        cand = [i for i, tm in ready.items() if max(tm, free.get(ops[i]["eng"], 0.0)) <= t0 + 1e-9]
-        eng = ops[cand[0]]["eng"]
-        cand = [i for i, tm in ready.items() if ops[i]["eng"] == eng and tm <= t0 + 1e-9 + PAR["look"]]
-        i = max(cand, key=lambda c: (prio[c], -c))
-        start[i] = max(ready[i], free.get(eng, 0.0))
-        free[eng] = start[i] + ops[i]["dur"]
-        del ready[i]
-        seq.append(i)
-        for s in succ[i]:
-            left[s] -= 1
-            if left[s] == 0:
-                ready[s] = max(start[j] + d for j, d in pred[s].items())
-    return seq, start
+    dur = [o["dur"] for o in ops]
+    back = [{s: dur[s] + pred[s][i] - dur[i] for s in succ[i]} for i in range(n)]
+
+    def place(rank, before, release):
+        busy = {}
+        start = [0.0] * n
+        for i in rank:
+            t = max([release[i]] + [start[j] + d for j, d in before[i].items()])
+            line = busy.setdefault(ops[i]["eng"], [])
+            k = len(line)
+            while k > 0 and line[k - 1][1] > t:
+                k -= 1
+            while k < len(line) and line[k][0] < t + dur[i] - 1e-9:
+                t = max(t, line[k][1])
+                k += 1
+            line.insert(k, (t, t + dur[i]))
+            start[i] = t
+        return start
+
+    def ranked(key, before, after):
+        left = [len(p) for p in before]
+        free = sorted((key[i], i) for i in range(n) if not left[i])
+        out = []
+        while free:
+            i = free.pop(0)[1]
+            out.append(i)
+            for s in after[i]:
+                left[s] -= 1
+                if not left[s]:
+                    k = len(free)
+                    while k > 0 and free[k - 1] > (key[s], s):
+                        k -= 1
+                    free.insert(k, (key[s], s))
+        return out
+
+    def greedy(key):
+        left = [len(p) for p in pred]
+        ready = {i: 0.0 for i in range(n) if not left[i]}
+        free, start = {}, [0.0] * n
+        while ready:
+            t0, i0 = min((max(tm, free.get(ops[i]["eng"], 0.0)), i) for i, tm in ready.items())
+            eng = ops[i0]["eng"]
+            i = min((key[i], i) for i, tm in ready.items() if ops[i]["eng"] == eng and tm <= t0 + 1e-9 + PAR["look"])[1]
+            start[i] = max(ready.pop(i), free.get(eng, 0.0))
+            free[eng] = start[i] + dur[i]
+            for s in succ[i]:
+                left[s] -= 1
+                if not left[s]:
+                    ready[s] = max(start[j] + d for j, d in pred[s].items())
+        return start
+    zero, tail = [0.0] * n, [o["lat"] for o in ops]
+    start = greedy([-prio[i] - ops[i]["bonus"] for i in range(n)])
+    best = (max(start[i] + dur[i] + tail[i] for i in range(n)), start)
+    for _ in range(PAR["rounds"]):
+        rev = place(ranked([-start[i] - dur[i] for i in range(n)], back, pred), back, tail)
+        key = [-rev[i] - dur[i] - PAR["keep"] * ops[i]["bonus"] for i in range(n)]
+        start = greedy(key) if PAR["greedy"] else place(ranked(key, pred, succ), pred, zero)
+        end = max(start[i] + dur[i] + tail[i] for i in range(n))
+        if end < best[0]:
+            best = (end, start)
+    start = best[1]
+    return sorted(range(n), key=lambda i: (start[i], i)), start
 
 
 def emit(g, T, topo, core, ops, seq):

@@ -29,6 +29,21 @@ COST = {"cy": 1.0e-3, "ga": 1.656, "sc": 4.0, "pc": 0.5e-3, "hop": 0.218, "same"
         "rem": 2.841, "first": 2.0, "issue": 0.6}
 PAR.update({"own": [["vpVV", "ssvv"], ["pVVv", "vsvs"], ["VvVv", "sspv"]], "guest": [[["ppsv", "psvp"], ["vvps", "spsp"]], [["ppsv", "psvp"], ["ppvv", "spsp"]], [["psvp", "spvp"], ["svpv", "sppp"]]], "sg": [[2, 0], [1, 2]], "size": ["mamm", "ammm"], "sum": ["epep", "vevv"], "tree3": [0, 1], "evac": [1, 1], "split": [2, 1], "nch": 6, "xafter": 3, "tree": 2, "xzv": [[1, 1], [1, 1], [0, 1]], "oact": [0, 0], "ract": [[0, 0], [0, 0]], "first": 1.485, "upper": -1.33, "bonus": [0, 7.708], "rounds": 2, "look": 0, "greedy": 0, "lower": -0.236, "ownp": [-0.762, 4.275], "latep": [-6, -1.735], "xnp": [-5.724, -3.975], "nearp": [-1.057, 0.769], "expp": -6.421, "keep": 0})
 COST.update({"cy": 0.001, "ga": 1.7, "sc": 4.0, "pc": 0.0005, "hop": 0.218, "same": 0.138, "dma": 2.0, "rem": 2.628, "first": 2.0, "issue": 0.6})
+PAR.update({"askp": 0.0, "halfq": [1, 1, 1], "convp": 0.0})
+PAR.update({"wp": 0.0, "wact": [[1, 1], [1, 1], [1, 1]], "xnw": [[1024, 1024]] * 3, "expw": [[1024, 1024]] * 2})
+PAR.update({"own": [["vVVp", "vsvs"], ["VvpV", "vssv"], ["VvvV", "ssvv"]], "guest": [[["ppsv", "psvs"], ["vpvs", "spsp"]], [["ppsv", "pvsp"], ["pvvp", "spsp"]], [["psvp", "spvp"], ["vvps", "sppp"]]], "sg": [[2, 0], [2, 2]], "size": ["mamm", "ammm"], "sum": ["epep", "vevv"], "tree3": [1, 1], "evac": [1, 0], "split": [2, 2], "nch": 6, "xafter": 3, "tree": 3, "xzv": [[1, 1], [1, 1], [0, 1]], "oact": [0, 0], "ract": [[0, 0], [0, 0]], "first": 1.966, "upper": 0.174, "bonus": [0, 5.677], "rounds": 1, "look": 0, "greedy": 0, "lower": -0.236, "ownp": [-0.339, 3.912], "latep": [-6, 1.223], "xnp": [-5.01, -3.329], "nearp": [-1.057, 0.769], "expp": -0.258, "keep": 0, "askp": -2, "halfq": [1, 1, 1], "convp": -2.099})
+COST.update({"cy": 0.001, "ga": 1.694, "sc": 4.0, "pc": 0.0005, "hop": 0.219, "same": 0.138, "dma": 2.0, "rem": 3.288, "first": 2.0, "issue": 0.85})
+PAR.update({"conv": "aaaaaa"})
+PAR.update({"twact": [0, 0], "tpact": 0, "qact": [[0, 0], [0, 0], [0, 0]]})
+PAR.update({"own": [["hVvV", "vvhh"], ["VvVh", "hvhv"], ["VvVv", "hvvh"]], "guest": [[["hhhv", "vhhh"], ["vhvv", "hhhh"]], [["hhhv", "vhhh"], ["hvvh", "hhhh"]], [["hhvh", "vhhh"], ["vvhh", "hhhh"]]], "sg": [[1, 0], [1, 0]], "size": ["mamm", "ammm"], "sum": ["epep", "vevv"], "tree3": [0, 1], "evac": [1, 1], "split": [4, 2], "nch": 6, "xafter": 3, "tree": 2, "xzv": [[1, 1], [1, 1], [0, 0]], "oact": [0, 0], "ract": [[1, 0], [0, 0]], "first": 2.111, "upper": -1.566, "bonus": [0, 3.749], "rounds": 2, "look": 0, "greedy": 0, "lower": -0.332, "ownp": [1.857, 1.867], "latep": [-6, 0.646], "xnp": [-8, -1.135], "nearp": [-0.75, 0.769], "expp": -4.319, "keep": 0, "askp": -2, "halfq": [1, 1, 1], "convp": -2.531, "wp": -1.724, "wact": [[1, 1], [1, 1], [1, 1]], "xnw": [[1024, 1024], [1024, 1024], [2048, 1024]], "expw": [[2048, 2048], [1024, 2048]], "conv": "aaaaaa", "twact": [0, 0], "tpact": 0, "qact": [[0, 0], [0, 0], [0, 0]]})
+COST.update({"cy": 0.001042, "ga": 1.694, "sc": 4.0, "pc": 0.000521, "hop": 0.207, "same": 0.145, "dma": 2.0, "rem": 3.464, "first": 2.0, "issue": 0.916})
+COST.update({"row": 0.05, "far": 0.06, "byte": 1 / 25e3, "rem": 2.2})
+PAR.update({"xgate": ["ol", "w2"], "dl": [[1, 1], [1, 1]], "hs": [1, 1], "tree1": 1, "tree2": 2, "restp": -3.0})
+PAR.update({"own": [["hVvV", "hhvv"], ["vhVV", "hhvv"], ["VVvv", "hhvv"]], "guest": [[["hhhv", "vhhh"], ["vhvv", "hhhh"]], [["hhvv", "vhhh"], ["hvvh", "hhhh"]], [["hhvh", "vhhh"], ["hvvh", "hhhh"]]], "sg": [[1, 0], [1, 0]], "size": ["mamm", "ammm"], "sum": ["epep", "vvvv"], "tree3": [0, 1], "evac": [0, 1], "split": [4, 4], "nch": 4, "xafter": 2, "tree": 2, "xzv": [[1, 1], [1, 1], [0, 0]], "oact": [0, 0], "ract": [[1, 0], [0, 1]], "first": 2.788, "upper": -1.491, "bonus": [0, 2.523], "rounds": 2, "look": 0, "greedy": 0, "lower": -0.332, "ownp": [2.309, 1.867], "latep": [-3.364, -0.788], "xnp": [-8, 0.82], "nearp": [0.132, 0.769], "expp": -8.798, "keep": 0, "askp": -1.833, "halfq": [1, 1, 1], "convp": -4.527, "wp": -0.596, "wact": [[1, 1], [1, 1], [1, 1]], "xnw": [[1024, 1024], [1024, 1024], [2048, 1024]], "expw": [[2048, 1024], [1024, 1024]], "conv": "aaaava", "twact": [0, 0], "tpact": 0, "qact": [[0, 0], [0, 0], [0, 0]], "xgate": ["w1", "w1"], "dl": [[4, 4], [4, 4]], "hs": [1, 1], "tree1": 1, "tree2": 2, "restp": -2.502})
+COST.update({"cy": 0.00111, "ga": 1.694, "sc": 4.0, "pc": 0.000555, "hop": 0.207, "same": 0.156, "dma": 2.0, "rem": 2.36, "first": 2.0, "issue": 0.945, "row": 0.013, "far": 0.057, "byte": 4e-05})
+PAR.update({"early": [1, 1, 1], "cact": [[0, 0], [0, 0], [0, 0]]})
+PAR.update({"own": [["VhvV", "hvvh"], ["vVhV", "hvvh"], ["VvVV", "hvvh"]], "guest": [[["hhhv", "hhvh"], ["hvvv", "hhhh"]], [["hhhv", "hhvh"], ["hvvv", "hhhh"]], [["hhhv", "hhvh"], ["hvvv", "hhhh"]]], "sg": [[1, 0], [1, 0]], "size": ["mamm", "ammm"], "sum": ["epep", "vvev"], "tree3": [0, 1], "evac": [1, 1], "split": [2, 1], "nch": 4, "xafter": 2, "tree": 2, "xzv": [[1, 1], [0, 1], [0, 1]], "oact": [0, 1], "ract": [[1, 0], [0, 1]], "first": 1.535, "upper": -1.549, "bonus": [1.008, 2.523], "rounds": 2, "look": 0, "greedy": 0, "lower": -0.332, "ownp": [2.309, 3.353], "latep": [-2.956, -2.268], "xnp": [-6.44, -3.173], "nearp": [-0.994, 0.303], "expp": -0.959, "keep": 0.011, "askp": 1.286, "halfq": [1, 1, 1], "convp": -6, "wp": 1.353, "wact": [[1, 1], [1, 1], [1, 1]], "xnw": [[2048, 1024], [2048, 1024], [1024, 512]], "expw": [[1024, 1024], [1024, 1024]], "conv": "aaaaav", "twact": [0, 0], "tpact": 0, "qact": [[0, 0], [0, 0], [0, 0]], "xgate": ["w1", "w1"], "dl": [[4, 4], [4, 3]], "hs": [1, 1], "tree1": 2, "tree2": 3, "restp": -3.435, "early": [1, 1, 1], "cact": [[1, 1], [1, 0], [0, 0]]})
+COST.update({"cy": 0.00107165, "ga": 1.685, "sc": 4.0, "pc": 0.000535825, "hop": 0.207, "same": 0.156, "dma": 2.0, "rem": 2.397, "first": 2.0, "issue": 1.031, "row": 0.023, "far": 0.056, "byte": 4e-05})
 
 SCRATCH = {
     "ri": ("sbuf", [128, V], "int32"),
@@ -43,10 +58,11 @@ SCRATCH = {
     "nb": ("sbuf", [128, 4096], "bfloat16"),
     "xn": ("sbuf", [128, 4096], "bfloat16"),
     "gg": ("sbuf", [128, 4096], "float32"),
-    "gh": ("sbuf", [128, 2048], "float16"),
+    "gh": ("sbuf", [128, 4096], "float16"),
+    "w32": ("sbuf", [128, 512], "float32"),
     "ab0": ("sbuf", [128, 2, 2048], "float32"),
     "ab1": ("sbuf", [128, 2, 2048], "float32"),
-    "acc": ("sbuf", [128, 256], "float32"),
+    "acc": ("sbuf", [128, 512], "float32"),
     "c16": ("sbuf", [128, 512], "float16"),
     "w1": ("sbuf", [128, 512], "float16"),
     "w2": ("sbuf", [128, 512], "float16"),
@@ -95,18 +111,18 @@ SCRATCH = {
 }
 for _t in range(RO):
     for _b in range(2):
-        SCRATCH["qs%d%d" % (_t, _b)] = ("sbuf", [128, 272], "uint16")
-        SCRATCH["ql%d%d" % (_t, _b)] = ("sbuf", [128, 272], "uint16")
+        SCRATCH["qs%d%d" % (_t, _b)] = ("sbuf", [128, 256], "uint16")
+        SCRATCH["ql%d%d" % (_t, _b)] = ("sbuf", [128, 256], "uint16")
+        SCRATCH["vl%d%d" % (_t, _b)] = ("sbuf", [128, 16], "uint16")
         SCRATCH["rs%d%d" % (_t, _b)] = ("sbuf", [128, 256], "bfloat16")
         SCRATCH["rl%d%d" % (_t, _b)] = ("sbuf", [128, 256], "bfloat16")
-for _b in range(2):
-    SCRATCH["vs%d" % _b] = ("sbuf", [128, 16], "uint16")
-    SCRATCH["vl%d" % _b] = ("sbuf", [128, 16], "uint16")
+    SCRATCH["vs%d" % _t] = ("sbuf", [128, 32], "uint16")
 for _b in range(8):
     SCRATCH["p%d" % _b] = ("psum", [128, 512], "float32")
 
-SEMAPHORES = (["dve", "act", "pe", "pool", "sent", "av0", "av1"] + ["dm%d" % _i for _i in range(30)]
-              + ["aq%d%d" % (_t, _b) for _t in range(RO) for _b in range(2)]
+SEMAPHORES = (["dve", "act", "pe", "pool", "sent"] + ["dm%d" % _i for _i in range(40)]
+              + ["av%d%d" % (_t, _b) for _t in range(RO) for _b in range(2)]
+              + ["aq%d%d%d" % (_t, _b, _h) for _t in range(RO) for _b in range(2) for _h in range(2)]
               + ["ar%d%d%d" % (_t, _b, _h) for _t in range(RO) for _b in range(2) for _h in range(2)])
 
 AL = AluOpType
@@ -143,13 +159,15 @@ def price(ops, C):
     for o in ops:
         c = o["cost"]
         o["dur"] = (c.get("fix", 0.0) + C["cy"] * (c.get("cy", 0) + C["ga"] * c.get("ga", 0) + C["sc"] * c.get("sc", 0))
-                    + C["pc"] * c.get("pc", 0) + C["issue"] * c.get("issue", 0))
+                    + C["pc"] * c.get("pc", 0) + C["issue"] * c.get("issue", 0) + C["row"] * c.get("row", 0)
+                    + C["far"] * c.get("far", 0) + C["byte"] * c.get("byte", 0))
         o["lat"] = c.get("lat", 0.0) + C["dma"] * c.get("dma", 0) + C["rem"] * c.get("rem", 0) + C["first"] * c.get("first", 0)
 
 
 def build(g, core, T, topo, rank):
     ops = []
     ahead = [0.0]
+    table = []
 
     def ap(r):
         if len(r) == 2:
@@ -209,6 +227,9 @@ def build(g, core, T, topo, rank):
                 k["scale"] = scale
             return g.scalar.activation(ap(out), ap(in0), func, **k)
         c = {"fix": 0.065, "ga": cnt(out)} if len(in0) == 2 else {"fix": 0.03, "cy": max(cnt(out), 64)}
+        if func == AF.Exp and not table:
+            table.append(1)
+            c["fix"] += 1.3
         return add("act", fn, [in0], [out], c, **kw)
 
     def mm(out, lhs, rhs, start, stop, fam=None, **kw):
@@ -233,20 +254,30 @@ def build(g, core, T, topo, rank):
         return add("pool", lambda: g.affine_select(ap(buf), ap(buf), pattern, op, value, base, cm), [buf], [buf],
                    {"fix": 0.17, "cy": 2 * cnt(buf)}, **kw)
 
-    def dma(eng, fn, reads, writes, nbytes, **kw):
-        c = {"dma": 1, "lat": nbytes / 600e3}
-        c.update({"issue": 1} if eng == "pool" else {"fix": 0.1})
-        return add(eng, fn, reads, writes, c, kind="dma", **kw)
+    def narrow(dst, src):
+        return add("pool", lambda: g.affine_select(ap(dst), ap(src), [[0, cnt(src)]], AL.is_ge, 0.0, 0, 0), [src], [dst],
+                   {"fix": 0.17, "cy": 2 * cnt(src)})
 
-    def send(src, dst_name, sem, to_rank, first=False):
+    def moving(i, reads, writes, cost):
+        j = add("ring", None, reads, writes, cost, kind="rows")
+        ops[j]["of"] = i
+        return j
+
+    def dma(eng, fn, reads, writes, rows, row, **kw):
+        i = add(eng, fn, reads, writes, {"issue": 1, "dma": 0.65} if eng == "pool" else {"fix": 0.1, "dma": 0.65}, kind="dma", **kw)
+        return moving(i, reads, writes, {"row": rows / 16, "fix": rows / 16 * row / 38e3, "dma": 0.35})
+
+    def send(src, dst_name, sem, to_rank, first=False, at=None):
         to = T.cores[to_rank]
         rid, pid, _ = topo.addr(to)
+        at = src[1] if at is None else at
 
         def fn():
-            return g.remote_dma(T[dst_name][:, src[1]:src[2]], ap(src), T.sem[sem], T.sem.sent, pid, rid, topo.mask(core, to))
-        i = add("pool", fn, [src], [], {"issue": 1, "rem": 1, "first": 1 if first else 0}, kind="rem")
+            return g.remote_dma(T[dst_name][:, at:at + cnt(src)], ap(src), T.sem[sem], T.sem.sent, pid, rid, topo.mask(core, to))
+        i = add("pool", fn, [src], [], {"issue": 1, "rem": 0.5, "first": 1 if first else 0}, kind="rem")
         ops[i]["width"] = len(topo.engines(core, to))
-        return i
+        rows = 128 / ops[i]["width"]
+        return moving(i, [src], [], {"far": rows, "byte": rows * 2 * cnt(src), "rem": 0.5})
 
     def jsl(name, shift):
         x = (-shift) % 128
@@ -255,23 +286,23 @@ def build(g, core, T, topo, rank):
     RW = rf("rw", 0, V)
     I16 = rf("jj", 0, 128)
 
-    ahead[0] = 9.0
-    dma("sync", lambda: g.sync.dma_start(T.wi[:], T.w0[:]), [], [rf("wi")], 8192)
-    ahead[0] = 0.0
+    loads = [dma("sync", lambda: g.sync.dma_start(T.wi[:], T.w0[:]), [], [rf("wi")], 128, 64) - 1]
     nch = PAR["nch"]
     step = V // nch
     pieces = [(i * step, V if i == nch - 1 else (i + 1) * step) for i in range(nch)]
     for i, (a, b) in enumerate(pieces):
         q = g.scalar if i % 2 == 0 else g.sync
-        ahead[0] = 8.0 - i
-        dma("act" if i % 2 == 0 else "sync", (lambda q=q, a=a, b=b: q.dma_start(T.ri[:, a:b], T.rec[:, a:b])), [],
-            [rf("ri", a, b)], 128 * 4 * b)
-    ahead[0] = 0.0
-    gate = [rf("ri", *pieces[PAR["xafter"]])]
-    late = 128 * 4 * (V - pieces[PAR["xafter"]][1])
-    dma("sync", lambda: g.sync.dma_start(T.xs[:, 15:15 + V], T.x[:]), gate, [rf("xs", 15, 15 + V)], late + 128 * 2 * V)
-    dma("sync", lambda: g.sync.dma_start(T.xs[:, 15 + V:17 + V], T.x[:, 0:2]), gate, [rf("xs", 15 + V, 17 + V)], late + 128 * 2 * V)
-    dma("sync", lambda: g.sync.dma_start(T.xu[:], T.x[:]), [rf("xs", 15, 15 + V)], [rf("xu")], 128 * 2 * V)
+        loads.append(dma("act" if i % 2 == 0 else "sync", (lambda q=q, a=a, b=b: q.dma_start(T.ri[:, a:b], T.rec[:, a:b])), [],
+                         [rf("ri", a, b)], 128, 4 * (b - a), after=loads[-2:-1]) - 1)
+
+    def states(which, gate):
+        if which == 0:
+            dma("sync", lambda: g.sync.dma_start(T.xs[:, 15:15 + V], T.x[:]), gate, [rf("xs", 15, 15 + V)], 128, 2 * V)
+            act(rf("xs", 15 + V, 16 + V), rf("xs", 15, 16), AF.Copy)
+        else:
+            dma("sync", lambda: g.sync.dma_start(T.xu[:], T.x[:]), gate, [rf("xu")], 128, 2 * V)
+    if PAR["xgate"][0] == "ri":
+        states(0, [rf("ri", *pieces[PAR["xafter"]])])
     XS = rf("xs", 16, 16 + V)
 
     iota(rf("kp", 0, 4), [[0, 4]], 0, 1)
@@ -296,7 +327,8 @@ def build(g, core, T, topo, rank):
     fill(rf("rw", V, V + 128), 0.0)
     fill(rf("bo"), 1.0)
     fill(rf("thr"), 7.5)
-    fill(rf("cut"), 1.0)
+    for c0 in (0, 256):
+        act(rf("cut", c0, c0 + 256), rf("ka"), AF.Exp, scale=0.0)
     fill(rf("cut", 0, 512, 64), 0.0)
     cp(rf("bf"), rf("bb", 0, 128, 16))
     iota(rf("kq"), [[-1, 3], [0, 8], [1, 16]], 15, 0)
@@ -313,13 +345,23 @@ def build(g, core, T, topo, rank):
 
     cp(rf("wl"), rf("wi"))
     ts(rf("w16"), rf("wi"), float(CEN), None, AL.subtract)
-    wsend = []
-    for b in range(2):
-        group(rf("p%d" % (b + 1), 256, 272), [(jsl("jj", 16 * (1 + b)), rf("w16"))])
-        ts(rf("vs%d" % b), rf("p%d" % (b + 1), 256, 272), float(CEN), None, AL.add)
-        wsend.append(send(rf("vs%d" % b), "vl%d" % b, "av%d" % b, (rank + HOPS[0][b]) % NR, first=True))
-    for a, b in pieces:
-        ts(rf("rw", a, b), rf("ri", a, b), float(CEN), None, AL.subtract)
+    wsend = {}
+
+    def times_ahead(t):
+        for b in range(2):
+            group(rf("p3", 288 + 16 * b, 304 + 16 * b), [(jsl("jj", 16 * (t + 1 + b)), rf("w16"))])
+        ts(rf("vs%d" % t), rf("p3", 288, 320), float(CEN), None, AL.add)
+        for b in range(2):
+            wsend[(t, b)] = send(rf("vs%d" % t, 16 * b, 16 * b + 16), "vl%d%d" % (t, b), "av%d%d" % (t, b),
+                                 (rank + HOPS[t][b]) % NR, first=(t == 0), at=0)
+    times_ahead(0)
+    ahead[0] = PAR["convp"]
+    for i, (a, b) in enumerate(pieces):
+        if PAR["conv"][i] == "a":
+            act(rf("rw", a, b), rf("ri", a, b), AF.Identity, bias=-float(CEN))
+        else:
+            ts(rf("rw", a, b), rf("ri", a, b), float(CEN), None, AL.subtract)
+    ahead[0] = 0.0
 
     ring = {"p": 0, "g": 0, "h": 0}
 
@@ -330,7 +372,10 @@ def build(g, core, T, topo, rank):
         return "p%d" % banks[ring["p"] % len(banks)]
 
     def twice(buf, h):
-        cp(rf(buf, 384 * h, 384 * h + 128), rf(buf, 128 + 128 * h, 256 + 128 * h))
+        if PAR["twact"][buf != "c16"]:
+            act(rf(buf, 384 * h, 384 * h + 128), rf(buf, 128 + 128 * h, 256 + 128 * h), AF.Copy)
+        else:
+            cp(rf(buf, 384 * h, 384 * h + 128), rf(buf, 128 + 128 * h, 256 + 128 * h))
 
     def count_rows(dbuf, h, k, cbank, c0, shift, fam):
         x = (16 * shift) % 128
@@ -343,10 +388,21 @@ def build(g, core, T, topo, rank):
         wref, wone = rf(wbuf, 256 * h, 256 * h + 256), rf(wbuf, 128 + 128 * h, 256 + 128 * h)
         d0, l0 = 2048 * h, 128 * h
         for unit, how in enumerate(kinds):
-            if how not in "psuv":
+            if how not in "hpsuv":
                 continue
             k0, k1 = 2 * unit, 2 * unit + 2
             dd = rf(dbuf, d0 + 256 * k0, d0 + 256 * k1)
+            if how == "h":
+                pb, e0 = bank(), 512 * (ring["h"] % 8)
+                ring["h"] += 1
+                act(rf("gh", e0, e0 + 512), (RW, rf(lists, l0 + 16 * k0, l0 + 16 * k1)), AF.Copy, arrive=arrive)
+                for i in range(4):
+                    group(rf(pb, 128 * i, 128 * i + 128),
+                          [(rf("ni"), wone), (I16, rf("gh", e0 + 128 * i, e0 + 128 * i + 128))])
+                ts(dd, rf(pb), MAGIC, MAGIC, AL.add, AL.is_equal)
+                for k in range(2 * k0, 2 * k1):
+                    count_rows(dbuf, h, k, cbank, 128 * h, shift, fam)
+                continue
             if how != "v":
                 c0 = 512 * (ring["g"] % 8)
                 ring["g"] += 1
@@ -354,9 +410,7 @@ def build(g, core, T, topo, rank):
             if how == "p":
                 pb, e0 = bank(), 512 * (ring["h"] % 4)
                 ring["h"] += 1
-                src, dst = rf("gg", c0, c0 + 512), rf("gh", e0, e0 + 512)
-                add("pool", (lambda src=src, dst=dst: g.affine_select(ap(dst), ap(src), [[0, 512]], AL.is_ge, 0.0, 0, 0)),
-                    [src], [dst], {"fix": 0.17, "cy": 1024})
+                narrow(rf("gh", e0, e0 + 512), rf("gg", c0, c0 + 512))
                 for i in range(4):
                     group(rf(pb, 128 * i, 128 * i + 128),
                           [(rf("ni"), wone), (I16, rf("gh", e0 + 128 * i, e0 + 128 * i + 128))])
@@ -383,15 +437,37 @@ def build(g, core, T, topo, rank):
             return act(out, counts, AF.Sign, bias=-9.5)
         return ts(out, counts, 9.5, None, AL.is_ge)
 
-    def halve(s, levels, after):
+    def offsets(out, names, by_scalar):
+        if by_scalar:
+            return act(out, names, AF.Identity, bias=float(CEN))
+        return ts(out, names, float(CEN), None, AL.add)
+
+    def halve(s, levels, after, part):
         buf = "ab%d" % (s % 2)
+        h0, h1 = min(part), max(part) + 1
+        region = rf(buf, 2048 * h0, 2048 * h1)
         for lv in levels:
+            if lv >= PAR["dl"][s][h0]:
+                continue
             w = 1024 >> lv
-            dma("pool", (lambda w=w: g.dma_start(T[buf][:, :, 0:w], T[buf][:, :, w:2 * w], accum_op=AL.add)),
-                [rf(buf, 0, 4096)], [rf(buf, 0, 4096)], 128 * 16 * w, after=after)
+            dma("pool", (lambda w=w: g.dma_start(T[buf][:, h0:h1, 0:w], T[buf][:, h0:h1, w:2 * w], accum_op=AL.add)),
+                [region], [region], 128 * len(part), 8 * w, after=after)
             if lv == 3:
-                dma("sync", lambda: g.sync.dma_start(T.y[:, 256 * s:256 * s + 256], T[buf][:, :, 0:128]),
-                    [rf(buf, 0, 4096)], [], 128 * 1024)
+                dma("sync", lambda: g.sync.dma_start(T.y[:, 256 * s + 128 * h0:256 * s + 128 * h1], T[buf][:, h0:h1, 0:128]),
+                    [region], [], 128 * len(part), 512)
+
+    def rest(s):
+        buf = "ab%d" % (s % 2)
+        halves = [h for h in (1, 0) if PAR["dl"][s][h if PAR["hs"][s] else 0] < 4]
+        for h in halves:
+            rows = 16 >> PAR["dl"][s][h if PAR["hs"][s] else 0]
+            group(rf("p3", 128 * h, 128 * h + 128), [(rf("i32"), rf(buf, 2048 * h + 128 * k, 2048 * h + 128 * k + 128))
+                                                     for k in range(rows)])
+        if halves:
+            a, b = 128 * min(halves), 128 * max(halves) + 128
+            act(rf("acc", 256 + a, 256 + b), rf("p3", a, b), AF.Copy)
+            dma("sync", lambda: g.sync.dma_start(T.y[:, 256 * s + a:256 * s + b], T.acc[:, 256 + a:256 + b]),
+                [rf("acc", 256 + a, 256 + b)], [], 128, 4 * (b - a))
 
     def choose(t, h, answers):
         a, b, m0, m1 = 128 * h, 128 * h + 128, 8 * h, 8 * h + 8
@@ -401,7 +477,7 @@ def build(g, core, T, topo, rank):
         ts(rf("ok", a, b), rf(pb, 0, 128), 2.5, -BIG, AL.is_ge, AL.mult)
         group(rf(pb, 128, 256), [(I16, rf("c16", 128 + a, 128 + b)), (rf("ni"), rf("tp", a, b)),
                                  (rf("uu", 128 * t, 128 * t + 128), rf("ok", a, b))])
-        none = rf("p3", 256 + m0, 256 + m1)
+        none = rf(pb if PAR["early"][t] and h else "p3", 272 + m0, 272 + m1)
         group(none, [(I16, rf("w16", m0, m1)), (rf("ni"), rf("t16", m0, m1))]
               + [(jsl("bb", r), rf("ok", a + r, b, 16)) for r in range(16)])
         ts(rf("sn", a, b), rf(pb, 128, 256), BIG + LOW, BIG, AL.max, AL.subtract)
@@ -416,7 +492,8 @@ def build(g, core, T, topo, rank):
         if t == RO - 1:
             return
         ts(rf("qq", m0, m1), zs, TOZ, None, AL.add)
-        ts(rf("w16", m0, m1), zs, TOZ - CEN, None, AL.add)
+        if h == 0:
+            ts(rf("w16"), rf("wl"), float(CEN), None, AL.subtract)
         mm(rf(pb), I16, rf("tri"), True, False)
         for m in range(8):
             c0 = a + 64 * (m // 4)
@@ -459,8 +536,8 @@ def build(g, core, T, topo, rank):
         group(rf(pb, 384, 512), [(rf("np_", a, b), I16)])
         tt(rf("qe", a, b), rf(pb, 384, 512), rf("ee", a, b), AL.mult)
         keep, ahead[0] = ahead[0], PAR["expp"]
-        for i in range(4):
-            ab = rf(buf, 2048 * h + 512 * i, 2048 * h + 512 * i + 512)
+        for c0 in range(2048 * h, 2048 * h + 2048, PAR["expw"][t][h]):
+            ab = rf(buf, c0, c0 + PAR["expw"][t][h])
             act(ab, ab, AF.Exp, scale=-1.0)
         ahead[0] = keep
 
@@ -540,41 +617,52 @@ def build(g, core, T, topo, rank):
             onto(total)
         elif nblocks:
             act(acc, total, AF.Copy)
-        dma("sync", lambda: g.sync.dma_start(T.y[:, 256 * t + a:256 * t + b], T.acc[:, a:b]), [acc], [], 128 * 512)
+        dma("sync", lambda: g.sync.dma_start(T.y[:, 256 * t + a:256 * t + b], T.acc[:, a:b]), [acc], [], 128, 512)
 
     for t in range(RO):
         last = t == RO - 1
         ring["t"] = t
         CC = rf("c16", 128, 384)
-        if t == 0:
-            ts(CC, (rf("ri"), rf("wl")), float(CEN), None, AL.subtract)
-        else:
-            cp(CC, (RW, rf("wl")))
-        for be in range(8):
-            o = rf("t2", 128 * (be // 4) + be % 4, 128 * (be // 4) + 128, 4)
-            i = rf("c16", 128 + 32 * be, 160 + 32 * be)
-            add("dve", (lambda o=o, i=i: g.vector.transpose(ap(o), ap(i))), [i], [o], {"cy": 64})
-        sends = []
-        for b, pb in ((0, "p1"), (1, "p2"), (2, "p3")):
-            s = 0 if b == 2 else t + 1 + b
-            for h in range(2):
-                for gp in range(2):
-                    group(rf(pb, 128 * h + gp, 128 * h + 128, 2),
-                          [(jsl("j%d" % gp, 16 * (ga - gp + s)), rf("t2", 128 * h + 64 * ga, 128 * h + 64 * ga + 64))
-                           for ga in range(2)])
-            if b < 2:
-                wide = 256 if t == 0 else 272
-                if wide > 256:
-                    group(rf(pb, 256, 272), [(jsl("jj", 16 * s), rf("w16"))])
-                ts(rf("qs%d%d" % (t, b), 0, wide), rf(pb, 0, wide), float(CEN), None, AL.add)
-                sends.append(send(rf("qs%d%d" % (t, b), 0, wide), "ql%d%d" % (t, b), "aq%d%d" % (t, b),
-                                  (rank + HOPS[t][b]) % NR))
+        sends, arr = [], {}
+        ahead[0] = PAR["askp"]
+        for part in (((1,), (0,)) if PAR["halfq"][t] else ((1, 0),)):
+            a, e = 128 * min(part), 128 * max(part) + 128
+            cc, wl = rf("c16", 128 + a, 128 + e), rf("wl", a // 16, e // 16)
+            if t == 0:
+                ts(cc, (rf("ri"), wl), float(CEN), None, AL.subtract)
+            elif PAR["cact"][t][part[0]]:
+                act(cc, (RW, wl), AF.Copy)
             else:
-                ts(rf("ol"), rf(pb, 0, 256), float(CEN), None, AL.add)
+                cp(cc, (RW, wl))
+            for be in range(a // 64, e // 64):
+                o = rf("t2", 128 * (be // 2) + be % 2, 128 * (be // 2) + 128, 2)
+                i = rf("c16", 128 + 64 * be, 192 + 64 * be)
+                add("dve", (lambda o=o, i=i: g.vector.transpose(ap(o), ap(i))), [i], [o], {"cy": 64})
+            for b in range(3):
+                s = 0 if b == 2 else t + 1 + b
+                pb = ("p1", "p2", "p3")[b] if 1 in part else ("p4", "p5", "p6")[b]
+                for h in part:
+                    for m in range(4):
+                        gp, c0 = m % 2, 128 * h + 64 * (m // 2)
+                        group(rf(pb, 128 * h + m, 128 * h + 128, 4),
+                              [(jsl("j%d" % gp, 16 * (ga - gp + s)), rf("t2", c0 + 32 * ga, c0 + 32 * ga + 32))
+                               for ga in range(2)])
+                if b < 2:
+                    sem = "aq%d%d%d" % (t, b, part[0])
+                    offsets(rf("qs%d%d" % (t, b), a, e), rf(pb, a, e), PAR["qact"][b][part[0]])
+                    sends.append(send(rf("qs%d%d" % (t, b), a, e), "ql%d%d" % (t, b), sem, (rank + HOPS[t][b]) % NR))
+                    for h in part:
+                        arr[(b, h)] = (sem, sends[-1])
+                else:
+                    offsets(rf("ol", a, e), rf(pb, a, e), PAR["qact"][b][part[0]])
+        ahead[0] = 0.0
         for h in range(2):
             if "v" in PAR["own"][t][h].lower():
                 twice("c16", h)
-        ts(rf("tp"), CC, V - CEN - 1.5, float(V), AL.is_gt, AL.mult)
+        if PAR["tpact"]:
+            act(rf("tp"), CC, AF.Relu, bias=-float(V * (V - CEN - 2)), scale=float(V))
+        else:
+            ts(rf("tp"), CC, V - CEN - 1.5, float(V), AL.is_gt, AL.mult)
         if t == 0:
             for buf, rep in ((rf("uu"), 3), (rf("bo"), 1)):
                 asel(buf, [[0, rep], [-16, 8], [0, 16]], AL.is_ge, 0.0, 0, 1, after=sends)
@@ -586,22 +674,30 @@ def build(g, core, T, topo, rank):
                         asel(rf("thr", 256 * s + 128 * h, 256 * s + 128 * h + 128), [[0, 8], [1, 16]], AL.is_ge, -0.5,
                              -4 * PAR["sg"][s][h], 0, after=sends)
         else:
-            halve(t - 1, range(PAR["tree"]), sends)
+            halve(t - 1, range(PAR["tree"]), sends, (0,) if PAR["hs"][t - 1] else (0, 1))
+            if PAR["hs"][t - 1]:
+                halve(t - 1, range(PAR["tree1"], max(PAR["tree1"], PAR["tree2"])), sends, (1,))
         ts(rf("t16"), rf("w16"), float(V - CEN - 1), float(V), AL.is_equal, AL.mult)
         if not last:
             group(rf("p3", 0, 256), [(I16, CC), (rf("ni"), rf("tp"))])
             act(rf("n32"), rf("p3", 0, 256), AF.Identity, bias=1.0)
 
-        arr = [("aq%d%d" % (t, b), sends[b]) for b in range(2)]
         for b in range(2):
             wb = "w%d" % (b + 1)
-            if t == 0:
-                cp(rf(wb, 128, 384), (RW, rf("vl%d" % b)), arrive=("av%d" % b, wsend[b]))
+            came = ("av%d%d" % (t, b), wsend[(t, b)])
+            ahead[0] = PAR["wp"]
+            if PAR["wact"][t][b]:
+                act(rf(wb, 128, 384), (RW, rf("vl%d%d" % (t, b))), AF.Copy, arrive=came)
             else:
-                cp(rf(wb, 128, 384), (RW, rf("ql%d%d" % (t, b), 256, 272)), arrive=arr[b])
+                cp(rf(wb, 128, 384), (RW, rf("vl%d%d" % (t, b))), arrive=came)
+            ahead[0] = 0.0
             for h in range(2):
                 if "v" in PAR["guest"][t][b][h]:
                     twice(wb, h)
+
+        for i in range(2):
+            if t == 0 and PAR["xgate"][i] != "ri":
+                states(i, [rf(PAR["xgate"][i], 128, 256)])
 
         def own_rows(h, late, after):
             kinds = PAR["own"][t][h].swapcase() if late else PAR["own"][t][h]
@@ -616,25 +712,30 @@ def build(g, core, T, topo, rank):
         for h in (1, 0):
             for b in range(2):
                 ahead[0] = PAR["bonus"][h] + (0.0 if b else PAR["first"])
-                wb, pb = "w%d" % (b + 1), "p%d" % (b + 1)
+                wb, pb = "w%d" % (b + 1), "p3" if PAR["early"][t] and (b, h) == (0, 0) else "p%d" % (b + 1)
                 kinds, wps = PAR["guest"][t][b][h], rf("p7", 256 * b, 256 * b + 256)
                 if "u" in kinds:
                     for i in range(2):
                         group(rf("p7", 256 * b + 128 * i, 256 * b + 128 * i + 128), [(I16, rf(wb, 128 + 128 * h, 256 + 128 * h))])
-                likeness("d%d" % (b + 1), h, "ql%d%d" % (t, b), wb, kinds, wps, arr[b], pb, t + 1 + b, "g%d%d%d" % (t, b, h))
+                likeness("d%d" % (b + 1), h, "ql%d%d" % (t, b), wb, kinds, wps, arr[(b, h)], pb, t + 1 + b, "g%d%d%d" % (t, b, h))
                 rs = rf("rs%d%d" % (t, b), 128 * h, 128 * h + 128)
                 made.append(enough(rs, rf(pb, 128 * h, 128 * h + 128), PAR["ract"][b][h]))
                 answers[(b, h)] = send(rs, "rl%d%d" % (t, b), "ar%d%d%d" % (t, b, h), (rank - HOPS[t][b]) % NR)
         ahead[0] = 0.0
         if t > 0:
-            halve(t - 1, range(PAR["tree"], 4), list(answers.values()))
+            later = list(answers.values())
+            halve(t - 1, range(PAR["tree"], 4), later, (0,) if PAR["hs"][t - 1] else (0, 1))
+            if PAR["hs"][t - 1]:
+                halve(t - 1, range(max(PAR["tree1"], PAR["tree2"]), 4), later, (1,))
+            ahead[0] = PAR["restp"]
+            rest(t - 1)
         ahead[0] = PAR["latep"][1]
         own_rows(1, True, made)
         for h in (1, 0):
             ahead[0] = PAR["xnp"][h]
-            for i in range(4):
-                c0 = 2048 * h + 512 * i
-                act(rf("xn", c0, c0 + 512), (XS, rf("ol", c0 // 16, c0 // 16 + 32)), AF.Copy)
+            w = PAR["xnw"][t][h]
+            for c0 in range(2048 * h, 2048 * h + 2048, w):
+                act(rf("xn", c0, c0 + w), (XS, rf("ol", c0 // 16, (c0 + w) // 16)), AF.Copy)
 
         ahead[0] = PAR["upper"]
         enough(rf("o0", 128, 256), rf("p0", 128, 256), PAR["oact"][1])
@@ -653,6 +754,9 @@ def build(g, core, T, topo, rank):
             near(t, 1)
             ahead[0] = PAR["lower"]
             choose(t, 0, answers)
+            times_ahead(t + 1)
+            if PAR["hs"][t]:
+                halve(t, range(PAR["tree1"]), None, (1,))
             rewrite(1)
             ahead[0] = PAR["nearp"][0]
             near(t, 0)
@@ -666,6 +770,11 @@ def plan(ops):
     seen, older = {}, {}
     for i, o in enumerate(ops):
         dep, soft = set(), set()
+        if o["kind"] == "rows":
+            for r, isw in [(r, False) for r in o["r"]] + [(r, True) for r in o["w"]]:
+                seen.setdefault(r[0], []).append((i, r, isw))
+            o["dep"], o["soft"] = {o["of"]}, soft
+            continue
         for r in o["r"] + o["w"]:
             if in_psum(r) and seen.get(r[0]) and ops[seen[r[0]][-1][0]]["eng"] != o["eng"]:
                 older[r[0]], seen[r[0]] = seen[r[0]], []
@@ -681,7 +790,7 @@ def plan(ops):
                         soft.add(j)
                 elif (isw or wasw) and meet(r, q):
                     dep.add(j)
-        for r, isw in [(r, False) for r in o["r"]] + [(r, True) for r in o["w"]]:
+        for r, isw in [(r, False) for r in o["r"]] + [(r, True) for r in o["w"]] if o["kind"] == "c" else []:
             lst = seen.setdefault(r[0], [])
             if isw and not in_psum(r) and r[3] == 1:
                 lst[:] = [e for e in lst if not (r[1] <= e[1][1] and e[1][2] <= r[2])]
@@ -696,7 +805,7 @@ def order(ops):
     for i, o in enumerate(ops):
         p = {}
         for j in o["dep"]:
-            p[j] = ops[j]["dur"] + ops[j]["lat"] + (C["same"] if ops[j]["eng"] == o["eng"] else C["hop"])
+            p[j] = ops[j]["dur"] + ops[j]["lat"] + (0.0 if o["kind"] == "rows" else C["same"] if ops[j]["eng"] == o["eng"] else C["hop"])
         for j in o["soft"]:
             p.setdefault(j, ops[j]["dur"])
         for j in o["after"] or ():
@@ -771,6 +880,7 @@ def order(ops):
     for _ in range(PAR["rounds"]):
         rev = place(ranked([-start[i] - dur[i] for i in range(n)], back, pred), back, tail)
         key = [-rev[i] - dur[i] - PAR["keep"] * ops[i]["bonus"] for i in range(n)]
+        key = [key[ops[i].get("of", i)] for i in range(n)]
         start = greedy(key) if PAR["greedy"] else place(ranked(key, pred, succ), pred, zero)
         end = max(start[i] + dur[i] + tail[i] for i in range(n))
         if end < best[0]:
@@ -781,6 +891,9 @@ def order(ops):
 
 def emit(g, T, topo, core, ops, seq):
     queue = {"dve": g.vector, "act": g.scalar, "pe": g.tensor, "pool": g, "sync": g.sync}
+    seq = [i for i in seq if ops[i]["kind"] != "rows"]
+    for o in ops:
+        o["dep"] = {ops[j].get("of", j) for j in o["dep"]}
     num, key = {}, {}
     ndma = 0
     for i in seq:
@@ -820,7 +933,7 @@ def emit(g, T, topo, core, ops, seq):
     rank = T.rank_of(core)
 
     def arrival(name):
-        hop = HOPS[0][int(name[2])] if name[1] == "v" else HOPS[int(name[2])][int(name[3])]
+        hop = HOPS[int(name[2])][int(name[3])]
         sender = (rank + hop if name[1] == "r" else rank - hop) % NR
         return len(topo.engines(T.cores[sender], core))
     nsent = 0

from concourse.mybir import AluOpType, ActivationFunctionType

V, RO, NR = 3328, 3, 6
CEN = 1664
BIG = 8192.0
LOW = -1681.0
TOZ = CEN + 1 - 16 * LOW
MAGIC = 50331648.0
HALF = 12582912.0
HOPS = ((1, 2), (3, 4), (5, 1))

PAR = {
    "own": (("VvVv", "vssv"), ("vVuV", "vssv"), ("VvvV", "vssv")),
    "guest": ((("uvss", "ssvu"), ("ssvu", "suss")), (("svsu", "ssvu"), ("suvs", "svss")), (("svus", "ssvu"), ("ssvu", "sssv"))),
    "sg": ((2, 1), (0, 1)),
    "size": ("ammm", "amma"),
    "sum": ("vvve", "vvvv"),
    "tree3": (0, 1), "evac": (1, 0),
    "split": (1, 1),
    "nch": 6,
    "xafter": 3,
    "tree": 3,
    "xzv": ((1, 1), (1, 1), (1, 1)),
    "oact": (0, 0), "ract": ((0, 0), (0, 0)),
    "first": 1.33, "upper": 1.07, "bonus": (1.04, 4.32), "rounds": 1, "look": 0.0, "greedy": 0,
    "lower": 0.0, "ownp": (0.0, 0.0), "latep": (0.0, 0.0), "xnp": (0.0, 0.0), "nearp": (0.0, 0.0), "expp": 0.0, "keep": 0.0,
}
COST = {"cy": 1.0e-3, "ga": 1.656, "sc": 4.0, "pc": 0.5e-3, "hop": 0.218, "same": 0.239, "dma": 2.0,
        "rem": 2.841, "first": 2.0, "issue": 0.6}
PAR.update({"own": [["vpVV", "ssvv"], ["pVVv", "vsvs"], ["VvVv", "sspv"]], "guest": [[["ppsv", "psvp"], ["vvps", "spsp"]], [["ppsv", "psvp"], ["ppvv", "spsp"]], [["psvp", "spvp"], ["svpv", "sppp"]]], "sg": [[2, 0], [1, 2]], "size": ["mamm", "ammm"], "sum": ["epep", "vevv"], "tree3": [0, 1], "evac": [1, 1], "split": [2, 1], "nch": 6, "xafter": 3, "tree": 2, "xzv": [[1, 1], [1, 1], [0, 1]], "oact": [0, 0], "ract": [[0, 0], [0, 0]], "first": 1.485, "upper": -1.33, "bonus": [0, 7.708], "rounds": 2, "look": 0, "greedy": 0, "lower": -0.236, "ownp": [-0.762, 4.275], "latep": [-6, -1.735], "xnp": [-5.724, -3.975], "nearp": [-1.057, 0.769], "expp": -6.421, "keep": 0})
COST.update({"cy": 0.001, "ga": 1.7, "sc": 4.0, "pc": 0.0005, "hop": 0.218, "same": 0.138, "dma": 2.0, "rem": 2.628, "first": 2.0, "issue": 0.6})
PAR.update({"askp": 0.0, "halfq": [1, 1, 1], "convp": 0.0})
PAR.update({"wp": 0.0, "wact": [[1, 1], [1, 1], [1, 1]], "xnw": [[1024, 1024]] * 3, "expw": [[1024, 1024]] * 2})
PAR.update({"own": [["vVVp", "vsvs"], ["VvpV", "vssv"], ["VvvV", "ssvv"]], "guest": [[["ppsv", "psvs"], ["vpvs", "spsp"]], [["ppsv", "pvsp"], ["pvvp", "spsp"]], [["psvp", "spvp"], ["vvps", "sppp"]]], "sg": [[2, 0], [2, 2]], "size": ["mamm", "ammm"], "sum": ["epep", "vevv"], "tree3": [1, 1], "evac": [1, 0], "split": [2, 2], "nch": 6, "xafter": 3, "tree": 3, "xzv": [[1, 1], [1, 1], [0, 1]], "oact": [0, 0], "ract": [[0, 0], [0, 0]], "first": 1.966, "upper": 0.174, "bonus": [0, 5.677], "rounds": 1, "look": 0, "greedy": 0, "lower": -0.236, "ownp": [-0.339, 3.912], "latep": [-6, 1.223], "xnp": [-5.01, -3.329], "nearp": [-1.057, 0.769], "expp": -0.258, "keep": 0, "askp": -2, "halfq": [1, 1, 1], "convp": -2.099})
COST.update({"cy": 0.001, "ga": 1.694, "sc": 4.0, "pc": 0.0005, "hop": 0.219, "same": 0.138, "dma": 2.0, "rem": 3.288, "first": 2.0, "issue": 0.85})
PAR.update({"conv": "aaaaaa"})
PAR.update({"twact": [0, 0], "tpact": 0, "qact": [[0, 0], [0, 0], [0, 0]]})
PAR.update({"own": [["hVvV", "vvhh"], ["VvVh", "hvhv"], ["VvVv", "hvvh"]], "guest": [[["hhhv", "vhhh"], ["vhvv", "hhhh"]], [["hhhv", "vhhh"], ["hvvh", "hhhh"]], [["hhvh", "vhhh"], ["vvhh", "hhhh"]]], "sg": [[1, 0], [1, 0]], "size": ["mamm", "ammm"], "sum": ["epep", "vevv"], "tree3": [0, 1], "evac": [1, 1], "split": [4, 2], "nch": 6, "xafter": 3, "tree": 2, "xzv": [[1, 1], [1, 1], [0, 0]], "oact": [0, 0], "ract": [[1, 0], [0, 0]], "first": 2.111, "upper": -1.566, "bonus": [0, 3.749], "rounds": 2, "look": 0, "greedy": 0, "lower": -0.332, "ownp": [1.857, 1.867], "latep": [-6, 0.646], "xnp": [-8, -1.135], "nearp": [-0.75, 0.769], "expp": -4.319, "keep": 0, "askp": -2, "halfq": [1, 1, 1], "convp": -2.531, "wp": -1.724, "wact": [[1, 1], [1, 1], [1, 1]], "xnw": [[1024, 1024], [1024, 1024], [2048, 1024]], "expw": [[2048, 2048], [1024, 2048]], "conv": "aaaaaa", "twact": [0, 0], "tpact": 0, "qact": [[0, 0], [0, 0], [0, 0]]})
COST.update({"cy": 0.001042, "ga": 1.694, "sc": 4.0, "pc": 0.000521, "hop": 0.207, "same": 0.145, "dma": 2.0, "rem": 3.464, "first": 2.0, "issue": 0.916})
COST.update({"row": 0.05, "far": 0.06, "byte": 1 / 25e3, "rem": 2.2})
PAR.update({"xgate": ["ol", "w2"], "dl": [[1, 1], [1, 1]], "hs": [1, 1], "tree1": 1, "tree2": 2, "restp": -3.0})
PAR.update({"own": [["hVvV", "hhvv"], ["vhVV", "hhvv"], ["VVvv", "hhvv"]], "guest": [[["hhhv", "vhhh"], ["vhvv", "hhhh"]], [["hhvv", "vhhh"], ["hvvh", "hhhh"]], [["hhvh", "vhhh"], ["hvvh", "hhhh"]]], "sg": [[1, 0], [1, 0]], "size": ["mamm", "ammm"], "sum": ["epep", "vvvv"], "tree3": [0, 1], "evac": [0, 1], "split": [4, 4], "nch": 4, "xafter": 2, "tree": 2, "xzv": [[1, 1], [1, 1], [0, 0]], "oact": [0, 0], "ract": [[1, 0], [0, 1]], "first": 2.788, "upper": -1.491, "bonus": [0, 2.523], "rounds": 2, "look": 0, "greedy": 0, "lower": -0.332, "ownp": [2.309, 1.867], "latep": [-3.364, -0.788], "xnp": [-8, 0.82], "nearp": [0.132, 0.769], "expp": -8.798, "keep": 0, "askp": -1.833, "halfq": [1, 1, 1], "convp": -4.527, "wp": -0.596, "wact": [[1, 1], [1, 1], [1, 1]], "xnw": [[1024, 1024], [1024, 1024], [2048, 1024]], "expw": [[2048, 1024], [1024, 1024]], "conv": "aaaava", "twact": [0, 0], "tpact": 0, "qact": [[0, 0], [0, 0], [0, 0]], "xgate": ["w1", "w1"], "dl": [[4, 4], [4, 4]], "hs": [1, 1], "tree1": 1, "tree2": 2, "restp": -2.502})
COST.update({"cy": 0.00111, "ga": 1.694, "sc": 4.0, "pc": 0.000555, "hop": 0.207, "same": 0.156, "dma": 2.0, "rem": 2.36, "first": 2.0, "issue": 0.945, "row": 0.013, "far": 0.057, "byte": 4e-05})
PAR.update({"early": [1, 1, 1], "cact": [[0, 0], [0, 0], [0, 0]]})
PAR.update({"own": [["VhvV", "hvvh"], ["vVhV", "hvvh"], ["VvVV", "hvvh"]], "guest": [[["hhhv", "hhvh"], ["hvvv", "hhhh"]], [["hhhv", "hhvh"], ["hvvv", "hhhh"]], [["hhhv", "hhvh"], ["hvvv", "hhhh"]]], "sg": [[1, 0], [1, 0]], "size": ["mamm", "ammm"], "sum": ["epep", "vvev"], "tree3": [0, 1], "evac": [1, 1], "split": [2, 1], "nch": 4, "xafter": 2, "tree": 2, "xzv": [[1, 1], [0, 1], [0, 1]], "oact": [0, 1], "ract": [[1, 0], [0, 1]], "first": 1.535, "upper": -1.549, "bonus": [1.008, 2.523], "rounds": 2, "look": 0, "greedy": 0, "lower": -0.332, "ownp": [2.309, 3.353], "latep": [-2.956, -2.268], "xnp": [-6.44, -3.173], "nearp": [-0.994, 0.303], "expp": -0.959, "keep": 0.011, "askp": 1.286, "halfq": [1, 1, 1], "convp": -6, "wp": 1.353, "wact": [[1, 1], [1, 1], [1, 1]], "xnw": [[2048, 1024], [2048, 1024], [1024, 512]], "expw": [[1024, 1024], [1024, 1024]], "conv": "aaaaav", "twact": [0, 0], "tpact": 0, "qact": [[0, 0], [0, 0], [0, 0]], "xgate": ["w1", "w1"], "dl": [[4, 4], [4, 3]], "hs": [1, 1], "tree1": 2, "tree2": 3, "restp": -3.435, "early": [1, 1, 1], "cact": [[1, 1], [1, 0], [0, 0]]})
COST.update({"cy": 0.00107165, "ga": 1.685, "sc": 4.0, "pc": 0.000535825, "hop": 0.207, "same": 0.156, "dma": 2.0, "rem": 2.397, "first": 2.0, "issue": 1.031, "row": 0.023, "far": 0.056, "byte": 4e-05})

SCRATCH = {
    "ri": ("sbuf", [128, V], "int32"),
    "rw": ("sbuf", [128, V + 128], "float32"),
    "xs": ("sbuf", [128, V + 32], "bfloat16"),
    "xu": ("sbuf", [128, V], "bfloat16"),
    "wi": ("sbuf", [128, 16], "int32"),
    "d0": ("sbuf", [128, 4096], "float16"),
    "d1": ("sbuf", [128, 4096], "float16"),
    "d2": ("sbuf", [128, 4096], "float16"),
    "mn": ("sbuf", [128, 2048], "bfloat16"),
    "nb": ("sbuf", [128, 4096], "bfloat16"),
    "xn": ("sbuf", [128, 4096], "bfloat16"),
    "gg": ("sbuf", [128, 4096], "float32"),
    "gh": ("sbuf", [128, 4096], "float16"),
    "w32": ("sbuf", [128, 512], "float32"),
    "ab0": ("sbuf", [128, 2, 2048], "float32"),
    "ab1": ("sbuf", [128, 2, 2048], "float32"),
    "acc": ("sbuf", [128, 512], "float32"),
    "c16": ("sbuf", [128, 512], "float16"),
    "w1": ("sbuf", [128, 512], "float16"),
    "w2": ("sbuf", [128, 512], "float16"),
    "t2": ("sbuf", [128, 256], "float16"),
    "ol": ("sbuf", [128, 256], "uint16"),
    "tp": ("sbuf", [128, 256], "float16"),
    "n32": ("sbuf", [128, 256], "float32"),
    "ee": ("sbuf", [128, 256], "float32"),
    "qe": ("sbuf", [128, 256], "float32"),
    "eq": ("sbuf", [128, 1024], "float16"),
    "run": ("sbuf", [128, 1024], "float16"),
    "o0": ("sbuf", [128, 256], "bfloat16"),
    "ok": ("sbuf", [128, 256], "float16"),
    "np_": ("sbuf", [128, 256], "float16"),
    "sn": ("sbuf", [128, 256], "float16"),
    "xz": ("sbuf", [128, 256], "bfloat16"),
    "wl": ("sbuf", [128, 16], "uint16"),
    "w16": ("sbuf", [128, 16], "float16"),
    "t16": ("sbuf", [128, 16], "float16"),
    "fb": ("sbuf", [128, 16], "float16"),
    "qq": ("sbuf", [128, 16], "float32"),
    "hh": ("sbuf", [128, 16], "float32"),
    "so": ("sbuf", [128, 16], "uint16"),
    "ka": ("sbuf", [128, 256], "float32"),
    "kq": ("sbuf", [128, 384], "int32"),
    "kr": ("sbuf", [128, 256], "float32"),
    "kp": ("sbuf", [128, 16], "int32"),
    "kp2": ("sbuf", [128, 16], "int32"),
    "kf": ("sbuf", [128, 16], "float32"),
    "jj": ("sbuf", [128, 256], "float16"),
    "j0": ("sbuf", [128, 256], "float16"),
    "j1": ("sbuf", [128, 256], "float16"),
    "bb": ("sbuf", [128, 256], "float16"),
    "bf": ("sbuf", [128, 8], "bfloat16"),
    "thr": ("sbuf", [128, 512], "float16"),
    "ni": ("sbuf", [128, 128], "float16"),
    "i32": ("sbuf", [128, 128], "float32"),
    "ib": ("sbuf", [128, 128], "bfloat16"),
    "ib2": ("sbuf", [128, 128], "bfloat16"),
    "nib": ("sbuf", [128, 128], "bfloat16"),
    "bo": ("sbuf", [128, 128], "float16"),
    "uu": ("sbuf", [128, 384], "float16"),
    "tri": ("sbuf", [128, 512], "float16"),
    "cut": ("sbuf", [128, 512], "float16"),
    "dum": ("sbuf", [128, 4], "float32"),
}
for _t in range(RO):
    for _b in range(2):
        SCRATCH["qs%d%d" % (_t, _b)] = ("sbuf", [128, 256], "uint16")
        SCRATCH["ql%d%d" % (_t, _b)] = ("sbuf", [128, 256], "uint16")
        SCRATCH["vl%d%d" % (_t, _b)] = ("sbuf", [128, 16], "uint16")
        SCRATCH["rs%d%d" % (_t, _b)] = ("sbuf", [128, 256], "bfloat16")
        SCRATCH["rl%d%d" % (_t, _b)] = ("sbuf", [128, 256], "bfloat16")
    SCRATCH["vs%d" % _t] = ("sbuf", [128, 32], "uint16")
for _b in range(8):
    SCRATCH["p%d" % _b] = ("psum", [128, 512], "float32")

SEMAPHORES = (["dve", "act", "pe", "pool", "sent"] + ["dm%d" % _i for _i in range(40)]
              + ["av%d%d" % (_t, _b) for _t in range(RO) for _b in range(2)]
              + ["aq%d%d%d" % (_t, _b, _h) for _t in range(RO) for _b in range(2) for _h in range(2)]
              + ["ar%d%d%d" % (_t, _b, _h) for _t in range(RO) for _b in range(2) for _h in range(2)])

AL = AluOpType
AF = ActivationFunctionType


def rf(name, a=0, b=None, s=1):
    if b is None:
        b = SCRATCH[name][1][1]
    return (name, a, b, s)


def cnt(r):
    return len(range(r[1], r[2], r[3]))


def meet(r, q):
    if r[2] <= q[1] or q[2] <= r[1]:
        return False
    if r[3] == 1 and q[3] == 1:
        return True
    return len(set(range(r[1], r[2], r[3])) & set(range(q[1], q[2], q[3]))) > 0


def two_bytes(r):
    return SCRATCH[r[0]][2] in ("float16", "bfloat16", "uint16")


def in_psum(r):
    return SCRATCH[r[0]][0] == "psum"


def price(ops, C):
    for o in ops:
        c = o["cost"]
        o["dur"] = (c.get("fix", 0.0) + C["cy"] * (c.get("cy", 0) + C["ga"] * c.get("ga", 0) + C["sc"] * c.get("sc", 0))
                    + C["pc"] * c.get("pc", 0) + C["issue"] * c.get("issue", 0) + C["row"] * c.get("row", 0)
                    + C["far"] * c.get("far", 0) + C["byte"] * c.get("byte", 0))
        o["lat"] = c.get("lat", 0.0) + C["dma"] * c.get("dma", 0) + C["rem"] * c.get("rem", 0) + C["first"] * c.get("first", 0)


def build(g, core, T, topo, rank):
    ops = []
    ahead = [0.0]
    table = []

    def ap(r):
        if len(r) == 2:
            return ap(r[0]).indirect(ap(r[1]))
        if len(SCRATCH[r[0]][1]) == 3:
            h = r[1] // 2048
            return T[r[0]][:, h, r[1] - 2048 * h:r[2] - 2048 * h]
        return T[r[0]][:, r[1]:r[2]] if r[3] == 1 else T[r[0]][:, r[1]:r[2]:r[3]]

    def flat(rs):
        out = []
        for r in rs:
            if isinstance(r, tuple):
                out.extend(r if len(r) == 2 else [r])
        return out

    def add(eng, fn, reads, writes, cost, kind="c", arrive=None, after=None):
        ops.append({"eng": eng, "fn": fn, "r": flat(reads), "w": flat(writes), "cost": cost, "kind": kind,
                    "arrive": arrive, "after": after, "bonus": ahead[0]})
        return len(ops) - 1

    def sc(x):
        return ap(x) if isinstance(x, tuple) else x

    def vcost(out, ins, both=False):
        if len(ins[0]) == 2:
            return {"fix": 0.05, "ga": cnt(out)}
        n = cnt(out) * (2.0 if both else 1.0)
        if not both and two_bytes(out) and all(two_bytes(i) for i in ins):
            n *= 0.5
        return {"cy": max(n, 64)}

    def ts(out, in0, s1, s2, op0, op1=None, **kw):
        def fn():
            if op1 is None:
                return g.vector.tensor_scalar(ap(out), ap(in0), sc(s1), None, op0)
            return g.vector.tensor_scalar(ap(out), ap(in0), sc(s1), sc(s2), op0, op1)
        return add("dve", fn, [in0, s1, s2], [out], vcost(out, [in0]), **kw)

    def tt(out, in0, in1, op, **kw):
        both = len(in0) == 4 and not in_psum(in0) and not in_psum(in1)
        return add("dve", lambda: g.vector.tensor_tensor(ap(out), ap(in0), ap(in1), op), [in0, in1], [out],
                   vcost(out, [in0, in1], both), **kw)

    def cp(out, in0, **kw):
        return add("dve", lambda: g.vector.tensor_copy(ap(out), ap(in0)), [in0], [out], vcost(out, [in0]), **kw)

    def fill(out, value):
        return add("dve", lambda: g.vector.memset(ap(out), value), [], [out], vcost(out, [out]))

    def act(out, in0, func, bias=None, scale=None, **kw):
        def fn():
            k = {}
            if bias is not None:
                k["bias"] = bias
            if scale is not None:
                k["scale"] = scale
            return g.scalar.activation(ap(out), ap(in0), func, **k)
        c = {"fix": 0.065, "ga": cnt(out)} if len(in0) == 2 else {"fix": 0.03, "cy": max(cnt(out), 64)}
        if func == AF.Exp and not table:
            table.append(1)
            c["fix"] += 1.3
        return add("act", fn, [in0], [out], c, **kw)

    def mm(out, lhs, rhs, start, stop, fam=None, **kw):
        c = {"pc": max(64, cnt(rhs)) * (4 if SCRATCH[rhs[0]][2] == "float32" else 1), "lat": 0.05}
        i = add("pe", lambda: g.tensor.matmul(ap(out), ap(lhs), ap(rhs), start, stop), [lhs, rhs], [out], c, **kw)
        ops[i]["fam"] = fam
        return i

    def group(out, terms):
        for i, term in enumerate(terms):
            kw = term[2] if len(term) > 2 else {}
            mm(out, term[0], term[1], i == 0, i == len(terms) - 1, **kw)

    def iota(out, pattern, base, cm):
        def fn():
            if SCRATCH[out[0]][2] == "int32":
                return g.iota(ap(out), pattern, base, cm)
            return g.iota(ap(out), pattern, base, cm, allow_small_or_imprecise_dtypes=True)
        return add("pool", fn, [], [out], {"fix": 0.13, "cy": 2 * cnt(out)})

    def asel(buf, pattern, op, value, base, cm, **kw):
        return add("pool", lambda: g.affine_select(ap(buf), ap(buf), pattern, op, value, base, cm), [buf], [buf],
                   {"fix": 0.17, "cy": 2 * cnt(buf)}, **kw)

    def narrow(dst, src):
        return add("pool", lambda: g.affine_select(ap(dst), ap(src), [[0, cnt(src)]], AL.is_ge, 0.0, 0, 0), [src], [dst],
                   {"fix": 0.17, "cy": 2 * cnt(src)})

    def moving(i, reads, writes, cost):
        j = add("ring", None, reads, writes, cost, kind="rows")
        ops[j]["of"] = i
        return j

    def dma(eng, fn, reads, writes, rows, row, **kw):
        i = add(eng, fn, reads, writes, {"issue": 1, "dma": 0.65} if eng == "pool" else {"fix": 0.1, "dma": 0.65}, kind="dma", **kw)
        return moving(i, reads, writes, {"row": rows / 16, "fix": rows / 16 * row / 38e3, "dma": 0.35})

    def send(src, dst_name, sem, to_rank, first=False, at=None):
        to = T.cores[to_rank]
        rid, pid, _ = topo.addr(to)
        at = src[1] if at is None else at

        def fn():
            return g.remote_dma(T[dst_name][:, at:at + cnt(src)], ap(src), T.sem[sem], T.sem.sent, pid, rid, topo.mask(core, to))
        i = add("pool", fn, [src], [], {"issue": 1, "rem": 0.5, "first": 1 if first else 0}, kind="rem")
        ops[i]["width"] = len(topo.engines(core, to))
        rows = 128 / ops[i]["width"]
        return moving(i, [src], [], {"far": rows, "byte": rows * 2 * cnt(src), "rem": 0.5})

    def jsl(name, shift):
        x = (-shift) % 128
        return rf(name, x, x + 128)

    RW = rf("rw", 0, V)
    I16 = rf("jj", 0, 128)

    loads = [dma("sync", lambda: g.sync.dma_start(T.wi[:], T.w0[:]), [], [rf("wi")], 128, 64) - 1]
    nch = PAR["nch"]
    step = V // nch
    pieces = [(i * step, V if i == nch - 1 else (i + 1) * step) for i in range(nch)]
    for i, (a, b) in enumerate(pieces):
        q = g.scalar if i % 2 == 0 else g.sync
        loads.append(dma("act" if i % 2 == 0 else "sync", (lambda q=q, a=a, b=b: q.dma_start(T.ri[:, a:b], T.rec[:, a:b])), [],
                         [rf("ri", a, b)], 128, 4 * (b - a), after=loads[-2:-1]) - 1)

    def states(which, gate):
        if which == 0:
            dma("sync", lambda: g.sync.dma_start(T.xs[:, 15:15 + V], T.x[:]), gate, [rf("xs", 15, 15 + V)], 128, 2 * V)
            act(rf("xs", 15 + V, 16 + V), rf("xs", 15, 16), AF.Copy)
        else:
            dma("sync", lambda: g.sync.dma_start(T.xu[:], T.x[:]), gate, [rf("xu")], 128, 2 * V)
    if PAR["xgate"][0] == "ri":
        states(0, [rf("ri", *pieces[PAR["xafter"]])])
    XS = rf("xs", 16, 16 + V)

    iota(rf("kp", 0, 4), [[0, 4]], 0, 1)
    iota(rf("ka"), [[0, 2], [1, 128]], 0, -1)
    iota(rf("kp", 4, 7), [[-1, 3]], 15, 1)
    ts(rf("kp2", 0, 1), rf("kp", 0, 1), 16, None, AL.bitwise_and)
    ts(rf("kp2", 1, 7), rf("kp", 1, 7), 15, None, AL.bitwise_and)
    cp(rf("kf", 0, 7), rf("kp2", 0, 7))
    PR = rf("kf", 1, 2)
    ts(rf("kf", 8, 9), rf("kf", 0, 1), 0.0, None, AL.is_equal)
    ts(rf("kf", 9, 10), rf("kf", 0, 1), 0.0, None, AL.is_gt)
    ts(rf("jj"), rf("ka"), 0.0, None, AL.is_equal)
    ts(rf("j0"), rf("jj"), rf("kf", 8, 9), None, AL.mult)
    ts(rf("j1"), rf("jj"), rf("kf", 9, 10), None, AL.mult)
    ts(rf("bb"), rf("ka"), PR, 0.0, AL.add, AL.is_equal)
    ts(rf("ni"), I16, -1.0, None, AL.mult)
    act(rf("i32"), rf("ka", 0, 128), AF.Abs)
    act(rf("i32"), rf("i32"), AF.Relu, bias=1.0, scale=-1.0)
    act(rf("nib"), rf("i32"), AF.Identity, scale=-1.0)
    act(rf("ib"), rf("i32"), AF.Identity)
    act(rf("ib2"), rf("i32"), AF.Identity, scale=2.0)
    fill(rf("rw", V, V + 128), 0.0)
    fill(rf("bo"), 1.0)
    fill(rf("thr"), 7.5)
    for c0 in (0, 256):
        act(rf("cut", c0, c0 + 256), rf("ka"), AF.Exp, scale=0.0)
    fill(rf("cut", 0, 512, 64), 0.0)
    cp(rf("bf"), rf("bb", 0, 128, 16))
    iota(rf("kq"), [[-1, 3], [0, 8], [1, 16]], 15, 0)
    iota(rf("kr"), [[-16, 4], [1, 64]], 0, 0)
    ts(rf("kq"), rf("kq"), 15, None, AL.bitwise_and)
    for t in range(RO):
        ts(rf("uu", 128 * t, 128 * t + 128), rf("kq", 128 * t, 128 * t + 128), rf("kf", 4 + t, 5 + t), None, AL.is_gt)
    ts(rf("tri", 0, 256), rf("kr"), PR, 14080.0, AL.is_ge, AL.mult)
    ts(rf("tri", 0, 256), rf("tri", 0, 256), TOZ + LOW, None, AL.add)
    fill(rf("tri", 63, 256, 64), float(CEN + 1))
    cp(rf("tri", 256, 512), rf("tri", 0, 256))
    iota(rf("dum"), [[32, 4]], V, 0)
    ts(rf("dum"), rf("dum"), PR, PR, AL.add, AL.add)

    cp(rf("wl"), rf("wi"))
    ts(rf("w16"), rf("wi"), float(CEN), None, AL.subtract)
    wsend = {}

    def times_ahead(t):
        for b in range(2):
            group(rf("p3", 288 + 16 * b, 304 + 16 * b), [(jsl("jj", 16 * (t + 1 + b)), rf("w16"))])
        ts(rf("vs%d" % t), rf("p3", 288, 320), float(CEN), None, AL.add)
        for b in range(2):
            wsend[(t, b)] = send(rf("vs%d" % t, 16 * b, 16 * b + 16), "vl%d%d" % (t, b), "av%d%d" % (t, b),
                                 (rank + HOPS[t][b]) % NR, first=(t == 0), at=0)
    times_ahead(0)
    ahead[0] = PAR["convp"]
    for i, (a, b) in enumerate(pieces):
        if PAR["conv"][i] == "a":
            act(rf("rw", a, b), rf("ri", a, b), AF.Identity, bias=-float(CEN))
        else:
            ts(rf("rw", a, b), rf("ri", a, b), float(CEN), None, AL.subtract)
    ahead[0] = 0.0

    ring = {"p": 0, "g": 0, "h": 0}

    def bank():
        kinds = "".join(y for x in list(PAR["guest"][ring["t"]]) + [PAR["own"][ring["t"]]] for y in x)
        banks = (4, 5, 6) if "u" in kinds.lower() else (4, 5, 6, 7)
        ring["p"] += 1
        return "p%d" % banks[ring["p"] % len(banks)]

    def twice(buf, h):
        if PAR["twact"][buf != "c16"]:
            act(rf(buf, 384 * h, 384 * h + 128), rf(buf, 128 + 128 * h, 256 + 128 * h), AF.Copy)
        else:
            cp(rf(buf, 384 * h, 384 * h + 128), rf(buf, 128 + 128 * h, 256 + 128 * h))

    def count_rows(dbuf, h, k, cbank, c0, shift, fam):
        x = (16 * shift) % 128
        a = 2048 * h + 128 * k
        mm(rf(cbank, c0 + k, c0 + 128, 16), rf(dbuf, a, a + 128),
           rf("bf") if dbuf == "nb" else rf("bb", x, x + 128, 16), True, True, fam=fam)

    def likeness(dbuf, h, lists, wbuf, kinds, wps, arrive, cbank, shift, fam, after=None):
        kw = {"arrive": arrive, "after": after}
        wref, wone = rf(wbuf, 256 * h, 256 * h + 256), rf(wbuf, 128 + 128 * h, 256 + 128 * h)
        d0, l0 = 2048 * h, 128 * h
        for unit, how in enumerate(kinds):
            if how not in "hpsuv":
                continue
            k0, k1 = 2 * unit, 2 * unit + 2
            dd = rf(dbuf, d0 + 256 * k0, d0 + 256 * k1)
            if how == "h":
                pb, e0 = bank(), 512 * (ring["h"] % 8)
                ring["h"] += 1
                act(rf("gh", e0, e0 + 512), (RW, rf(lists, l0 + 16 * k0, l0 + 16 * k1)), AF.Copy, arrive=arrive)
                for i in range(4):
                    group(rf(pb, 128 * i, 128 * i + 128),
                          [(rf("ni"), wone), (I16, rf("gh", e0 + 128 * i, e0 + 128 * i + 128))])
                ts(dd, rf(pb), MAGIC, MAGIC, AL.add, AL.is_equal)
                for k in range(2 * k0, 2 * k1):
                    count_rows(dbuf, h, k, cbank, 128 * h, shift, fam)
                continue
            if how != "v":
                c0 = 512 * (ring["g"] % 8)
                ring["g"] += 1
                act(rf("gg", c0, c0 + 512), (RW, rf(lists, l0 + 16 * k0, l0 + 16 * k1)), AF.Copy, arrive=arrive)
            if how == "p":
                pb, e0 = bank(), 512 * (ring["h"] % 4)
                ring["h"] += 1
                narrow(rf("gh", e0, e0 + 512), rf("gg", c0, c0 + 512))
                for i in range(4):
                    group(rf(pb, 128 * i, 128 * i + 128),
                          [(rf("ni"), wone), (I16, rf("gh", e0 + 128 * i, e0 + 128 * i + 128))])
                ts(dd, rf(pb), MAGIC, MAGIC, AL.add, AL.is_equal)
            elif how == "s":
                pb = bank()
                for i in range(4):
                    group(rf(pb, 128 * i, 128 * i + 128),
                          [(rf("ni"), wone), (rf("i32"), rf("gg", c0 + 128 * i, c0 + 128 * i + 128))])
                ts(dd, rf(pb), MAGIC, MAGIC, AL.add, AL.is_equal)
            else:
                for k in range(k0, k1):
                    dk = rf(dbuf, d0 + 256 * k, d0 + 256 * k + 256)
                    if how == "u":
                        tt(dk, rf("gg", c0 + 256 * (k - k0), c0 + 256 * (k - k0) + 256), wps, AL.subtract)
                    else:
                        tt(dk, (RW, rf(lists, l0 + 16 * k, l0 + 16 * k + 16)), wref, AL.subtract, **kw)
                ts(dd, dd, MAGIC, MAGIC, AL.add, AL.is_equal)
            for k in range(2 * k0, 2 * k1):
                count_rows(dbuf, h, k, cbank, 128 * h, shift, fam)

    def enough(out, counts, by_scalar):
        if by_scalar:
            return act(out, counts, AF.Sign, bias=-9.5)
        return ts(out, counts, 9.5, None, AL.is_ge)

    def offsets(out, names, by_scalar):
        if by_scalar:
            return act(out, names, AF.Identity, bias=float(CEN))
        return ts(out, names, float(CEN), None, AL.add)

    def halve(s, levels, after, part):
        buf = "ab%d" % (s % 2)
        h0, h1 = min(part), max(part) + 1
        region = rf(buf, 2048 * h0, 2048 * h1)
        for lv in levels:
            if lv >= PAR["dl"][s][h0]:
                continue
            w = 1024 >> lv
            dma("pool", (lambda w=w: g.dma_start(T[buf][:, h0:h1, 0:w], T[buf][:, h0:h1, w:2 * w], accum_op=AL.add)),
                [region], [region], 128 * len(part), 8 * w, after=after)
            if lv == 3:
                dma("sync", lambda: g.sync.dma_start(T.y[:, 256 * s + 128 * h0:256 * s + 128 * h1], T[buf][:, h0:h1, 0:128]),
                    [region], [], 128 * len(part), 512)

    def rest(s):
        buf = "ab%d" % (s % 2)
        halves = [h for h in (1, 0) if PAR["dl"][s][h if PAR["hs"][s] else 0] < 4]
        for h in halves:
            rows = 16 >> PAR["dl"][s][h if PAR["hs"][s] else 0]
            group(rf("p3", 128 * h, 128 * h + 128), [(rf("i32"), rf(buf, 2048 * h + 128 * k, 2048 * h + 128 * k + 128))
                                                     for k in range(rows)])
        if halves:
            a, b = 128 * min(halves), 128 * max(halves) + 128
            act(rf("acc", 256 + a, 256 + b), rf("p3", a, b), AF.Copy)
            dma("sync", lambda: g.sync.dma_start(T.y[:, 256 * s + a:256 * s + b], T.acc[:, 256 + a:256 + b]),
                [rf("acc", 256 + a, 256 + b)], [], 128, 4 * (b - a))

    def choose(t, h, answers):
        a, b, m0, m1 = 128 * h, 128 * h + 128, 8 * h, 8 * h + 8
        pb = "p1" if h else "p2"
        group(rf(pb, 0, 128), [(rf("o0", a, b), rf("ib"))]
              + [(rf("rl%d%d" % (t, i), a, b), rf("ib"), {"arrive": ("ar%d%d%d" % (t, i, h), answers[(i, h)])}) for i in range(2)])
        ts(rf("ok", a, b), rf(pb, 0, 128), 2.5, -BIG, AL.is_ge, AL.mult)
        group(rf(pb, 128, 256), [(I16, rf("c16", 128 + a, 128 + b)), (rf("ni"), rf("tp", a, b)),
                                 (rf("uu", 128 * t, 128 * t + 128), rf("ok", a, b))])
        none = rf(pb if PAR["early"][t] and h else "p3", 272 + m0, 272 + m1)
        group(none, [(I16, rf("w16", m0, m1)), (rf("ni"), rf("t16", m0, m1))]
              + [(jsl("bb", r), rf("ok", a + r, b, 16)) for r in range(16)])
        ts(rf("sn", a, b), rf(pb, 128, 256), BIG + LOW, BIG, AL.max, AL.subtract)
        ts(rf("fb", m0, m1), none, LOW, None, AL.max)
        zs = rf(pb, 256, 264)
        group(zs, [(jsl("bb", r), rf("sn", a + r, b, 16)) for r in range(16)] + [(I16, rf("fb", m0, m1))])
        ts(rf("wl", m0, m1), zs, TOZ, None, AL.add)
        if PAR["xzv"][t][h]:
            cp(rf("xz", a, b), (rf("xu"), rf("wl", m0, m1)))
        else:
            act(rf("xz", a, b), (rf("xu"), rf("wl", m0, m1)), AF.Copy)
        if t == RO - 1:
            return
        ts(rf("qq", m0, m1), zs, TOZ, None, AL.add)
        if h == 0:
            ts(rf("w16"), rf("wl"), float(CEN), None, AL.subtract)
        mm(rf(pb), I16, rf("tri"), True, False)
        for m in range(8):
            c0 = a + 64 * (m // 4)
            mm(rf(pb, 64 * m, 64 * m + 63), rf("bo"), rf("sn", c0, c0 + 63), False, False)
        mm(rf(pb, 63, 512, 64), I16, rf("fb", m0, m1), False, True)
        tt(rf("ee", a, b), (RW, rf("wl", m0, m1)), rf("n32", a, b), AL.subtract)
        e0 = 512 * h
        for m in range(8):
            ts(rf("eq", e0 + 64 * m, e0 + 64 * m + 64), rf(pb, 64 * m, 64 * m + 64), rf("qq", m0 + m, m0 + m + 1),
               rf("dum", m % 4, m % 4 + 1), AL.is_equal, AL.mult)
        eq, run = rf("eq", e0, e0 + 512), rf("run", e0, e0 + 512)
        add("dve", lambda: g.vector.tensor_tensor_scan(ap(run), ap(rf("cut")), ap(eq), 0.0, AL.mult, AL.max),
            [rf("cut"), eq], [run], {"cy": 256})
        tt(rf("hh", m0, m1), rf("run", e0 + 63, e0 + 512, 64), rf("qq", m0, m1), AL.max)
        cp(rf("so", m0, m1), rf("hh", m0, m1))

    def differ(pb, h, i, lhs, close):
        mm(rf(pb), rf(lhs), rf("xn", 2048 * h + 512 * i, 2048 * h + 512 * i + 512), True, False)
        for j in range(4):
            mm(rf(pb, 128 * j, 128 * j + 128), rf("nib"), rf("xz", 128 * h, 128 * h + 128), False, close and j == 3)

    def near(t, h):
        sg, buf = PAR["sg"][t][h], "ab%d" % (t % 2)
        a, b = 128 * h, 128 * h + 128
        for i in [0, 3, 2, 1]:
            pb = "p%d" % (4 + i)
            c0 = 2048 * h + 512 * i
            differ(pb, h, i, "ib", True)
            if i < sg:
                act(rf(buf, c0, c0 + 512), rf(pb), AF.Abs)
                act(rf("nb", c0, c0 + 512), rf(buf, c0, c0 + 512), AF.Sign, bias=0.5 + 2.0 ** -21, scale=-1.0)
            else:
                ts(rf("d0", c0, c0 + 512), rf(pb), HALF, HALF, AL.add, AL.is_equal)
            for k in range(4 * i, 4 * i + 4):
                count_rows("nb" if i < sg else "d0", h, k, "p0", 256 + a, 0, "near%d%d" % (t, h))
        for i in range(3, sg - 1, -1):
            act(rf(buf, 2048 * h + 512 * i, 2048 * h + 512 * i + 512), rf("p%d" % (4 + i)), AF.Abs)
        tt(rf("np_", a, b), rf("p0", 256 + a, 256 + b), rf("thr", 256 * t + a, 256 * t + b), AL.is_lt)
        pb = "p1" if h else "p2"
        group(rf(pb, 384, 512), [(rf("np_", a, b), I16)])
        tt(rf("qe", a, b), rf(pb, 384, 512), rf("ee", a, b), AL.mult)
        keep, ahead[0] = ahead[0], PAR["expp"]
        for c0 in range(2048 * h, 2048 * h + 2048, PAR["expw"][t][h]):
            ab = rf(buf, c0, c0 + PAR["expw"][t][h])
            act(ab, ab, AF.Exp, scale=-1.0)
        ahead[0] = keep

    def rewrite(h):
        win = rf("rw")
        for m in (8 * h + 4, 8 * h):
            add("dve", (lambda m=m: g.vector.tensor_tensor(ap((win, rf("so", m, m + 4))), T.qe[:, 16 * m:16 * m + 64],
                                                           T.n32[:, 16 * m:16 * m + 64], AL.add)),
                [rf("so", m, m + 4), rf("qe", 16 * m, 16 * m + 64), rf("n32", 16 * m, 16 * m + 64)], [win],
                {"fix": 0.05, "sc": 64})

    def sums(t, h):
        size, ways, buf, xb = PAR["size"][h], PAR["sum"][h], "ab%d" % (t % 2), ("p1" if h else "p2")
        a, b = 128 * h, 128 * h + 128
        if "m" in size:
            group(rf(xb, 0, 128), [(rf("ib"), rf("xz", a, b))])
        total, acc = rf("p7" if h else "p0", 0, 128), rf("acc", a, b)
        chain = [i for i in range(4) if ways[i] == "v"]
        tree = PAR["tree3"][h] and len(chain) > 1
        nblocks = 4 * ways.count("p") + (4 if chain and not tree else 0)
        done = {"blocks": 0, "acc": False}

        def fold(c0, c1):
            for c in range(c0, c1, 128):
                done["blocks"] += 1
                mm(total, rf("i32"), rf(buf, c, c + 128), done["blocks"] == 1, done["blocks"] == nblocks)

        def onto(piece):
            if done["acc"]:
                tt(acc, piece, acc, AL.add)
            else:
                cp(acc, piece)
            done["acc"] = True
        for i in range(4):
            pb = ("p4", "p5", "p6", "p4")[i] if h else ("p5", "p6", "p4", "p7")[i]
            c0 = 2048 * h + 512 * i
            w = 512 // PAR["split"][h] if i == 3 else 512
            if size[i] == "m":
                differ(pb, h, i, "nib", False)
                for j in range(4):
                    tt(rf("mn", 512 * i + 128 * j, 512 * i + 128 * j + 128), rf("xn", c0 + 128 * j, c0 + 128 * j + 128),
                       rf(xb, 0, 128), AL.min)
                mm(rf(pb), rf("ib2"), rf("mn", 512 * i, 512 * i + 512), False, True)
            else:
                differ(pb, h, i, "ib", True)
                act(rf(buf, c0, c0 + 512), rf(pb), AF.Abs)
            stay = ways[i] == "e" or (ways[i] == "v" and i != chain[0])
            for c in range(0, 512, w):
                out = rf(pb, c, c + w) if stay else rf(buf, c0 + c, c0 + c + w)
                if size[i] == "m":
                    act(out, rf(pb, c, c + w), AF.Exp)
                else:
                    act(out, rf(buf, c0 + c, c0 + c + w), AF.Exp, scale=-1.0)
                if ways[i] == "p":
                    fold(c0 + c, c0 + c + w)
            if ways[i] == "e":
                for c in range(0, 512, 128):
                    onto(rf(pb, c, c + 128))
            if ways[i] == "v":
                f0 = 2048 * h + 512 * chain[0]
                if tree and i == chain[-1]:
                    tt(rf(buf, f0, f0 + 256), rf(pb, 0, 256), rf(buf, f0, f0 + 256), AL.add)
                    tt(rf(pb, 256, 512), rf(pb, 256, 512), rf(buf, f0 + 256, f0 + 512), AL.add)
                    tt(rf(buf, f0, f0 + 128), rf(pb, 256, 384), rf(buf, f0, f0 + 128), AL.add)
                    tt(rf(pb, 384, 512), rf(pb, 384, 512), rf(buf, f0 + 128, f0 + 256), AL.add)
                    if done["acc"]:
                        onto(rf(pb, 384, 512))
                        tt(acc, rf(buf, f0, f0 + 128), acc, AL.add)
                    else:
                        tt(acc, rf(pb, 384, 512), rf(buf, f0, f0 + 128), AL.add)
                        done["acc"] = True
                elif i != chain[0]:
                    tt(rf(buf, f0, f0 + 512), rf(pb), rf(buf, f0, f0 + 512), AL.add)
                if i == chain[-1] and not tree:
                    fold(f0, f0 + 512)
        if nblocks and (done["acc"] or PAR["evac"][h]):
            onto(total)
        elif nblocks:
            act(acc, total, AF.Copy)
        dma("sync", lambda: g.sync.dma_start(T.y[:, 256 * t + a:256 * t + b], T.acc[:, a:b]), [acc], [], 128, 512)

    for t in range(RO):
        last = t == RO - 1
        ring["t"] = t
        CC = rf("c16", 128, 384)
        sends, arr = [], {}
        ahead[0] = PAR["askp"]
        for part in (((1,), (0,)) if PAR["halfq"][t] else ((1, 0),)):
            a, e = 128 * min(part), 128 * max(part) + 128
            cc, wl = rf("c16", 128 + a, 128 + e), rf("wl", a // 16, e // 16)
            if t == 0:
                ts(cc, (rf("ri"), wl), float(CEN), None, AL.subtract)
            elif PAR["cact"][t][part[0]]:
                act(cc, (RW, wl), AF.Copy)
            else:
                cp(cc, (RW, wl))
            for be in range(a // 64, e // 64):
                o = rf("t2", 128 * (be // 2) + be % 2, 128 * (be // 2) + 128, 2)
                i = rf("c16", 128 + 64 * be, 192 + 64 * be)
                add("dve", (lambda o=o, i=i: g.vector.transpose(ap(o), ap(i))), [i], [o], {"cy": 64})
            for b in range(3):
                s = 0 if b == 2 else t + 1 + b
                pb = ("p1", "p2", "p3")[b] if 1 in part else ("p4", "p5", "p6")[b]
                for h in part:
                    for m in range(4):
                        gp, c0 = m % 2, 128 * h + 64 * (m // 2)
                        group(rf(pb, 128 * h + m, 128 * h + 128, 4),
                              [(jsl("j%d" % gp, 16 * (ga - gp + s)), rf("t2", c0 + 32 * ga, c0 + 32 * ga + 32))
                               for ga in range(2)])
                if b < 2:
                    sem = "aq%d%d%d" % (t, b, part[0])
                    offsets(rf("qs%d%d" % (t, b), a, e), rf(pb, a, e), PAR["qact"][b][part[0]])
                    sends.append(send(rf("qs%d%d" % (t, b), a, e), "ql%d%d" % (t, b), sem, (rank + HOPS[t][b]) % NR))
                    for h in part:
                        arr[(b, h)] = (sem, sends[-1])
                else:
                    offsets(rf("ol", a, e), rf(pb, a, e), PAR["qact"][b][part[0]])
        ahead[0] = 0.0
        for h in range(2):
            if "v" in PAR["own"][t][h].lower():
                twice("c16", h)
        if PAR["tpact"]:
            act(rf("tp"), CC, AF.Relu, bias=-float(V * (V - CEN - 2)), scale=float(V))
        else:
            ts(rf("tp"), CC, V - CEN - 1.5, float(V), AL.is_gt, AL.mult)
        if t == 0:
            for buf, rep in ((rf("uu"), 3), (rf("bo"), 1)):
                asel(buf, [[0, rep], [-16, 8], [0, 16]], AL.is_ge, 0.0, 0, 1, after=sends)
                asel(buf, [[0, rep], [16, 8], [0, 16]], AL.is_ge, 0.0, 15, -1)
            asel(rf("uu"), [[0, 3], [-1, 128]], AL.not_equal, -1.0, 0, 1)
            for s in range(RO - 1):
                for h in range(2):
                    if PAR["sg"][s][h]:
                        asel(rf("thr", 256 * s + 128 * h, 256 * s + 128 * h + 128), [[0, 8], [1, 16]], AL.is_ge, -0.5,
                             -4 * PAR["sg"][s][h], 0, after=sends)
        else:
            halve(t - 1, range(PAR["tree"]), sends, (0,) if PAR["hs"][t - 1] else (0, 1))
            if PAR["hs"][t - 1]:
                halve(t - 1, range(PAR["tree1"], max(PAR["tree1"], PAR["tree2"])), sends, (1,))
        ts(rf("t16"), rf("w16"), float(V - CEN - 1), float(V), AL.is_equal, AL.mult)
        if not last:
            group(rf("p3", 0, 256), [(I16, CC), (rf("ni"), rf("tp"))])
            act(rf("n32"), rf("p3", 0, 256), AF.Identity, bias=1.0)

        for b in range(2):
            wb = "w%d" % (b + 1)
            came = ("av%d%d" % (t, b), wsend[(t, b)])
            ahead[0] = PAR["wp"]
            if PAR["wact"][t][b]:
                act(rf(wb, 128, 384), (RW, rf("vl%d%d" % (t, b))), AF.Copy, arrive=came)
            else:
                cp(rf(wb, 128, 384), (RW, rf("vl%d%d" % (t, b))), arrive=came)
            ahead[0] = 0.0
            for h in range(2):
                if "v" in PAR["guest"][t][b][h]:
                    twice(wb, h)

        for i in range(2):
            if t == 0 and PAR["xgate"][i] != "ri":
                states(i, [rf(PAR["xgate"][i], 128, 256)])

        def own_rows(h, late, after):
            kinds = PAR["own"][t][h].swapcase() if late else PAR["own"][t][h]
            if "u" in kinds:
                for i in range(2):
                    group(rf("p7", 128 * i, 128 * i + 128), [(I16, rf("c16", 128 + 128 * h, 256 + 128 * h))])
            likeness("d0", h, "ol", "c16", kinds, rf("p7", 0, 256), None, "p0", 0, "own%d" % t, after)
        for h in (1, 0):
            ahead[0] = PAR["ownp"][h]
            own_rows(h, False, None)
        answers, made = {}, []
        for h in (1, 0):
            for b in range(2):
                ahead[0] = PAR["bonus"][h] + (0.0 if b else PAR["first"])
                wb, pb = "w%d" % (b + 1), "p3" if PAR["early"][t] and (b, h) == (0, 0) else "p%d" % (b + 1)
                kinds, wps = PAR["guest"][t][b][h], rf("p7", 256 * b, 256 * b + 256)
                if "u" in kinds:
                    for i in range(2):
                        group(rf("p7", 256 * b + 128 * i, 256 * b + 128 * i + 128), [(I16, rf(wb, 128 + 128 * h, 256 + 128 * h))])
                likeness("d%d" % (b + 1), h, "ql%d%d" % (t, b), wb, kinds, wps, arr[(b, h)], pb, t + 1 + b, "g%d%d%d" % (t, b, h))
                rs = rf("rs%d%d" % (t, b), 128 * h, 128 * h + 128)
                made.append(enough(rs, rf(pb, 128 * h, 128 * h + 128), PAR["ract"][b][h]))
                answers[(b, h)] = send(rs, "rl%d%d" % (t, b), "ar%d%d%d" % (t, b, h), (rank - HOPS[t][b]) % NR)
        ahead[0] = 0.0
        if t > 0:
            later = list(answers.values())
            halve(t - 1, range(PAR["tree"], 4), later, (0,) if PAR["hs"][t - 1] else (0, 1))
            if PAR["hs"][t - 1]:
                halve(t - 1, range(max(PAR["tree1"], PAR["tree2"]), 4), later, (1,))
            ahead[0] = PAR["restp"]
            rest(t - 1)
        ahead[0] = PAR["latep"][1]
        own_rows(1, True, made)
        for h in (1, 0):
            ahead[0] = PAR["xnp"][h]
            w = PAR["xnw"][t][h]
            for c0 in range(2048 * h, 2048 * h + 2048, w):
                act(rf("xn", c0, c0 + w), (XS, rf("ol", c0 // 16, (c0 + w) // 16)), AF.Copy)

        ahead[0] = PAR["upper"]
        enough(rf("o0", 128, 256), rf("p0", 128, 256), PAR["oact"][1])
        choose(t, 1, answers)
        ahead[0] = PAR["latep"][0]
        own_rows(0, True, made)
        enough(rf("o0", 0, 128), rf("p0", 0, 128), PAR["oact"][0])
        ahead[0] = PAR["nearp"][1]
        if last:
            sums(t, 1)
            ahead[0] = PAR["lower"]
            choose(t, 0, answers)
            ahead[0] = PAR["nearp"][0]
            sums(t, 0)
        else:
            near(t, 1)
            ahead[0] = PAR["lower"]
            choose(t, 0, answers)
            times_ahead(t + 1)
            if PAR["hs"][t]:
                halve(t, range(PAR["tree1"]), None, (1,))
            rewrite(1)
            ahead[0] = PAR["nearp"][0]
            near(t, 0)
            rewrite(0)
        ahead[0] = 0.0
    price(ops, COST)
    return ops


def plan(ops):
    seen, older = {}, {}
    for i, o in enumerate(ops):
        dep, soft = set(), set()
        if o["kind"] == "rows":
            for r, isw in [(r, False) for r in o["r"]] + [(r, True) for r in o["w"]]:
                seen.setdefault(r[0], []).append((i, r, isw))
            o["dep"], o["soft"] = {o["of"]}, soft
            continue
        for r in o["r"] + o["w"]:
            if in_psum(r) and seen.get(r[0]) and ops[seen[r[0]][-1][0]]["eng"] != o["eng"]:
                older[r[0]], seen[r[0]] = seen[r[0]], []
        for r, isw in [(r, False) for r in o["r"]] + [(r, True) for r in o["w"]]:
            for j, q, wasw in older.get(r[0], []) + seen.get(r[0], []):
                if j == i:
                    continue
                ej = ops[j]["eng"]
                if in_psum(r) and ej != o["eng"]:
                    dep.add(j)
                elif in_psum(r) and ej == "pe":
                    if o["fam"] is None or o["fam"] != ops[j]["fam"]:
                        soft.add(j)
                elif (isw or wasw) and meet(r, q):
                    dep.add(j)
        for r, isw in [(r, False) for r in o["r"]] + [(r, True) for r in o["w"]] if o["kind"] == "c" else []:
            lst = seen.setdefault(r[0], [])
            if isw and not in_psum(r) and r[3] == 1:
                lst[:] = [e for e in lst if not (r[1] <= e[1][1] and e[1][2] <= r[2])]
            lst.append((i, r, isw))
        o["dep"], o["soft"] = dep, soft


def order(ops):
    n = len(ops)
    C = COST
    pred = []
    for i, o in enumerate(ops):
        p = {}
        for j in o["dep"]:
            p[j] = ops[j]["dur"] + ops[j]["lat"] + (0.0 if o["kind"] == "rows" else C["same"] if ops[j]["eng"] == o["eng"] else C["hop"])
        for j in o["soft"]:
            p.setdefault(j, ops[j]["dur"])
        for j in o["after"] or ():
            p.setdefault(j, ops[j]["dur"])
        if o["arrive"] is not None:
            j = o["arrive"][1]
            p[j] = ops[j]["dur"] + ops[j]["lat"]
        pred.append(p)
    succ = [[] for _ in range(n)]
    for i in range(n):
        for j in pred[i]:
            succ[j].append(i)
    prio = [0.0] * n
    for i in range(n - 1, -1, -1):
        best = ops[i]["dur"] + ops[i]["lat"]
        for s in succ[i]:
            best = max(best, pred[s][i] + prio[s])
        prio[i] = best
    dur = [o["dur"] for o in ops]
    back = [{s: dur[s] + pred[s][i] - dur[i] for s in succ[i]} for i in range(n)]

    def place(rank, before, release):
        busy = {}
        start = [0.0] * n
        for i in rank:
            t = max([release[i]] + [start[j] + d for j, d in before[i].items()])
            line = busy.setdefault(ops[i]["eng"], [])
            k = len(line)
            while k > 0 and line[k - 1][1] > t:
                k -= 1
            while k < len(line) and line[k][0] < t + dur[i] - 1e-9:
                t = max(t, line[k][1])
                k += 1
            line.insert(k, (t, t + dur[i]))
            start[i] = t
        return start

    def ranked(key, before, after):
        left = [len(p) for p in before]
        free = sorted((key[i], i) for i in range(n) if not left[i])
        out = []
        while free:
            i = free.pop(0)[1]
            out.append(i)
            for s in after[i]:
                left[s] -= 1
                if not left[s]:
                    k = len(free)
                    while k > 0 and free[k - 1] > (key[s], s):
                        k -= 1
                    free.insert(k, (key[s], s))
        return out

    def greedy(key):
        left = [len(p) for p in pred]
        ready = {i: 0.0 for i in range(n) if not left[i]}
        free, start = {}, [0.0] * n
        while ready:
            t0, i0 = min((max(tm, free.get(ops[i]["eng"], 0.0)), i) for i, tm in ready.items())
            eng = ops[i0]["eng"]
            i = min((key[i], i) for i, tm in ready.items() if ops[i]["eng"] == eng and tm <= t0 + 1e-9 + PAR["look"])[1]
            start[i] = max(ready.pop(i), free.get(eng, 0.0))
            free[eng] = start[i] + dur[i]
            for s in succ[i]:
                left[s] -= 1
                if not left[s]:
                    ready[s] = max(start[j] + d for j, d in pred[s].items())
        return start
    zero, tail = [0.0] * n, [o["lat"] for o in ops]
    start = greedy([-prio[i] - ops[i]["bonus"] for i in range(n)])
    best = (max(start[i] + dur[i] + tail[i] for i in range(n)), start)
    for _ in range(PAR["rounds"]):
        rev = place(ranked([-start[i] - dur[i] for i in range(n)], back, pred), back, tail)
        key = [-rev[i] - dur[i] - PAR["keep"] * ops[i]["bonus"] for i in range(n)]
        key = [key[ops[i].get("of", i)] for i in range(n)]
        start = greedy(key) if PAR["greedy"] else place(ranked(key, pred, succ), pred, zero)
        end = max(start[i] + dur[i] + tail[i] for i in range(n))
        if end < best[0]:
            best = (end, start)
    start = best[1]
    return sorted(range(n), key=lambda i: (start[i], i)), start


def emit(g, T, topo, core, ops, seq):
    queue = {"dve": g.vector, "act": g.scalar, "pe": g.tensor, "pool": g, "sync": g.sync}
    seq = [i for i in seq if ops[i]["kind"] != "rows"]
    for o in ops:
        o["dep"] = {ops[j].get("of", j) for j in o["dep"]}
    num, key = {}, {}
    ndma = 0
    for i in seq:
        o = ops[i]
        if o["kind"] == "c":
            num[o["eng"]] = num.get(o["eng"], 0) + 1
            key[i] = (o["eng"], num[o["eng"]])
        elif o["kind"] == "dma":
            key[i] = ("dm%d" % ndma, 1)
            ndma += 1
    clock = {e: {} for e in queue}
    snap, waits, needed = {}, {}, set()
    for i in seq:
        o = ops[i]
        ck = clock[o["eng"]]
        ws = []
        if o["arrive"] is not None and ck.get(o["arrive"][0], 0) < 1:
            ck[o["arrive"][0]] = 1
            ws.append(("arrive", o["arrive"][0]))
        deps = sorted([j for j in o["dep"] if j in key], key=lambda j: -key[j][1])
        for j in deps:
            s, c = key[j]
            if ck.get(s, 0) < c:
                ws.append(("op", j))
                needed.add(j)
                for s2, c2 in snap[j].items():
                    if ck.get(s2, 0) < c2:
                        ck[s2] = c2
                ck[s] = c
        waits[i] = ws
        snap[i] = dict(ck)
    count, value = {}, {}
    for i in seq:
        if i in needed and ops[i]["kind"] == "c":
            count[ops[i]["eng"]] = count.get(ops[i]["eng"], 0) + 1
            value[i] = count[ops[i]["eng"]]
    rank = T.rank_of(core)

    def arrival(name):
        hop = HOPS[int(name[2])][int(name[3])]
        sender = (rank + hop if name[1] == "r" else rank - hop) % NR
        return len(topo.engines(T.cores[sender], core))
    nsent = 0
    for i in seq:
        o = ops[i]
        q = queue[o["eng"]]
        for kind, j in waits[i]:
            if kind == "arrive":
                q.wait_ge(T.sem[j], arrival(j))
            elif ops[j]["kind"] == "dma":
                q.wait_ge(T.sem[key[j][0]], 16)
            else:
                q.wait_ge(T.sem[key[j][0]], value[j])
        ins = o["fn"]()
        if o["kind"] == "dma":
            ins.then_inc(T.sem[key[i][0]], 16)
        elif o["kind"] == "rem":
            nsent += o["width"]
        elif i in needed:
            ins.then_inc(T.sem[o["eng"]], 1)
    for i in seq:
        if ops[i]["kind"] == "dma" and i not in needed:
            g.sync.wait_ge(T.sem[key[i][0]], 16)
    g.wait_ge(T.sem.sent, nsent)


def rank_program(g, core, T, topo):
    rank = T.rank_of(core)
    if rank is None:
        return
    ops = build(g, core, T, topo, rank)
    plan(ops)
    seq, _ = order(ops)
    emit(g, T, topo, core, ops, seq)
